import numpy as np
import ml_dtypes


def mxq(x, axis, fmt="e4m3"):
    dtype, down = {"e4m3": (ml_dtypes.float8_e4m3fn, 7), "e5m2": (ml_dtypes.float8_e5m2, 14)}[fmt]
    v = np.moveaxis(np.asarray(x, np.float32).astype(ml_dtypes.bfloat16).astype(np.float64), axis, -1)
    blocks = v.reshape(v.shape[:-1] + (-1, 32))
    amax = np.abs(blocks).max(-1, keepdims=True)
    byte = np.maximum(np.where(amax > 0, np.frexp(amax)[1] - 1 + 127, 0) - down, 1)
    scale = np.exp2(byte - 127.0)
    codes = (blocks / scale).astype(np.float32).astype(dtype).astype(np.float64)
    return np.moveaxis((codes * scale).reshape(v.shape), -1, axis)


WIDE = False


def mx_kscale(k):
    if not WIDE:
        return np.ones(k)
    levels = np.array([10, -10, 5, -5, 0])
    if k % 512:
        return np.exp2(np.random.permutation(np.resize(levels, k // 32))).repeat(32)
    a = np.empty((k // 512, 16))
    for p in range(k // 512):
        a[p, :8] = np.random.permutation(np.resize(levels, 8))
        for g in range(8):
            far = levels[np.abs(levels - a[p, g]) >= 10]
            a[p, g + 8] = far[np.random.randint(len(far))]
    return np.exp2(a.ravel()).repeat(32)


BF16 = ml_dtypes.bfloat16


def bf(x):
    return np.asarray(x, np.float32).astype(BF16)


def f64(x):
    return np.asarray(x).astype(np.float64)


B, D, K, M, T = 1024, 1024, 2, 512, 2
H = K * M


def sigmoid(v):
    return 1.0 / (1.0 + np.exp(-v))


def draw0():
    c = mx_kscale(D)
    t = mx_kscale(H)
    return {
        "x": bf(np.random.standard_normal((B, D)) * c),
        "s": bf(np.random.standard_normal((T, D))),
        "w1": bf(np.random.standard_normal((D, H)) / np.sqrt(D) / c[:, None]),
        "w2": bf(np.random.standard_normal((D, H)) / np.sqrt(D) / c[:, None]),
        "r": bf(np.random.standard_normal(H) * t),
        "wf": bf(1.5 * np.random.standard_normal((K, M, M)) / np.sqrt(M) / t.reshape(K, M)[:, :, None]),
        "a": bf(np.random.standard_normal((T, H)) * 0.7),
    }


def gated_stream(x, logits, w):
    gated = x * (2.0 * sigmoid(logits))
    return np.maximum(mxq(gated, 1, "e4m3") @ mxq(w, 0, "e4m3"), 0.0)


def headwise_product(u, wf):
    heads, width, _ = wf.shape
    u_heads = u.reshape(u.shape[0], heads, width).transpose(1, 0, 2)
    f_heads = mxq(u_heads, 2, "e4m3") @ mxq(wf, 1, "e4m3")
    return f_heads.transpose(1, 0, 2).reshape(u.shape)


def core(x, s, w1, w2, r, wf, a):
    x, s, w1, w2, r, wf, a = f64(x), f64(s), f64(w1), f64(w2), f64(r), f64(wf), f64(a)
    o1 = gated_stream(x, s[0], w1)
    o2 = gated_stream(x, s[1], w2)
    u = o1 * r
    f = headwise_product(u, wf)
    return (f + a[1]) * o2 + a[0] * o1


def e4m3fn_bytes(y):
    return np.clip(np.asarray(y, np.float64), -448.0, 448.0).astype(np.float32).astype(ml_dtypes.float8_e4m3fn).view(np.uint8)


def e4m3fn_values(b):
    return np.asarray(b, np.uint8).view(ml_dtypes.float8_e4m3fn).astype(np.float64)


def setup_inputs():
    d = draw0()
    x0 = np.asarray(d['w2']).astype(np.float64)
    s = (np.max(np.abs(x0), axis=(1,), keepdims=True) / 448.0).astype(np.float32)
    out = {}
    for k, v in d.items():
        if k == 'w2':
            out['w2_bytes'] = e4m3fn_bytes(x0 / s.astype(np.float64))
            out['w2_scale'] = s
        else:
            out[k] = v
    return out


def reference(x, s, w1, w2_bytes, w2_scale, r, wf, a):
    return core(x, s, w1, e4m3fn_values(w2_bytes) * w2_scale.astype(np.float64), r, wf, a)

@@ -1,0 +1,500 @@
+from contextlib import ExitStack
+
+import concourse.mybir as mybir
+from concourse.masks import make_identity
+
+F32 = mybir.dt.float32
+BF16 = mybir.dt.bfloat16
+U32 = mybir.dt.uint32
+U8 = mybir.dt.uint8
+FP8 = mybir.dt.float8_e4m3fn
+X4 = mybir.dt.float8_e4m3fn_x4
+ALU = mybir.AluOpType
+ACT = mybir.ActivationFunctionType
+
+B, D, HEADS, W = 1024, 1024, 2, 512
+H = HEADS * W
+FLOPS = 2 * (2 * B * D * H + HEADS * B * W * W)
+
+P = 128
+PASSES = D // 512
+TB = 256
+NB = B // TB
+TT = TB // P
+ON_GPSIMD = ()
+SPLIT = ((0, 0), (0, 1), (1, 0), (1, 1), (2, 0), (3, 0))
+EVAC_V = ((0, 0, 0), (0, 1, 1))
+
+
+def tile_finalmlptwostreamfusion_kernel(tc, x, s, w1, w2_bytes, w2_scale, r, wf, a, out):
+    nc = tc.nc
+    with ExitStack() as ctx:
+        keep = ctx.enter_context(tc.tile_pool(name="keep", bufs=1))
+        work = ctx.enter_context(tc.tile_pool(name="work", bufs=1))
+        psum = ctx.enter_context(tc.psum_pool(name="psum", bufs=1))
+
+        ident = keep.tile([P, P], F32, name="ident")
+        make_identity(nc, ident[:])
+
+        ctx.enter_context(tc.manual_schedule())
+
+        s_bf = keep.tile([P, 2 * PASSES, 4], BF16, name="s_bf")
+        nc.scalar.dma_start(out=s_bf[:], in_=s.rearrange("k (g p t) -> p (k g) t", p=P, t=4))
+        ws = keep.tile([P, PASSES, 4], F32, name="ws")
+        r_bf = keep.tile([P, HEADS, 4], BF16, name="r_bf")
+        a_bf = keep.tile([P, 2 * HEADS, 4], BF16, name="a_bf")
+
+        x_raw = [keep.tile([P, TT, D], BF16, name="x_raw%d" % b) for b in range(NB)]
+        w1_raw = [work.tile([P, 4, H], BF16, name="big", bufs=12) for g in range(PASSES)]
+        w2_raw = [keep.tile([P, 4, H], U8, name="w2_raw%d" % g) for g in range(PASSES)]
+        wf_raw = [keep.tile([P, 4, W], BF16, name="wf_raw%d" % h) for h in range(HEADS)]
+
+        def load_x(b):
+            nc.sync.dma_start(out=x_raw[b][:], in_=x[b * TB : (b + 1) * TB, :].rearrange("(i p) k -> p i k", p=P))
+
+        def load_w(dst, src):
+            nc.sync.dma_start(out=dst[:], in_=src.rearrange("(p j) n -> p j n", j=4))
+
+        for g in range(PASSES):
+            nc.sync.dma_start(
+                out=x_raw[0][:, :, g * 512 : (g + 1) * 512],
+                in_=x[0:TB, g * 512 : (g + 1) * 512].rearrange("(i p) k -> p i k", p=P),
+            )
+        load_w(w1_raw[0], w1[0:512, :])
+        load_x(1)
+        load_w(w1_raw[1], w1[512:1024, :])
+        load_x(2)
+        load_w(w2_raw[0], w2_bytes[0:512, :])
+        load_x(3)
+        load_w(w2_raw[1], w2_bytes[512:1024, :])
+        nc.sync.dma_start(out=ws[:], in_=w2_scale.rearrange("(g p t) o -> p g (t o)", p=P, t=4))
+        load_w(wf_raw[0], wf[0])
+        load_w(wf_raw[1], wf[1])
+        nc.sync.dma_start(out=r_bf[:], in_=r.rearrange("(h p t) -> p h t", p=P, t=4))
+        nc.sync.dma_start(out=a_bf[:], in_=a.rearrange("k (h p t) -> p (k h) t", p=P, t=4))
+
+        sig = keep.tile([P, 2 * PASSES, 4], F32, name="sig")
+        nc.scalar.activation(out=sig[:], in_=s_bf[:], func=ACT.Sigmoid)
+        gate = keep.tile([P, 2 * PASSES, 4], F32, name="gate")
+        nc.vector.tensor_scalar(out=gate[:], in0=sig[:], scalar1=2.0, scalar2=None, op0=ALU.mult)
+        r_f = keep.tile([P, HEADS, 4], F32, name="r_f")
+        a_f = keep.tile([P, 2 * HEADS, 4], F32, name="a_f")
+
+        def widen_vectors():
+            nc.gpsimd.tensor_copy(out=r_f[:], in_=r_bf[:])
+            nc.gpsimd.tensor_copy(out=a_f[:], in_=a_bf[:])
+
+        def planes(n, name):
+            codes = keep.tile([P, 2, n], U32, name=name + "_c", align_bytes=64)
+            scales = keep.tile([P, 2, n], U8, name=name + "_s", align_bytes=64)
+            return codes, scales
+
+        w1_q = planes(H, "w1q")
+        w2_q = planes(H, "w2q")
+        wf_q = planes(W, "wfq")
+        g_q = []
+        for k in range(2):
+            codes = keep.tile([P, NB, PASSES, TB], U32, name="g%dq_c" % k, align_bytes=64)
+            scales = keep.tile([P, NB, PASSES, TB], U8, name="g%dq_s" % k, align_bytes=64)
+            g_q.append((codes, scales))
+        u_q = planes(B, "uq")
+
+        def quantize(q, index, lo, hi, grouped):
+            codes, scales = q
+            nc.vector.quantize_mx(out=codes[:, index, lo:hi].bitcast(X4), scales=scales[:, index, lo:hi], in_=grouped)
+
+        def mx(dst, lq, li, l0, rq, ri, r0, n, start, stop):
+            nc.tensor.matmul_mx(
+                out=dst,
+                lhsT=lq[0][:, li, l0 : l0 + P].bitcast(X4),
+                lhsT_scale=lq[1][:, li, l0 : l0 + P],
+                rhs=rq[0][:, ri, r0 : r0 + n].bitcast(X4),
+                rhs_scale=rq[1][:, ri, r0 : r0 + n],
+                start=start,
+                stop=stop,
+            )
+
+        xt = {}
+
+        def turn_x(b, g):
+            if True:
+                bank = psum.tile([P, 2, TB], F32, name="t_bank", bufs=3)
+                for u in range(2):
+                    for i in range(TT):
+                        words = x_raw[b][:, i, :].bitcast(F32)
+                        nc.tensor.transpose(
+                            bank[:, u, i * P : (i + 1) * P], words[:, 256 * g + u : 256 * (g + 1) : 2], ident[:]
+                        )
+                xt[b, g] = bank
+
+        xg = {}
+
+        def gate_x(b, g):
+            if (b, 0) not in xg:
+                for k in range(2):
+                    xg[b, k] = work.tile([P, PASSES, TB, 4], BF16, name="xg", bufs=4, align_bytes=64)
+            src = xt[b, g][:].bitcast(BF16).rearrange("p u (r e) -> p r u e", e=2)
+            if True:
+                for k in range(2):
+                    factor = gate[:, 2 * k + g, :].rearrange("p (u e) -> p u e", e=2).unsqueeze(1)
+                    nc.vector.tensor_tensor(
+                        out=xg[b, k][:, g, :, :].rearrange("p r (u e) -> p r u e", e=2),
+                        in0=src,
+                        in1=factor.to_broadcast([P, TB, 2, 2]),
+                        op=ALU.mult,
+                    )
+
+        def quant_x(b, k):
+            if True:
+                codes, scales = g_q[k]
+                nc.vector.quantize_mx(
+                    out=codes[:, b, :, :].rearrange("p g n -> p (g n)").bitcast(X4),
+                    scales=scales[:, b, :, :].rearrange("p g n -> p (g n)"),
+                    in_=xg[b, k][:].rearrange("p g r t -> p (g r t)"),
+                )
+
+        wg = {}
+
+        def group_w(tag, index, h, src):
+            tile = work.tile([P, 4 * W], BF16, name="wg", bufs=4, align_bytes=64)
+            dst = tile[:].rearrange("p (t m j) -> p m t j", t=4, j=4)
+            src = src.rearrange("p j (m t) -> p m t j", t=4)
+            if (tag, index, h) in ON_GPSIMD:
+                for m in range(0, P, 32):
+                    nc.gpsimd.tensor_scalar(
+                        out=dst[:, m : m + 32, :, :],
+                        in0=src[:, m : m + 32, :, :],
+                        scalar1=1.0,
+                        scalar2=0.0,
+                        op0=ALU.mult,
+                        op1=ALU.add,
+                    )
+            else:
+                nc.scalar.copy(out=dst, in_=src)
+            wg[tag, index, h] = tile
+
+        def group_w1(h, g):
+            group_w("w1", g, h, w1_raw[g][:, :, h * W : (h + 1) * W])
+
+        def quant_w1(h, g):
+            quantize(w1_q, g, h * W, (h + 1) * W, wg["w1", g, h][:])
+
+        w2_wide = {}
+
+        def widen_w2(g, half):
+            if g not in w2_wide:
+                w2_wide[g] = work.tile([P, 4, H], BF16, name="big", bufs=12)
+            for j in (2 * half, 2 * half + 1):
+                nc.scalar.activation(
+                    out=w2_wide[g][:, j, :],
+                    in_=w2_raw[g][:, j, :].bitcast(FP8),
+                    func=ACT.Copy,
+                    scale=ws[:, g, j : j + 1],
+                )
+
+        def group_w2(h, g):
+            group_w("w2", g, h, w2_wide[g][:, :, h * W : (h + 1) * W])
+
+        def quant_w2(h, g):
+            quantize(w2_q, g, h * W, (h + 1) * W, wg["w2", g, h][:])
+
+        def group_wf(h):
+            group_w("wf", h, 0, wf_raw[h][:])
+
+        def quant_wf(h):
+            quantize(wf_q, h, 0, W, wg["wf", h, 0][:])
+
+        z1 = {}
+
+        def mul_z1(b, h):
+            for i in range(TT):
+                bank = psum.tile([P, 4, P], F32, name="z_bank", bufs=5)
+                for t in range(4):
+                    for g in range(PASSES):
+                        nc.tensor.matmul_mx(
+                            out=bank[:, t, :],
+                            lhsT=w1_q[0][:, g, h * W + t * P : h * W + (t + 1) * P].bitcast(X4),
+                            lhsT_scale=w1_q[1][:, g, h * W + t * P : h * W + (t + 1) * P],
+                            rhs=g_q[0][0][:, b, g, i * P : (i + 1) * P].bitcast(X4),
+                            rhs_scale=g_q[0][1][:, b, g, i * P : (i + 1) * P],
+                            start=(g == 0),
+                            stop=(g == PASSES - 1),
+                        )
+                z1[b, h, i] = bank
+
+        ug = {}
+        o1a = {}
+
+        def gain_z1(b, h):
+            ug[b, h] = work.tile([P, TT, P, 4], BF16, name="ug", bufs=3, align_bytes=64)
+            for i in range(TT):
+                nc.vector.scalar_tensor_tensor(
+                    out=ug[b, h][:, i, :, :],
+                    in0=z1[b, h, i][:].rearrange("p t n -> p n t"),
+                    scalar=0.0,
+                    in1=r_f[:, h, :].unsqueeze(1).to_broadcast([P, P, 4]),
+                    op0=ALU.max,
+                    op1=ALU.mult,
+                )
+
+        def linear_z1(b, h):
+            if b not in o1a:
+                o1a[b] = work.tile([P, HEADS, TT, 4, P], F32, name="big", bufs=12)
+            for i in range(TT):
+                if (b, h) in SPLIT:
+                    nc.scalar.activation(out=o1a[b][:, h, i, :, :], in_=z1[b, h, i][:], func=ACT.Relu)
+                else:
+                    nc.vector.scalar_tensor_tensor(
+                        out=o1a[b][:, h, i, :, :],
+                        in0=z1[b, h, i][:],
+                        scalar=0.0,
+                        in1=a_f[:, h, :].unsqueeze(2).to_broadcast([P, 4, P]),
+                        op0=ALU.max,
+                        op1=ALU.mult,
+                    )
+
+        def weigh_z1(b, h):
+            if (b, h) in SPLIT:
+                for t in range(4):
+                    part = o1a[b][:, h, :, t, :]
+                    nc.vector.tensor_scalar(
+                        out=part, in0=part, scalar1=a_f[:, h, t : t + 1], scalar2=None, op0=ALU.mult
+                    )
+
+        def quant_u(b, h):
+            quantize(u_q, h, b * TB, (b + 1) * TB, ug[b, h][:].rearrange("p i n t -> p (i n t)"))
+
+        z2 = {}
+        o2 = {}
+
+        def mul_z2(c, h, pair):
+            for t in (2 * pair, 2 * pair + 1):
+                bank = psum.tile([P, 2, TB], F32, name="z_bank", bufs=5)
+                for half in range(2):
+                    for g in range(PASSES):
+                        nc.tensor.matmul_mx(
+                            out=bank[:, half, :],
+                            lhsT=w2_q[0][:, g, h * W + t * P : h * W + (t + 1) * P].bitcast(X4),
+                            lhsT_scale=w2_q[1][:, g, h * W + t * P : h * W + (t + 1) * P],
+                            rhs=g_q[1][0][:, 2 * c + half, g, :].bitcast(X4),
+                            rhs_scale=g_q[1][1][:, 2 * c + half, g, :],
+                            start=(g == 0),
+                            stop=(g == PASSES - 1),
+                        )
+                z2[c, h, t] = bank
+
+        def use_z2(c, h, pair):
+            if (c, h) not in o2:
+                o2[c, h] = work.tile([P, 4, 2, TB], F32, name="big", bufs=12)
+            for t in (2 * pair, 2 * pair + 1):
+                nc.scalar.activation(out=o2[c, h][:, t, :, :], in_=z2[c, h, t][:], func=ACT.Relu)
+
+        fb = {}
+
+        def mul_f(b, h):
+            for tt in range(2):
+                bank = psum.tile([P, 2, TB], F32, name="z_bank", bufs=5)
+                for v in range(2):
+                    t = 2 * tt + v
+                    mx(bank[:, v, :], wf_q, h, t * P, u_q, h, b * TB, TB, True, True)
+                fb[b, h, tt] = bank
+
+        fused = {}
+
+        def fuse(b, h):
+            if b not in fused:
+                fused[b] = work.tile([P, HEADS, 4, TB], F32, name="big", bufs=12)
+            for t in range(4):
+                nc.vector.scalar_tensor_tensor(
+                    out=fused[b][:, h, t, :],
+                    in0=fb[b, h, t // 2][:, t % 2, :],
+                    scalar=a_f[:, HEADS + h, t : t + 1],
+                    in1=o2[b // 2, h][:, t, b % 2, :],
+                    op0=ALU.add,
+                    op1=ALU.mult,
+                )
+
+        tr = {}
+
+        def turn_out(b, h, i):
+            if True:
+                bank = psum.tile([P, 4, P], F32, name="t_bank", bufs=3)
+                for t in range(4):
+                    nc.tensor.matmul(
+                        bank[:, t, :], lhsT=o1a[b][:, h, i, t, :], rhs=ident[:], start=True, stop=False, is_transpose=True
+                    )
+                    nc.tensor.matmul(
+                        bank[:, t, :],
+                        lhsT=fused[b][:, h, t, i * P : (i + 1) * P],
+                        rhs=ident[:],
+                        start=False,
+                        stop=True,
+                        is_transpose=True,
+                    )
+                tr[b, h, i] = bank
+
+        def store(b, h, i):
+            if True:
+                rows = work.tile([P, W], F32, name="rows", bufs=6)
+                dst = rows[:].rearrange("n (m t) -> n m t", t=4)
+                src = tr[b, h, i][:].rearrange("n t m -> n m t")
+                if (b, h, i) in EVAC_V:
+                    nc.vector.tensor_copy(out=dst, in_=src)
+                else:
+                    nc.scalar.copy(out=dst, in_=src)
+                n0 = b * TB + i * P
+                nc.sync.dma_start(out=out[n0 : n0 + P, h * W : (h + 1) * W], in_=rows[:])
+
+        turn_x(0, 0)
+        widen_vectors()
+        turn_x(0, 1)
+        turn_x(1, 1)
+        gate_x(0, 0)
+        group_w1(1, 0)
+        turn_x(1, 0)
+        gate_x(0, 1)
+        quant_x(0, 0)
+        quant_w1(1, 0)
+        group_w1(0, 0)
+        gate_x(1, 1)
+        quant_x(0, 1)
+        group_w1(1, 1)
+        turn_x(2, 0)
+        gate_x(1, 0)
+        turn_x(3, 1)
+        group_w1(0, 1)
+        quant_w1(1, 1)
+        turn_x(2, 1)
+        quant_x(1, 0)
+        mul_z1(1, 1)
+        gate_x(3, 1)
+        turn_x(3, 0)
+        widen_w2(1, 0)
+        gain_z1(1, 1)
+        quant_w1(0, 0)
+        widen_w2(0, 1)
+        widen_w2(1, 1)
+        mul_z1(0, 1)
+        gate_x(3, 0)
+        quant_x(3, 0)
+        gate_x(2, 0)
+        widen_w2(0, 0)
+        gain_z1(0, 1)
+        mul_z1(3, 1)
+        gain_z1(3, 1)
+        linear_z1(1, 1)
+        gate_x(2, 1)
+        linear_z1(3, 1)
+        group_w2(1, 1)
+        group_w2(1, 0)
+        linear_z1(0, 1)
+        quant_x(2, 0)
+        quant_w2(1, 1)
+        quant_w2(1, 0)
+        quant_x(1, 1)
+        mul_z1(2, 1)
+        weigh_z1(3, 1)
+        weigh_z1(1, 1)
+        mul_z2(0, 1, 0)
+        quant_u(3, 1)
+        quant_u(1, 1)
+        mul_z2(0, 1, 1)
+        quant_x(2, 1)
+        quant_x(3, 1)
+        gain_z1(2, 1)
+        group_wf(1)
+        mul_z2(1, 1, 1)
+        mul_z2(1, 1, 0)
+        quant_wf(1)
+        mul_f(1, 1)
+        use_z2(0, 1, 0)
+        use_z2(0, 1, 1)
+        use_z2(1, 1, 1)
+        quant_w1(0, 1)
+        use_z2(1, 1, 0)
+        mul_z1(3, 0)
+        mul_f(3, 1)
+        linear_z1(2, 1)
+        fuse(1, 1)
+        turn_out(1, 1, 0)
+        mul_z1(2, 0)
+        turn_out(1, 1, 1)
+        quant_u(0, 1)
+        gain_z1(3, 0)
+        group_w2(0, 0)
+        mul_z1(0, 0)
+        fuse(3, 1)
+        gain_z1(2, 0)
+        quant_w2(0, 0)
+        group_w2(0, 1)
+        linear_z1(2, 0)
+        linear_z1(3, 0)
+        quant_w2(0, 1)
+        mul_z2(1, 0, 0)
+        quant_u(2, 1)
+        weigh_z1(0, 1)
+        mul_f(0, 1)
+        mul_z1(1, 0)
+        gain_z1(0, 0)
+        weigh_z1(2, 1)
+        mul_f(2, 1)
+        fuse(0, 1)
+        use_z2(1, 0, 0)
+        linear_z1(0, 0)
+        fuse(2, 1)
+        weigh_z1(3, 0)
+        turn_out(0, 1, 1)
+        store(1, 1, 0)
+        quant_u(2, 0)
+        turn_out(0, 1, 0)
+        mul_z2(1, 0, 1)
+        turn_out(2, 1, 1)
+        store(1, 1, 1)
+        group_wf(0)
+        store(0, 1, 1)
+        turn_out(2, 1, 0)
+        quant_u(3, 0)
+        quant_wf(0)
+        store(0, 1, 0)
+        use_z2(1, 0, 1)
+        gain_z1(1, 0)
+        mul_z2(0, 0, 1)
+        linear_z1(1, 0)
+        mul_f(2, 0)
+        turn_out(3, 1, 1)
+        weigh_z1(2, 0)
+        turn_out(3, 1, 0)
+        fuse(2, 0)
+        store(2, 1, 0)
+        mul_f(3, 0)
+        store(2, 1, 1)
+        quant_u(1, 0)
+        store(3, 1, 1)
+        fuse(3, 0)
+        turn_out(2, 0, 1)
+        turn_out(2, 0, 0)
+        use_z2(0, 0, 1)
+        store(3, 1, 0)
+        weigh_z1(1, 0)
+        store(2, 0, 1)
+        mul_z2(0, 0, 0)
+        use_z2(0, 0, 0)
+        mul_f(1, 0)
+        turn_out(3, 0, 1)
+        store(3, 0, 1)
+        weigh_z1(0, 0)
+        turn_out(3, 0, 0)
+        store(3, 0, 0)
+        quant_u(0, 0)
+        mul_f(0, 0)
+        fuse(1, 0)
+        store(2, 0, 0)
+        turn_out(1, 0, 1)
+        store(1, 0, 1)
+        turn_out(1, 0, 0)
+        store(1, 0, 0)
+        fuse(0, 0)
+        turn_out(0, 0, 1)
+        store(0, 0, 1)
+        turn_out(0, 0, 0)
+        store(0, 0, 0)

@@ -21,9 +21,6 @@ PASSES = D // 512
 TB = 256
 NB = B // TB
 TT = TB // P
-ON_GPSIMD = ()
-SPLIT = ((0, 0), (0, 1), (1, 0), (1, 1), (2, 0), (3, 0))
-EVAC_V = ((0, 0, 0), (0, 1, 1))
 
 
 def tile_finalmlptwostreamfusion_kernel(tc, x, s, w1, w2_bytes, w2_scale, r, wf, a, out):
@@ -31,7 +28,7 @@ def tile_finalmlptwostreamfusion_kernel(tc, x, s, w1, w2_bytes, w2_scale, r, wf,
     with ExitStack() as ctx:
         keep = ctx.enter_context(tc.tile_pool(name="keep", bufs=1))
         work = ctx.enter_context(tc.tile_pool(name="work", bufs=1))
-        psum = ctx.enter_context(tc.psum_pool(name="psum", bufs=1))
+        psum = ctx.enter_context(tc.psum_pool(name="psum", bufs=8))
 
         ident = keep.tile([P, P], F32, name="ident")
         make_identity(nc, ident[:])
@@ -39,462 +36,410 @@ def tile_finalmlptwostreamfusion_kernel(tc, x, s, w1, w2_bytes, w2_scale, r, wf,
         ctx.enter_context(tc.manual_schedule())
 
         s_bf = keep.tile([P, 2 * PASSES, 4], BF16, name="s_bf")
-        nc.scalar.dma_start(out=s_bf[:], in_=s.rearrange("k (g p t) -> p (k g) t", p=P, t=4))
         ws = keep.tile([P, PASSES, 4], F32, name="ws")
         r_bf = keep.tile([P, HEADS, 4], BF16, name="r_bf")
         a_bf = keep.tile([P, 2 * HEADS, 4], BF16, name="a_bf")
+        x_raw = {}
+        w1_raw = {}
+        w2_raw = {}
+        wf_raw = {}
 
-        x_raw = [keep.tile([P, TT, D], BF16, name="x_raw%d" % b) for b in range(NB)]
-        w1_raw = [work.tile([P, 4, H], BF16, name="big", bufs=12) for g in range(PASSES)]
-        w2_raw = [keep.tile([P, 4, H], U8, name="w2_raw%d" % g) for g in range(PASSES)]
-        wf_raw = [keep.tile([P, 4, W], BF16, name="wf_raw%d" % h) for h in range(HEADS)]
-
-        def load_x(b):
-            nc.sync.dma_start(out=x_raw[b][:], in_=x[b * TB : (b + 1) * TB, :].rearrange("(i p) k -> p i k", p=P))
-
-        def load_w(dst, src):
-            nc.sync.dma_start(out=dst[:], in_=src.rearrange("(p j) n -> p j n", j=4))
-
-        for g in range(PASSES):
+        def load_x(c, g):
+            x_raw[c, g] = keep.tile([P, TT, 512], BF16, name="x_raw%d_%d" % (c, g))
             nc.sync.dma_start(
-                out=x_raw[0][:, :, g * 512 : (g + 1) * 512],
-                in_=x[0:TB, g * 512 : (g + 1) * 512].rearrange("(i p) k -> p i k", p=P),
+                out=x_raw[c, g][:],
+                in_=x[c * TB : (c + 1) * TB, g * 512 : (g + 1) * 512].rearrange("(i p) k -> p i k", p=P),
             )
-        load_w(w1_raw[0], w1[0:512, :])
-        load_x(1)
-        load_w(w1_raw[1], w1[512:1024, :])
-        load_x(2)
-        load_w(w2_raw[0], w2_bytes[0:512, :])
-        load_x(3)
-        load_w(w2_raw[1], w2_bytes[512:1024, :])
-        nc.sync.dma_start(out=ws[:], in_=w2_scale.rearrange("(g p t) o -> p g (t o)", p=P, t=4))
-        load_w(wf_raw[0], wf[0])
-        load_w(wf_raw[1], wf[1])
+
+        def load_w1(h, g):
+            w1_raw[h, g] = keep.tile([P, 4, W], BF16, name="w1_raw%d_%d" % (h, g))
+            nc.sync.dma_start(
+                out=w1_raw[h, g][:],
+                in_=w1[g * 512 : (g + 1) * 512, h * W : (h + 1) * W].rearrange("(p j) n -> p j n", j=4),
+            )
+
+        def load_w2(g):
+            w2_raw[g] = keep.tile([P, 4, H], U8, name="w2_raw%d" % g)
+            nc.sync.dma_start(
+                out=w2_raw[g][:], in_=w2_bytes[g * 512 : (g + 1) * 512, :].rearrange("(p j) n -> p j n", j=4)
+            )
+
+        def load_wf(h):
+            wf_raw[h] = keep.tile([P, 4, W], BF16, name="wf_raw%d" % h)
+            nc.sync.dma_start(out=wf_raw[h][:], in_=wf[h].rearrange("(p j) n -> p j n", j=4))
+
+        nc.scalar.dma_start(out=s_bf[:], in_=s.rearrange("k (g p t) -> p (k g) t", p=P, t=4))
+        nc.scalar.dma_start(out=ws[:], in_=w2_scale.rearrange("(g p t) o -> p g (t o)", p=P, t=4))
+        load_x(0, 0)
+        load_w2(0)
+        load_x(0, 1)
+        load_w1(0, 0)
+        load_w1(0, 1)
+        load_w2(1)
+        load_x(1, 0)
+        load_x(1, 1)
+        load_wf(0)
         nc.sync.dma_start(out=r_bf[:], in_=r.rearrange("(h p t) -> p h t", p=P, t=4))
         nc.sync.dma_start(out=a_bf[:], in_=a.rearrange("k (h p t) -> p (k h) t", p=P, t=4))
+        load_w1(1, 0)
+        load_w1(1, 1)
+        load_x(2, 0)
+        load_wf(1)
+        load_x(2, 1)
+        load_x(3, 0)
+        load_x(3, 1)
 
         sig = keep.tile([P, 2 * PASSES, 4], F32, name="sig")
         nc.scalar.activation(out=sig[:], in_=s_bf[:], func=ACT.Sigmoid)
         gate = keep.tile([P, 2 * PASSES, 4], F32, name="gate")
         nc.vector.tensor_scalar(out=gate[:], in0=sig[:], scalar1=2.0, scalar2=None, op0=ALU.mult)
+        ident_bf = keep.tile([P, P], BF16, name="ident_bf")
+        nc.scalar.copy(out=ident_bf[:], in_=ident[:])
         r_f = keep.tile([P, HEADS, 4], F32, name="r_f")
         a_f = keep.tile([P, 2 * HEADS, 4], F32, name="a_f")
+        nc.gpsimd.tensor_copy(out=r_f[:], in_=r_bf[:])
+        nc.gpsimd.tensor_copy(out=a_f[:], in_=a_bf[:])
 
-        def widen_vectors():
-            nc.gpsimd.tensor_copy(out=r_f[:], in_=r_bf[:])
-            nc.gpsimd.tensor_copy(out=a_f[:], in_=a_bf[:])
-
-        def planes(n, name):
-            codes = keep.tile([P, 2, n], U32, name=name + "_c", align_bytes=64)
-            scales = keep.tile([P, 2, n], U8, name=name + "_s", align_bytes=64)
+        def planes(shape, name):
+            codes = keep.tile([P] + shape, U32, name=name + "_c", align_bytes=64)
+            scales = keep.tile([P] + shape, U8, name=name + "_s", align_bytes=64)
             return codes, scales
 
-        w1_q = planes(H, "w1q")
-        w2_q = planes(H, "w2q")
-        wf_q = planes(W, "wfq")
-        g_q = []
-        for k in range(2):
-            codes = keep.tile([P, NB, PASSES, TB], U32, name="g%dq_c" % k, align_bytes=64)
-            scales = keep.tile([P, NB, PASSES, TB], U8, name="g%dq_s" % k, align_bytes=64)
-            g_q.append((codes, scales))
-        u_q = planes(B, "uq")
+        w_q = {}
+        g_q = {}
+        u_q = {}
 
-        def quantize(q, index, lo, hi, grouped):
-            codes, scales = q
-            nc.vector.quantize_mx(out=codes[:, index, lo:hi].bitcast(X4), scales=scales[:, index, lo:hi], in_=grouped)
+        def quantize(q, grouped):
+            nc.vector.quantize_mx(out=q[0].bitcast(X4), scales=q[1], in_=grouped)
 
-        def mx(dst, lq, li, l0, rq, ri, r0, n, start, stop):
+        def mx(dst, lq, l0, rq, r0, n, start, stop):
             nc.tensor.matmul_mx(
                 out=dst,
-                lhsT=lq[0][:, li, l0 : l0 + P].bitcast(X4),
-                lhsT_scale=lq[1][:, li, l0 : l0 + P],
-                rhs=rq[0][:, ri, r0 : r0 + n].bitcast(X4),
-                rhs_scale=rq[1][:, ri, r0 : r0 + n],
+                lhsT=lq[0][:, l0 : l0 + P].bitcast(X4),
+                lhsT_scale=lq[1][:, l0 : l0 + P],
+                rhs=rq[0][:, r0 : r0 + n].bitcast(X4),
+                rhs_scale=rq[1][:, r0 : r0 + n],
                 start=start,
                 stop=stop,
             )
 
         xt = {}
-
-        def turn_x(b, g):
-            if True:
-                bank = psum.tile([P, 2, TB], F32, name="t_bank", bufs=3)
-                for u in range(2):
-                    for i in range(TT):
-                        words = x_raw[b][:, i, :].bitcast(F32)
-                        nc.tensor.transpose(
-                            bank[:, u, i * P : (i + 1) * P], words[:, 256 * g + u : 256 * (g + 1) : 2], ident[:]
-                        )
-                xt[b, g] = bank
-
         xg = {}
 
-        def gate_x(b, g):
-            if (b, 0) not in xg:
-                for k in range(2):
-                    xg[b, k] = work.tile([P, PASSES, TB, 4], BF16, name="xg", bufs=4, align_bytes=64)
-            src = xt[b, g][:].bitcast(BF16).rearrange("p u (r e) -> p r u e", e=2)
-            if True:
-                for k in range(2):
-                    factor = gate[:, 2 * k + g, :].rearrange("p (u e) -> p u e", e=2).unsqueeze(1)
-                    nc.vector.tensor_tensor(
-                        out=xg[b, k][:, g, :, :].rearrange("p r (u e) -> p r u e", e=2),
-                        in0=src,
-                        in1=factor.to_broadcast([P, TB, 2, 2]),
-                        op=ALU.mult,
-                    )
+        def turn_x(c, g):
+            xt[c, g] = psum.tile([P, 2, TB], F32, name="bank")
+            for u in range(2):
+                for i in range(TT):
+                    words = x_raw[c, g][:, i, :].bitcast(F32)
+                    nc.tensor.transpose(xt[c, g][:, u, i * P : (i + 1) * P], words[:, u::2], ident[:])
 
-        def quant_x(b, k):
-            if True:
-                codes, scales = g_q[k]
-                nc.vector.quantize_mx(
-                    out=codes[:, b, :, :].rearrange("p g n -> p (g n)").bitcast(X4),
-                    scales=scales[:, b, :, :].rearrange("p g n -> p (g n)"),
-                    in_=xg[b, k][:].rearrange("p g r t -> p (g r t)"),
-                )
+        def gate_x(c, g, k):
+            xg[c, g, k] = work.tile([P, TB, 4], BF16, name="xg", bufs=4, align_bytes=64)
+            src = xt[c, g][:].bitcast(BF16).rearrange("p u (n e) -> p n u e", e=2)
+            factor = gate[:, PASSES * k + g, :].rearrange("p (u e) -> p u e", e=2).unsqueeze(1)
+            nc.vector.tensor_tensor(
+                out=xg[c, g, k][:].rearrange("p n (u e) -> p n u e", e=2),
+                in0=src,
+                in1=factor.to_broadcast([P, TB, 2, 2]),
+                op=ALU.mult,
+            )
 
+        def quant_x(c, g, k):
+            codes, scales = planes([TB], "g%dq%d_%d" % (k, c, g))
+            g_q[c, g, k] = (codes, scales)
+            quantize((codes[:], scales[:]), xg[c, g, k][:].rearrange("p n t -> p (n t)"))
+
+        rows4 = {}
+        mixed = {}
         wg = {}
 
-        def group_w(tag, index, h, src):
-            tile = work.tile([P, 4 * W], BF16, name="wg", bufs=4, align_bytes=64)
-            dst = tile[:].rearrange("p (t m j) -> p m t j", t=4, j=4)
-            src = src.rearrange("p j (m t) -> p m t j", t=4)
-            if (tag, index, h) in ON_GPSIMD:
+        def widen_w2(h, g, eng):
+            wide = work.tile([P, 4, W], BF16, name="wide", bufs=3)
+            rows4["w2", h, g] = wide
+            for j in range(4):
+                src = w2_raw[g][:, j, h * W : (h + 1) * W].bitcast(FP8)
+                if eng == "v":
+                    nc.vector.tensor_scalar(
+                        out=wide[:, j, :], in0=src, scalar1=ws[:, g, j : j + 1], scalar2=None, op0=ALU.mult
+                    )
+                else:
+                    nc.scalar.activation(out=wide[:, j, :], in_=src, func=ACT.Copy, scale=ws[:, g, j : j + 1])
+
+        def mix_w(key):
+            src = rows4[key][:].rearrange("p j n -> p n j")
+            for half in range(2):
+                bank = psum.tile([P, 2, P, 4], BF16, name="bank")
+                for v in range(2):
+                    n0 = (2 * half + v) * P
+                    nc.tensor.matmul(bank[:, v, :, :], lhsT=ident_bf[:], rhs=src[:, n0 : n0 + P, :], start=True, stop=True)
+                mixed[key, half] = bank
+
+        def take_w(key):
+            wg[key] = work.tile([P, 4 * W], BF16, name="wg", bufs=4, align_bytes=64)
+            dst = wg[key][:].bitcast(F32).rearrange("p (t m v) -> p t m v", t=4, v=2)
+            for half in range(2):
+                src = mixed[key, half][:].rearrange("p a n j -> p (a n j)").bitcast(F32)
+                nc.scalar.copy(
+                    out=dst[:, :, 64 * half : 64 * (half + 1), :], in_=src.rearrange("p (m t v) -> p t m v", t=4, v=2)
+                )
+
+        def group_w(key, eng):
+            wg[key] = work.tile([P, 4 * W], BF16, name="wg", bufs=4, align_bytes=64)
+            dst = wg[key][:].rearrange("p (t m j) -> p m t j", t=4, j=4)
+            src = rows4[key][:].rearrange("p j (m t) -> p m t j", t=4)
+            if eng == "v":
+                nc.vector.tensor_copy(out=dst, in_=src)
+            elif eng == "g":
                 for m in range(0, P, 32):
                     nc.gpsimd.tensor_scalar(
-                        out=dst[:, m : m + 32, :, :],
-                        in0=src[:, m : m + 32, :, :],
-                        scalar1=1.0,
-                        scalar2=0.0,
-                        op0=ALU.mult,
-                        op1=ALU.add,
+                        out=dst[:, m : m + 32, :, :], in0=src[:, m : m + 32, :, :], scalar1=1.0, scalar2=0.0, op0=ALU.mult, op1=ALU.add
                     )
             else:
                 nc.scalar.copy(out=dst, in_=src)
-            wg[tag, index, h] = tile
 
-        def group_w1(h, g):
-            group_w("w1", g, h, w1_raw[g][:, :, h * W : (h + 1) * W])
+        def quant_w(key):
+            codes, scales = planes([W], "%sq%d_%d" % key)
+            w_q[key] = (codes, scales)
+            quantize((codes[:], scales[:]), wg[key][:])
 
-        def quant_w1(h, g):
-            quantize(w1_q, g, h * W, (h + 1) * W, wg["w1", g, h][:])
-
-        w2_wide = {}
-
-        def widen_w2(g, half):
-            if g not in w2_wide:
-                w2_wide[g] = work.tile([P, 4, H], BF16, name="big", bufs=12)
-            for j in (2 * half, 2 * half + 1):
-                nc.scalar.activation(
-                    out=w2_wide[g][:, j, :],
-                    in_=w2_raw[g][:, j, :].bitcast(FP8),
-                    func=ACT.Copy,
-                    scale=ws[:, g, j : j + 1],
-                )
-
-        def group_w2(h, g):
-            group_w("w2", g, h, w2_wide[g][:, :, h * W : (h + 1) * W])
-
-        def quant_w2(h, g):
-            quantize(w2_q, g, h * W, (h + 1) * W, wg["w2", g, h][:])
-
-        def group_wf(h):
-            group_w("wf", h, 0, wf_raw[h][:])
-
-        def quant_wf(h):
-            quantize(wf_q, h, 0, W, wg["wf", h, 0][:])
+        for h in range(HEADS):
+            rows4["wf", h, 0] = wf_raw[h]
+            for g in range(PASSES):
+                rows4["w1", h, g] = w1_raw[h, g]
 
         z1 = {}
+        ug = {}
+        o1 = {}
 
-        def mul_z1(b, h):
+        def mul_z1(c, h):
             for i in range(TT):
-                bank = psum.tile([P, 4, P], F32, name="z_bank", bufs=5)
+                z1[c, h, i] = psum.tile([P, 4, P], F32, name="bank")
                 for t in range(4):
                     for g in range(PASSES):
-                        nc.tensor.matmul_mx(
-                            out=bank[:, t, :],
-                            lhsT=w1_q[0][:, g, h * W + t * P : h * W + (t + 1) * P].bitcast(X4),
-                            lhsT_scale=w1_q[1][:, g, h * W + t * P : h * W + (t + 1) * P],
-                            rhs=g_q[0][0][:, b, g, i * P : (i + 1) * P].bitcast(X4),
-                            rhs_scale=g_q[0][1][:, b, g, i * P : (i + 1) * P],
-                            start=(g == 0),
-                            stop=(g == PASSES - 1),
-                        )
-                z1[b, h, i] = bank
+                        mx(z1[c, h, i][:, t, :], w_q["w1", h, g], t * P, g_q[c, g, 0], i * P, P, g == 0, g == PASSES - 1)
 
-        ug = {}
-        o1a = {}
-
-        def gain_z1(b, h):
-            ug[b, h] = work.tile([P, TT, P, 4], BF16, name="ug", bufs=3, align_bytes=64)
+        def gain_z1(c, h):
+            ug[c, h] = work.tile([P, TT, P, 4], BF16, name="ug", bufs=3, align_bytes=64)
             for i in range(TT):
                 nc.vector.scalar_tensor_tensor(
-                    out=ug[b, h][:, i, :, :],
-                    in0=z1[b, h, i][:].rearrange("p t n -> p n t"),
+                    out=ug[c, h][:, i, :, :],
+                    in0=z1[c, h, i][:].rearrange("p t n -> p n t"),
                     scalar=0.0,
                     in1=r_f[:, h, :].unsqueeze(1).to_broadcast([P, P, 4]),
                     op0=ALU.max,
                     op1=ALU.mult,
                 )
 
-        def linear_z1(b, h):
-            if b not in o1a:
-                o1a[b] = work.tile([P, HEADS, TT, 4, P], F32, name="big", bufs=12)
+        def relu_z1(c, h):
+            o1[c, h] = work.tile([P, 4, TB], F32, name="o1", bufs=4)
             for i in range(TT):
-                if (b, h) in SPLIT:
-                    nc.scalar.activation(out=o1a[b][:, h, i, :, :], in_=z1[b, h, i][:], func=ACT.Relu)
+                nc.scalar.activation(out=o1[c, h][:, :, i * P : (i + 1) * P], in_=z1[c, h, i][:], func=ACT.Relu)
+
+        def weigh_o1(c, h, eng):
+            for t in range(4):
+                part = o1[c, h][:, t, :]
+                if eng == "v":
+                    nc.vector.tensor_scalar(out=part, in0=part, scalar1=a_f[:, h, t : t + 1], scalar2=None, op0=ALU.mult)
+                elif eng == "g":
+                    nc.gpsimd.tensor_scalar(
+                        out=part, in0=part, scalar1=a_f[:, h, t : t + 1], scalar2=0.0, op0=ALU.mult, op1=ALU.add
+                    )
                 else:
-                    nc.vector.scalar_tensor_tensor(
-                        out=o1a[b][:, h, i, :, :],
-                        in0=z1[b, h, i][:],
-                        scalar=0.0,
-                        in1=a_f[:, h, :].unsqueeze(2).to_broadcast([P, 4, P]),
-                        op0=ALU.max,
-                        op1=ALU.mult,
-                    )
+                    nc.scalar.activation(out=part, in_=part, func=ACT.Copy, scale=a_f[:, h, t : t + 1])
 
-        def weigh_z1(b, h):
-            if (b, h) in SPLIT:
-                for t in range(4):
-                    part = o1a[b][:, h, :, t, :]
-                    nc.vector.tensor_scalar(
-                        out=part, in0=part, scalar1=a_f[:, h, t : t + 1], scalar2=None, op0=ALU.mult
-                    )
-
-        def quant_u(b, h):
-            quantize(u_q, h, b * TB, (b + 1) * TB, ug[b, h][:].rearrange("p i n t -> p (i n t)"))
+        def quant_u(c, h):
+            codes, scales = planes([TB], "uq%d_%d" % (c, h))
+            u_q[c, h] = (codes, scales)
+            quantize((codes[:], scales[:]), ug[c, h][:].rearrange("p i n t -> p (i n t)"))
 
         z2 = {}
         o2 = {}
 
-        def mul_z2(c, h, pair):
-            for t in (2 * pair, 2 * pair + 1):
-                bank = psum.tile([P, 2, TB], F32, name="z_bank", bufs=5)
-                for half in range(2):
+        def mul_z2(c, h):
+            for pair in range(2):
+                z2[c, h, pair] = psum.tile([P, 2, TB], F32, name="bank")
+                for v in range(2):
                     for g in range(PASSES):
-                        nc.tensor.matmul_mx(
-                            out=bank[:, half, :],
-                            lhsT=w2_q[0][:, g, h * W + t * P : h * W + (t + 1) * P].bitcast(X4),
-                            lhsT_scale=w2_q[1][:, g, h * W + t * P : h * W + (t + 1) * P],
-                            rhs=g_q[1][0][:, 2 * c + half, g, :].bitcast(X4),
-                            rhs_scale=g_q[1][1][:, 2 * c + half, g, :],
-                            start=(g == 0),
-                            stop=(g == PASSES - 1),
-                        )
-                z2[c, h, t] = bank
+                        t = 2 * pair + v
+                        mx(z2[c, h, pair][:, v, :], w_q["w2", h, g], t * P, g_q[c, g, 1], 0, TB, g == 0, g == PASSES - 1)
 
-        def use_z2(c, h, pair):
-            if (c, h) not in o2:
-                o2[c, h] = work.tile([P, 4, 2, TB], F32, name="big", bufs=12)
-            for t in (2 * pair, 2 * pair + 1):
-                nc.scalar.activation(out=o2[c, h][:, t, :, :], in_=z2[c, h, t][:], func=ACT.Relu)
+        def relu_z2(c, h):
+            o2[c, h] = work.tile([P, 4, TB], F32, name="o2", bufs=4)
+            for pair in range(2):
+                nc.scalar.activation(out=o2[c, h][:, 2 * pair : 2 * pair + 2, :], in_=z2[c, h, pair][:], func=ACT.Relu)
 
         fb = {}
-
-        def mul_f(b, h):
-            for tt in range(2):
-                bank = psum.tile([P, 2, TB], F32, name="z_bank", bufs=5)
-                for v in range(2):
-                    t = 2 * tt + v
-                    mx(bank[:, v, :], wf_q, h, t * P, u_q, h, b * TB, TB, True, True)
-                fb[b, h, tt] = bank
-
         fused = {}
+        tr = {}
 
-        def fuse(b, h):
-            if b not in fused:
-                fused[b] = work.tile([P, HEADS, 4, TB], F32, name="big", bufs=12)
-            for t in range(4):
+        def mul_f(c, h):
+            for pair in range(2):
+                fb[c, h, pair] = psum.tile([P, 2, TB], F32, name="bank")
+                for v in range(2):
+                    mx(fb[c, h, pair][:, v, :], w_q["wf", h, 0], (2 * pair + v) * P, u_q[c, h], 0, TB, True, True)
+
+        def fuse(c, h, pair):
+            if pair == 0:
+                fused[c, h] = work.tile([P, 4, TB], F32, name="fused", bufs=3)
+            for t in (2 * pair, 2 * pair + 1):
                 nc.vector.scalar_tensor_tensor(
-                    out=fused[b][:, h, t, :],
-                    in0=fb[b, h, t // 2][:, t % 2, :],
+                    out=fused[c, h][:, t, :],
+                    in0=fb[c, h, t // 2][:, t % 2, :],
                     scalar=a_f[:, HEADS + h, t : t + 1],
-                    in1=o2[b // 2, h][:, t, b % 2, :],
+                    in1=o2[c, h][:, t, :],
                     op0=ALU.add,
                     op1=ALU.mult,
                 )
 
-        tr = {}
+        def merge(c, h):
+            for t in range(4):
+                nc.vector.scalar_tensor_tensor(
+                    out=fused[c, h][:, t, :],
+                    in0=o1[c, h][:, t, :],
+                    scalar=a_f[:, h, t : t + 1],
+                    in1=fused[c, h][:, t, :],
+                    op0=ALU.mult,
+                    op1=ALU.add,
+                )
 
-        def turn_out(b, h, i):
-            if True:
-                bank = psum.tile([P, 4, P], F32, name="t_bank", bufs=3)
+        def turn_out(c, h, terms, tiles):
+            for i in tiles:
+                bank = psum.tile([P, 4, P], F32, name="bank")
                 for t in range(4):
-                    nc.tensor.matmul(
-                        bank[:, t, :], lhsT=o1a[b][:, h, i, t, :], rhs=ident[:], start=True, stop=False, is_transpose=True
-                    )
-                    nc.tensor.matmul(
-                        bank[:, t, :],
-                        lhsT=fused[b][:, h, t, i * P : (i + 1) * P],
-                        rhs=ident[:],
-                        start=False,
-                        stop=True,
-                        is_transpose=True,
-                    )
-                tr[b, h, i] = bank
+                    for j, term in enumerate(terms):
+                        nc.tensor.matmul(
+                            bank[:, t, :],
+                            lhsT=term[c, h][:, t, i * P : (i + 1) * P],
+                            rhs=ident[:],
+                            start=j == 0,
+                            stop=j == len(terms) - 1,
+                            is_transpose=True,
+                        )
+                tr[c, h, i] = bank
 
-        def store(b, h, i):
-            if True:
+        def store(c, h, tiles, eng="s"):
+            for i in tiles:
                 rows = work.tile([P, W], F32, name="rows", bufs=6)
                 dst = rows[:].rearrange("n (m t) -> n m t", t=4)
-                src = tr[b, h, i][:].rearrange("n t m -> n m t")
-                if (b, h, i) in EVAC_V:
+                src = tr[c, h, i][:].rearrange("n t m -> n m t")
+                if eng == "v":
                     nc.vector.tensor_copy(out=dst, in_=src)
                 else:
                     nc.scalar.copy(out=dst, in_=src)
-                n0 = b * TB + i * P
+                n0 = c * TB + i * P
                 nc.sync.dma_start(out=out[n0 : n0 + P, h * W : (h + 1) * W], in_=rows[:])
 
+        units = [(0, 0), (1, 0), (0, 1), (1, 1), (2, 0), (2, 1), (3, 0), (3, 1)]
+        gates = {-1: (1, 0), 0: (1, 1), 1: (2, 0), 3: (2, 1), 4: (3, 0), 5: (3, 1)}
+        A0, A1, B0, B1, F0 = ("w1", 0, 0), ("w1", 0, 1), ("w2", 0, 0), ("w2", 0, 1), ("wf", 0, 0)
+        C0, C1, D0, D1, F1 = ("w1", 1, 0), ("w1", 1, 1), ("w2", 1, 0), ("w2", 1, 1), ("wf", 1, 0)
         turn_x(0, 0)
-        widen_vectors()
         turn_x(0, 1)
-        turn_x(1, 1)
-        gate_x(0, 0)
-        group_w1(1, 0)
+        widen_w2(0, 0, "s")
+        gate_x(0, 0, 0)
+        gate_x(0, 0, 1)
+        mix_w(A0)
+        take_w(A0)
+        quant_x(0, 0, 0)
+        gate_x(0, 1, 0)
+        quant_x(0, 0, 1)
+        mix_w(A1)
+        take_w(A1)
+        gate_x(0, 1, 1)
+        quant_x(0, 1, 0)
         turn_x(1, 0)
-        gate_x(0, 1)
-        quant_x(0, 0)
-        quant_w1(1, 0)
-        group_w1(0, 0)
-        gate_x(1, 1)
-        quant_x(0, 1)
-        group_w1(1, 1)
-        turn_x(2, 0)
-        gate_x(1, 0)
-        turn_x(3, 1)
-        group_w1(0, 1)
-        quant_w1(1, 1)
-        turn_x(2, 1)
-        quant_x(1, 0)
-        mul_z1(1, 1)
-        gate_x(3, 1)
-        turn_x(3, 0)
-        widen_w2(1, 0)
-        gain_z1(1, 1)
-        quant_w1(0, 0)
-        widen_w2(0, 1)
-        widen_w2(1, 1)
-        mul_z1(0, 1)
-        gate_x(3, 0)
-        quant_x(3, 0)
-        gate_x(2, 0)
-        widen_w2(0, 0)
-        gain_z1(0, 1)
-        mul_z1(3, 1)
-        gain_z1(3, 1)
-        linear_z1(1, 1)
-        gate_x(2, 1)
-        linear_z1(3, 1)
-        group_w2(1, 1)
-        group_w2(1, 0)
-        linear_z1(0, 1)
-        quant_x(2, 0)
-        quant_w2(1, 1)
-        quant_w2(1, 0)
-        quant_x(1, 1)
-        mul_z1(2, 1)
-        weigh_z1(3, 1)
-        weigh_z1(1, 1)
-        mul_z2(0, 1, 0)
-        quant_u(3, 1)
-        quant_u(1, 1)
-        mul_z2(0, 1, 1)
-        quant_x(2, 1)
-        quant_x(3, 1)
-        gain_z1(2, 1)
-        group_wf(1)
-        mul_z2(1, 1, 1)
-        mul_z2(1, 1, 0)
-        quant_wf(1)
-        mul_f(1, 1)
-        use_z2(0, 1, 0)
-        use_z2(0, 1, 1)
-        use_z2(1, 1, 1)
-        quant_w1(0, 1)
-        use_z2(1, 1, 0)
-        mul_z1(3, 0)
-        mul_f(3, 1)
-        linear_z1(2, 1)
-        fuse(1, 1)
-        turn_out(1, 1, 0)
-        mul_z1(2, 0)
-        turn_out(1, 1, 1)
-        quant_u(0, 1)
-        gain_z1(3, 0)
-        group_w2(0, 0)
+        mix_w(B0)
+        widen_w2(0, 1, "s")
+        take_w(B0)
+        quant_w(A0)
+        quant_x(0, 1, 1)
+        quant_w(A1)
+        gate_x(1, 0, 0)
         mul_z1(0, 0)
-        fuse(3, 1)
-        gain_z1(2, 0)
-        quant_w2(0, 0)
-        group_w2(0, 1)
-        linear_z1(2, 0)
-        linear_z1(3, 0)
-        quant_w2(0, 1)
-        mul_z2(1, 0, 0)
-        quant_u(2, 1)
-        weigh_z1(0, 1)
-        mul_f(0, 1)
-        mul_z1(1, 0)
+        gate_x(1, 0, 1)
+        mix_w(B1)
+        turn_x(1, 1)
+        quant_x(1, 0, 0)
         gain_z1(0, 0)
-        weigh_z1(2, 1)
-        mul_f(2, 1)
-        fuse(0, 1)
-        use_z2(1, 0, 0)
-        linear_z1(0, 0)
-        fuse(2, 1)
-        weigh_z1(3, 0)
-        turn_out(0, 1, 1)
-        store(1, 1, 0)
-        quant_u(2, 0)
-        turn_out(0, 1, 0)
-        mul_z2(1, 0, 1)
-        turn_out(2, 1, 1)
-        store(1, 1, 1)
-        group_wf(0)
-        store(0, 1, 1)
-        turn_out(2, 1, 0)
-        quant_u(3, 0)
-        quant_wf(0)
-        store(0, 1, 0)
-        use_z2(1, 0, 1)
-        gain_z1(1, 0)
-        mul_z2(0, 0, 1)
-        linear_z1(1, 0)
-        mul_f(2, 0)
-        turn_out(3, 1, 1)
-        weigh_z1(2, 0)
-        turn_out(3, 1, 0)
-        fuse(2, 0)
-        store(2, 1, 0)
-        mul_f(3, 0)
-        store(2, 1, 1)
-        quant_u(1, 0)
-        store(3, 1, 1)
-        fuse(3, 0)
-        turn_out(2, 0, 1)
-        turn_out(2, 0, 0)
-        use_z2(0, 0, 1)
-        store(3, 1, 0)
-        weigh_z1(1, 0)
-        store(2, 0, 1)
-        mul_z2(0, 0, 0)
-        use_z2(0, 0, 0)
-        mul_f(1, 0)
-        turn_out(3, 0, 1)
-        store(3, 0, 1)
-        weigh_z1(0, 0)
-        turn_out(3, 0, 0)
-        store(3, 0, 0)
+        take_w(B1)
+        relu_z1(0, 0)
+        quant_x(1, 0, 1)
+        quant_w(B0)
         quant_u(0, 0)
-        mul_f(0, 0)
-        fuse(1, 0)
-        store(2, 0, 0)
-        turn_out(1, 0, 1)
-        store(1, 0, 1)
-        turn_out(1, 0, 0)
-        store(1, 0, 0)
-        fuse(0, 0)
-        turn_out(0, 0, 1)
-        store(0, 0, 1)
-        turn_out(0, 0, 0)
-        store(0, 0, 0)
+        quant_w(B1)
+        last = len(units) - 1
+        both = (o1, fused)
+        for n in range(last + 2):
+            cur = units[n] if n <= last else None
+            nxt = units[n + 1] if n < last else None
+            prev = units[n - 1] if n >= 1 else None
+            old = units[n - 2] if n >= 2 else None
+            gt = gates.get(n)
+            if cur:
+                mul_z2(*cur)
+            if old:
+                turn_out(*old, both, (1,))
+                store(*old, (0,))
+            if n == 0:
+                mix_w(C0)
+                take_w(C0)
+                mix_w(C1)
+                take_w(C1)
+            if n == 1:
+                mix_w(D0)
+                take_w(D0)
+                widen_w2(1, 1, "s")
+            if gt:
+                gate_x(*gt, 0)
+            if n == 0:
+                group_w(F0, "v")
+            if n == 2:
+                group_w(F1, "v")
+            if prev:
+                fuse(*prev, 0)
+            if gt:
+                quant_x(*gt, 0)
+            if n == 0:
+                quant_w(F0)
+            if n == 2:
+                quant_w(F1)
+            if prev:
+                fuse(*prev, 1)
+            if nxt:
+                mul_z1(*nxt)
+            if cur:
+                relu_z2(*cur)
+                mul_f(*cur)
+            if old:
+                store(*old, (1,))
+            if n == 1:
+                mix_w(D1)
+                take_w(D1)
+            if n == 0:
+                widen_w2(1, 0, "s")
+            if gt:
+                gate_x(*gt, 1)
+            if cur:
+                weigh_o1(*cur, "v" if n < 2 else "s")
+            if nxt:
+                gain_z1(*nxt)
+                relu_z1(*nxt)
+            if gt:
+                quant_x(*gt, 1)
+            if n == 0:
+                quant_w(C0)
+            if n == 1:
+                quant_w(D0)
+            if nxt:
+                quant_u(*nxt)
+            if n == 0:
+                quant_w(C1)
+            if n == 1:
+                quant_w(D1)
+            if gates.get(n + 1):
+                turn_x(*gates[n + 1])
+            if prev:
+                turn_out(*prev, both, (0,))
+        turn_out(*units[last], both, (1,))
+        store(*units[last], (0,), "v")
+        store(*units[last], (1,))

@@ -166,12 +166,13 @@ def tile_finalmlptwostreamfusion_kernel(tc, x, s, w1, w2_bytes, w2_scale, r, wf,
                     nc.scalar.activation(out=wide[:, j, :], in_=src, func=ACT.Copy, scale=ws[:, g, j : j + 1])
 
         def mix_w(key):
-            src = rows4[key][:].rearrange("p j n -> p n j")
+            src = rows4[key]
             for half in range(2):
                 bank = psum.tile([P, 2, P, 4], BF16, name="bank")
                 for v in range(2):
                     n0 = (2 * half + v) * P
-                    nc.tensor.matmul(bank[:, v, :, :], lhsT=ident_bf[:], rhs=src[:, n0 : n0 + P, :], start=True, stop=True)
+                    dst = bank[:, v, :, :].rearrange("p n j -> p j n")
+                    nc.tensor.matmul(dst, lhsT=ident_bf[:], rhs=src[:, :, n0 : n0 + P], start=True, stop=True)
                 mixed[key, half] = bank
 
         def take_w(key):

@@ -21,6 +21,7 @@ PASSES = D // 512
 TB = 256
 NB = B // TB
 TT = TB // P
+MERGED = (5, 6)
 
 
 def tile_finalmlptwostreamfusion_kernel(tc, x, s, w1, w2_bytes, w2_scale, r, wf, a, out):
@@ -69,16 +70,16 @@ def tile_finalmlptwostreamfusion_kernel(tc, x, s, w1, w2_bytes, w2_scale, r, wf,
             nc.sync.dma_start(out=wf_raw[h][:], in_=wf[h].rearrange("(p j) n -> p j n", j=4))
 
         nc.scalar.dma_start(out=s_bf[:], in_=s.rearrange("k (g p t) -> p (k g) t", p=P, t=4))
-        nc.scalar.dma_start(out=ws[:], in_=w2_scale.rearrange("(g p t) o -> p g (t o)", p=P, t=4))
         load_x(0, 0)
-        load_w2(0)
-        load_x(0, 1)
         load_w1(0, 0)
+        load_x(0, 1)
         load_w1(0, 1)
-        load_w2(1)
+        nc.scalar.dma_start(out=ws[:], in_=w2_scale.rearrange("(g p t) o -> p g (t o)", p=P, t=4))
+        load_w2(0)
         load_x(1, 0)
         load_x(1, 1)
         load_wf(0)
+        load_w2(1)
         nc.sync.dma_start(out=r_bf[:], in_=r.rearrange("(h p t) -> p h t", p=P, t=4))
         nc.sync.dma_start(out=a_bf[:], in_=a.rearrange("k (h p t) -> p (k h) t", p=P, t=4))
         load_w1(1, 0)
@@ -184,17 +185,12 @@ def tile_finalmlptwostreamfusion_kernel(tc, x, s, w1, w2_bytes, w2_scale, r, wf,
                     out=dst[:, :, 64 * half : 64 * (half + 1), :], in_=src.rearrange("p (m t v) -> p t m v", t=4, v=2)
                 )
 
-        def group_w(key, eng):
+        def group_w(key, eng, slot=0):
             wg[key] = work.tile([P, 4 * W], BF16, name="wg", bufs=4, align_bytes=64)
-            dst = wg[key][:].rearrange("p (t m j) -> p m t j", t=4, j=4)
-            src = rows4[key][:].rearrange("p j (m t) -> p m t j", t=4)
+            dst = wg[key][:].rearrange("p (t m e j) -> p m t j e", t=4, e=2, j=4)
+            src = rows4[key][:].rearrange("p j (m e t) -> p m t j e", e=2, t=4)
             if eng == "v":
                 nc.vector.tensor_copy(out=dst, in_=src)
-            elif eng == "g":
-                for m in range(0, P, 32):
-                    nc.gpsimd.tensor_scalar(
-                        out=dst[:, m : m + 32, :, :], in0=src[:, m : m + 32, :, :], scalar1=1.0, scalar2=0.0, op0=ALU.mult, op1=ALU.add
-                    )
             else:
                 nc.scalar.copy(out=dst, in_=src)
 
@@ -241,10 +237,6 @@ def tile_finalmlptwostreamfusion_kernel(tc, x, s, w1, w2_bytes, w2_scale, r, wf,
                 part = o1[c, h][:, t, :]
                 if eng == "v":
                     nc.vector.tensor_scalar(out=part, in0=part, scalar1=a_f[:, h, t : t + 1], scalar2=None, op0=ALU.mult)
-                elif eng == "g":
-                    nc.gpsimd.tensor_scalar(
-                        out=part, in0=part, scalar1=a_f[:, h, t : t + 1], scalar2=0.0, op0=ALU.mult, op1=ALU.add
-                    )
                 else:
                     nc.scalar.activation(out=part, in_=part, func=ACT.Copy, scale=a_f[:, h, t : t + 1])
 
@@ -318,6 +310,21 @@ def tile_finalmlptwostreamfusion_kernel(tc, x, s, w1, w2_bytes, w2_scale, r, wf,
                         )
                 tr[c, h, i] = bank
 
+        def open_out(c, h):
+            for i in range(TT):
+                tr[c, h, i] = psum.tile([P, 4, P], F32, name="bank")
+                for t in range(4):
+                    nc.tensor.matmul(
+                        tr[c, h, i][:, t, :], lhsT=o1[c, h][:, t, i * P : (i + 1) * P], rhs=ident[:], start=t == 0, stop=False, is_transpose=True
+                    )
+
+        def close_out(c, h, pair):
+            for t in (2 * pair, 2 * pair + 1):
+                for i in range(TT):
+                    nc.tensor.matmul(
+                        tr[c, h, i][:, t, :], lhsT=fused[c, h][:, t, i * P : (i + 1) * P], rhs=ident[:], start=False, stop=t == 3, is_transpose=True
+                    )
+
         def store(c, h, tiles, eng="s"):
             for i in tiles:
                 rows = work.tile([P, W], F32, name="rows", bufs=6)
@@ -330,117 +337,116 @@ def tile_finalmlptwostreamfusion_kernel(tc, x, s, w1, w2_bytes, w2_scale, r, wf,
                 n0 = c * TB + i * P
                 nc.sync.dma_start(out=out[n0 : n0 + P, h * W : (h + 1) * W], in_=rows[:])
 
-        units = [(0, 0), (1, 0), (0, 1), (1, 1), (2, 0), (2, 1), (3, 0), (3, 1)]
-        gates = {-1: (1, 0), 0: (1, 1), 1: (2, 0), 3: (2, 1), 4: (3, 0), 5: (3, 1)}
+        U = [(0, 0), (1, 0), (0, 1), (1, 1), (2, 0), (2, 1), (3, 0), (3, 1)]
         A0, A1, B0, B1, F0 = ("w1", 0, 0), ("w1", 0, 1), ("w2", 0, 0), ("w2", 0, 1), ("wf", 0, 0)
         C0, C1, D0, D1, F1 = ("w1", 1, 0), ("w1", 1, 1), ("w2", 1, 0), ("w2", 1, 1), ("wf", 1, 0)
-        turn_x(0, 0)
-        turn_x(0, 1)
-        widen_w2(0, 0, "s")
-        gate_x(0, 0, 0)
-        gate_x(0, 0, 1)
-        mix_w(A0)
-        take_w(A0)
-        quant_x(0, 0, 0)
-        gate_x(0, 1, 0)
-        quant_x(0, 0, 1)
-        mix_w(A1)
-        take_w(A1)
-        gate_x(0, 1, 1)
-        quant_x(0, 1, 0)
-        turn_x(1, 0)
-        mix_w(B0)
-        widen_w2(0, 1, "s")
-        take_w(B0)
-        quant_w(A0)
-        quant_x(0, 1, 1)
-        quant_w(A1)
-        gate_x(1, 0, 0)
-        mul_z1(0, 0)
-        gate_x(1, 0, 1)
-        mix_w(B1)
-        turn_x(1, 1)
-        quant_x(1, 0, 0)
-        gain_z1(0, 0)
-        take_w(B1)
-        relu_z1(0, 0)
-        quant_x(1, 0, 1)
-        quant_w(B0)
-        quant_u(0, 0)
-        quant_w(B1)
-        last = len(units) - 1
-        both = (o1, fused)
-        for n in range(last + 2):
-            cur = units[n] if n <= last else None
-            nxt = units[n + 1] if n < last else None
-            prev = units[n - 1] if n >= 1 else None
-            old = units[n - 2] if n >= 2 else None
-            gt = gates.get(n)
-            if cur:
-                mul_z2(*cur)
-            if old:
-                turn_out(*old, both, (1,))
-                store(*old, (0,))
-            if n == 0:
-                mix_w(C0)
-                take_w(C0)
-                mix_w(C1)
-                take_w(C1)
-            if n == 1:
-                mix_w(D0)
-                take_w(D0)
-                widen_w2(1, 1, "s")
+        MIXED = (A1, B0, B1, C0, D0)
+        last = len(U) - 1
+        def terms(k):
+            return (fused,) if k in MERGED else (o1, fused)
+        def T(k, i):
+            return (turn_out, *U[k], terms(k), (i,))
+        def E(k, i, e="s"):
+            return (store, *U[k], (i,), e)
+        gates = {2: (2, 0), 3: (2, 1), 4: (3, 0), 5: (3, 1)}
+        pe = [(turn_x, 0, 0), (turn_x, 0, 1), (mix_w, A1), (turn_x, 1, 0), (turn_x, 1, 1), (mix_w, B0), (mul_z1, 0, 0), (mix_w, B1), (mul_z1, 1, 0), (mix_w, C0), (mul_z2, 0, 0), (mul_f, 0, 0), (mix_w, D0), (turn_x, 2, 0), (mul_z2, 1, 0)]
+        sc = [(group_w, A0, "s"), (widen_w2, 0, 0, "s"), (take_w, A1), (widen_w2, 0, 1, "s"), (take_w, B0), (group_w, F0, "s"), (take_w, B1), (relu_z1, 0, 0), (widen_w2, 1, 0, "s"), (take_w, C0), (widen_w2, 1, 1, "s"), (relu_z2, 0, 0), (take_w, D0), (relu_z1, 1, 0), (relu_z2, 1, 0), (group_w, F1, "s")]
+        ve = [(gate_x, 0, 0, 0), (gate_x, 0, 0, 1), (quant_x, 0, 0, 0), (gate_x, 0, 1, 0), (quant_x, 0, 0, 1), (gate_x, 0, 1, 1), (quant_x, 0, 1, 0), (quant_w, A0), (quant_x, 0, 1, 1), (gate_x, 1, 0, 0), (quant_w, A1),
+              (gate_x, 1, 1, 0), (quant_x, 1, 0, 0), (gain_z1, 0, 0), (quant_x, 1, 1, 0), (gate_x, 1, 0, 1), (quant_u, 0, 0), (quant_w, B0), (gate_x, 1, 1, 1), (quant_w, F0), (quant_x, 1, 0, 1), (quant_x, 1, 1, 1), (quant_w, B1),
+              (group_w, C1, "v"), (gain_z1, 1, 0), (quant_w, C1), (weigh_o1, 0, 0, "v"), (quant_w, C0), (quant_u, 1, 0), (group_w, D1, "v"), (fuse, 0, 0, 0), (quant_w, D1), (fuse, 0, 0, 1), (quant_w, D0), (weigh_o1, 1, 0, "v")]
+        gp = []
+        for k in range(2, last - 1):
+            gt = gates.get(k)
+            pe.append((mul_z1, *U[k]))
+            pe.append((mul_f, *U[k - 1]))
+            if k > 2:
+                sc.append((weigh_o1, *U[k - 1], "s"))
+            pe.append(T(k - 2, 0))
+            pe.append((mul_z2, *U[k]))
+            pe.append(T(k - 2, 1))
+            if gates.get(k + 1):
+                pe.append((turn_x, *gates[k + 1]))
             if gt:
-                gate_x(*gt, 0)
-            if n == 0:
-                group_w(F0, "v")
-            if n == 2:
-                group_w(F1, "v")
-            if prev:
-                fuse(*prev, 0)
+                ve.append((gate_x, *gt, 0))
+
+                ve.append((gate_x, *gt, 1))
+                ve.append((quant_x, *gt, 0))
+            ve.append((gain_z1, *U[k]))
             if gt:
-                quant_x(*gt, 0)
-            if n == 0:
-                quant_w(F0)
-            if n == 2:
-                quant_w(F1)
-            if prev:
-                fuse(*prev, 1)
-            if nxt:
-                mul_z1(*nxt)
-            if cur:
-                relu_z2(*cur)
-                mul_f(*cur)
-            if old:
-                store(*old, (1,))
-            if n == 1:
-                mix_w(D1)
-                take_w(D1)
-            if n == 0:
-                widen_w2(1, 0, "s")
-            if gt:
-                gate_x(*gt, 1)
-            if cur:
-                weigh_o1(*cur, "v" if n < 2 else "s")
-            if nxt:
-                gain_z1(*nxt)
-                relu_z1(*nxt)
-            if gt:
-                quant_x(*gt, 1)
-            if n == 0:
-                quant_w(C0)
-            if n == 1:
-                quant_w(D0)
-            if nxt:
-                quant_u(*nxt)
-            if n == 0:
-                quant_w(C1)
-            if n == 1:
-                quant_w(D1)
-            if gates.get(n + 1):
-                turn_x(*gates[n + 1])
-            if prev:
-                turn_out(*prev, both, (0,))
-        turn_out(*units[last], both, (1,))
-        store(*units[last], (0,), "v")
-        store(*units[last], (1,))
+                ve.append((quant_x, *gt, 1))
+            ve.append((fuse, *U[k - 1], 0))
+            ve.append((quant_u, *U[k]))
+            ve.append((fuse, *U[k - 1], 1))
+            if k == 2:
+                ve.append((quant_w, F1))
+            sc.append(E(k - 2, 0))
+            sc.append((relu_z1, *U[k]))
+            sc.append(E(k - 2, 1))
+            sc.append((relu_z2, *U[k]))
+        a4, a5, a6, a7 = U[4:]
+        pe += [(mul_z1, *a6), (mul_f, *a5), (mul_z1, *a7), T(4, 0), (mul_z2, *a6), (mul_f, *a6), T(4, 1), (mul_z2, *a7), T(5, 0), (mul_f, *a7), T(5, 1), T(6, 0), T(6, 1), (open_out, *a7), (close_out, *a7, 0), (close_out, *a7, 1)]
+        ve += [(gain_z1, *a6), (fuse, *a5, 0), (quant_u, *a6), (fuse, *a5, 1), (gain_z1, *a7)] + ([(merge, *a5)] if 5 in MERGED else []) + [(quant_u, *a7), (fuse, *a6, 0), (fuse, *a6, 1)] + ([(merge, *a6)] if 6 in MERGED else []) + [(fuse, *a7, 0), (fuse, *a7, 1), E(6, 1, "v"), E(7, 1, "v")]
+        sc += ([] if 5 in MERGED else [(weigh_o1, *a5, "s")]) + [(relu_z1, *a6), E(4, 0), (relu_z1, *a7), (relu_z2, *a6), E(4, 1), (relu_z2, *a7)] + ([] if 6 in MERGED else [(weigh_o1, *a6, "s")]) + [(weigh_o1, *a7, "s"), E(5, 0), E(5, 1), E(6, 0), E(7, 0)]
+
+        def needs(fn, args):
+            if fn is gate_x:
+                return [(turn_x, args[:2])]
+            if fn is quant_x:
+                return [(gate_x, args)]
+            if fn in (mix_w, group_w):
+                return [(widen_w2, args[0][1:])] if args[0][0] == "w2" else []
+            if fn is take_w:
+                return [(mix_w, args)]
+            if fn is quant_w:
+                return [(take_w, args)] if args[0] in MIXED else [(group_w, args)]
+            c, h = args[:2]
+            if fn is mul_z1:
+                return [(quant_w, (("w1", h, g),)) for g in range(PASSES)] + [(quant_x, (c, g, 0)) for g in range(PASSES)]
+            if fn is mul_z2:
+                return [(quant_w, (("w2", h, g),)) for g in range(PASSES)] + [(quant_x, (c, g, 1)) for g in range(PASSES)]
+            if fn is gain_z1:
+                return [(mul_z1, (c, h))]
+            if fn is relu_z1:
+                return [(gain_z1, (c, h))]
+            if fn is weigh_o1:
+                return [(relu_z1, (c, h))]
+            if fn is quant_u:
+                return [(gain_z1, (c, h))]
+            if fn is relu_z2:
+                return [(mul_z2, (c, h))]
+            if fn is mul_f:
+                return [(quant_u, (c, h)), (quant_w, (("wf", h, 0),))]
+            if fn is fuse:
+                return [(mul_f, (c, h)), (relu_z2, (c, h))]
+            if fn is merge:
+                return [(fuse, (c, h, 1)), (relu_z1, (c, h))]
+            if fn is turn_out:
+                return [(merge, (c, h))] if len(args[2]) == 1 else [(fuse, (c, h, 1)), (weigh_o1, (c, h))]
+            if fn is open_out:
+                return [(weigh_o1, (c, h))]
+            if fn is close_out:
+                return [(fuse, args), (open_out, (c, h))]
+            if fn is store:
+                return [(close_out, (c, h, 1))] if (c, h) == U[last] else [(turn_out, (c, h, args[2]))]
+            return []
+
+        def name_of(fn, args):
+            if fn in (widen_w2, weigh_o1):
+                return (fn, args[:2])
+            if fn is group_w:
+                return (fn, args[:1])
+            if fn is turn_out:
+                return (fn, (args[0], args[1], args[3]))
+            return (fn, args)
+
+        done = set()
+        queues = [list(pe), list(ve), list(sc), list(gp)]
+        while any(queues):
+            moved = False
+            for queue in queues:
+                while queue and all(n in done for n in needs(queue[0][0], queue[0][1:])):
+                    item = queue.pop(0)
+                    item[0](*item[1:])
+                    done.add(name_of(item[0], item[1:]))
+                    moved = True
+            assert moved

@@ -72,18 +72,18 @@ def tile_finalmlptwostreamfusion_kernel(tc, x, s, w1, w2_bytes, w2_scale, r, wf,
         nc.scalar.dma_start(out=s_bf[:], in_=s.rearrange("k (g p t) -> p (k g) t", p=P, t=4))
         load_x(0, 0)
         load_w1(0, 0)
-        load_x(0, 1)
-        load_w1(0, 1)
         nc.scalar.dma_start(out=ws[:], in_=w2_scale.rearrange("(g p t) o -> p g (t o)", p=P, t=4))
         load_w2(0)
+        load_x(0, 1)
+        load_w1(0, 1)
         load_x(1, 0)
         load_x(1, 1)
-        load_wf(0)
         load_w2(1)
+        load_w1(1, 1)
+        load_wf(0)
+        load_w1(1, 0)
         nc.sync.dma_start(out=r_bf[:], in_=r.rearrange("(h p t) -> p h t", p=P, t=4))
         nc.sync.dma_start(out=a_bf[:], in_=a.rearrange("k (h p t) -> p (k h) t", p=P, t=4))
-        load_w1(1, 0)
-        load_w1(1, 1)
         load_x(2, 0)
         load_wf(1)
         load_x(2, 1)
@@ -98,8 +98,10 @@ def tile_finalmlptwostreamfusion_kernel(tc, x, s, w1, w2_bytes, w2_scale, r, wf,
         nc.scalar.copy(out=ident_bf[:], in_=ident[:])
         r_f = keep.tile([P, HEADS, 4], F32, name="r_f")
         a_f = keep.tile([P, 2 * HEADS, 4], F32, name="a_f")
-        nc.gpsimd.tensor_copy(out=r_f[:], in_=r_bf[:])
-        nc.gpsimd.tensor_copy(out=a_f[:], in_=a_bf[:])
+
+        def widen_vectors():
+            nc.scalar.copy(out=r_f[:], in_=r_bf[:])
+            nc.scalar.copy(out=a_f[:], in_=a_bf[:])
 
         def planes(shape, name):
             codes = keep.tile([P] + shape, U32, name=name + "_c", align_bytes=64)
@@ -185,7 +187,13 @@ def tile_finalmlptwostreamfusion_kernel(tc, x, s, w1, w2_bytes, w2_scale, r, wf,
                     out=dst[:, :, 64 * half : 64 * (half + 1), :], in_=src.rearrange("p (m t v) -> p t m v", t=4, v=2)
                 )
 
-        def group_w(key, eng, slot=0):
+        def group_w(key, eng):
+            if eng == "g":
+                wg[key] = work.tile([P, 4 * W], BF16, name="wg_pool", bufs=1, align_bytes=64)
+                dst = wg[key][:].rearrange("p (t m j) -> p m t j", t=4, j=4)
+                src = rows4[key][:].rearrange("p j (m t) -> p m t j", t=4)
+                nc.gpsimd.tensor_scalar(out=dst, in0=src, scalar1=1.0, scalar2=0.0, op0=ALU.mult, op1=ALU.add)
+                return
             wg[key] = work.tile([P, 4 * W], BF16, name="wg", bufs=4, align_bytes=64)
             dst = wg[key][:].rearrange("p (t m e j) -> p m t j e", t=4, e=2, j=4)
             src = rows4[key][:].rearrange("p j (m e t) -> p m t j e", e=2, t=4)
@@ -340,7 +348,7 @@ def tile_finalmlptwostreamfusion_kernel(tc, x, s, w1, w2_bytes, w2_scale, r, wf,
         U = [(0, 0), (1, 0), (0, 1), (1, 1), (2, 0), (2, 1), (3, 0), (3, 1)]
         A0, A1, B0, B1, F0 = ("w1", 0, 0), ("w1", 0, 1), ("w2", 0, 0), ("w2", 0, 1), ("wf", 0, 0)
         C0, C1, D0, D1, F1 = ("w1", 1, 0), ("w1", 1, 1), ("w2", 1, 0), ("w2", 1, 1), ("wf", 1, 0)
-        MIXED = (A1, B0, B1, C0, D0)
+        MIXED = (A1, B0, B1, C0)
         last = len(U) - 1
         def terms(k):
             return (fused,) if k in MERGED else (o1, fused)
@@ -349,46 +357,37 @@ def tile_finalmlptwostreamfusion_kernel(tc, x, s, w1, w2_bytes, w2_scale, r, wf,
         def E(k, i, e="s"):
             return (store, *U[k], (i,), e)
         gates = {2: (2, 0), 3: (2, 1), 4: (3, 0), 5: (3, 1)}
-        pe = [(turn_x, 0, 0), (turn_x, 0, 1), (mix_w, A1), (turn_x, 1, 0), (turn_x, 1, 1), (mix_w, B0), (mul_z1, 0, 0), (mix_w, B1), (mul_z1, 1, 0), (mix_w, C0), (mul_z2, 0, 0), (mul_f, 0, 0), (mix_w, D0), (turn_x, 2, 0), (mul_z2, 1, 0)]
-        sc = [(group_w, A0, "s"), (widen_w2, 0, 0, "s"), (take_w, A1), (widen_w2, 0, 1, "s"), (take_w, B0), (group_w, F0, "s"), (take_w, B1), (relu_z1, 0, 0), (widen_w2, 1, 0, "s"), (take_w, C0), (widen_w2, 1, 1, "s"), (relu_z2, 0, 0), (take_w, D0), (relu_z1, 1, 0), (relu_z2, 1, 0), (group_w, F1, "s")]
-        ve = [(gate_x, 0, 0, 0), (gate_x, 0, 0, 1), (quant_x, 0, 0, 0), (gate_x, 0, 1, 0), (quant_x, 0, 0, 1), (gate_x, 0, 1, 1), (quant_x, 0, 1, 0), (quant_w, A0), (quant_x, 0, 1, 1), (gate_x, 1, 0, 0), (quant_w, A1),
-              (gate_x, 1, 1, 0), (quant_x, 1, 0, 0), (gain_z1, 0, 0), (quant_x, 1, 1, 0), (gate_x, 1, 0, 1), (quant_u, 0, 0), (quant_w, B0), (gate_x, 1, 1, 1), (quant_w, F0), (quant_x, 1, 0, 1), (quant_x, 1, 1, 1), (quant_w, B1),
-              (group_w, C1, "v"), (gain_z1, 1, 0), (quant_w, C1), (weigh_o1, 0, 0, "v"), (quant_w, C0), (quant_u, 1, 0), (group_w, D1, "v"), (fuse, 0, 0, 0), (quant_w, D1), (fuse, 0, 0, 1), (quant_w, D0), (weigh_o1, 1, 0, "v")]
-        gp = []
+        pe = [(turn_x, 0, 0), (turn_x, 0, 1), (mix_w, A1), (turn_x, 1, 0), (turn_x, 1, 1), (mix_w, B0), (mul_z1, 0, 0), (mix_w, B1), (mix_w, C0), (mul_z1, 1, 0), (mul_z2, 0, 0), (mul_f, 0, 0), (turn_x, 2, 0)]
+        sc = [(widen_w2, 0, 0, "s"), (widen_w2, 1, 0, "s"), (take_w, A1), (widen_w2, 0, 1, "s"), (widen_vectors,), (take_w, B0), (group_w, F0, "s"), (take_w, B1), (relu_z1, 0, 0), (take_w, C0), (widen_w2, 1, 1, "s"), (relu_z2, 0, 0), (relu_z1, 1, 0), (weigh_o1, 0, 0, "s")]
+        ve = [(gate_x, 0, 0, 0), (gate_x, 0, 0, 1), (gate_x, 0, 1, 0), (gate_x, 0, 1, 1), (quant_x, 0, 0, 0), (quant_x, 0, 1, 0), (quant_x, 0, 0, 1), (quant_x, 0, 1, 1), (gate_x, 1, 0, 0), (quant_w, A1), (quant_w, A0),
+              (gate_x, 1, 1, 0), (gate_x, 1, 0, 1), (gate_x, 1, 1, 1), (gain_z1, 0, 0),
+              (quant_x, 1, 0, 0), (quant_x, 1, 1, 0), (quant_w, B0), (quant_u, 0, 0), (quant_w, B1), (quant_w, F0), (quant_x, 1, 0, 1), (quant_x, 1, 1, 1), (gain_z1, 1, 0), (quant_w, C0), (quant_u, 1, 0), (quant_w, C1),
+              (fuse, 0, 0, 0), (fuse, 0, 0, 1)]
+        gp = [(group_w, A0, "g"), (group_w, C1, "g"), (group_w, D1, "g"), (group_w, F1, "g")]
         for k in range(2, last - 1):
-            gt = gates.get(k)
-            pe.append((mul_z1, *U[k]))
-            pe.append((mul_f, *U[k - 1]))
-            if k > 2:
-                sc.append((weigh_o1, *U[k - 1], "s"))
-            pe.append(T(k - 2, 0))
-            pe.append((mul_z2, *U[k]))
-            pe.append(T(k - 2, 1))
-            if gates.get(k + 1):
-                pe.append((turn_x, *gates[k + 1]))
-            if gt:
-                ve.append((gate_x, *gt, 0))
-
-                ve.append((gate_x, *gt, 1))
-                ve.append((quant_x, *gt, 0))
-            ve.append((gain_z1, *U[k]))
-            if gt:
-                ve.append((quant_x, *gt, 1))
-            ve.append((fuse, *U[k - 1], 0))
-            ve.append((quant_u, *U[k]))
-            ve.append((fuse, *U[k - 1], 1))
+            gt = gates[k]
             if k == 2:
-                ve.append((quant_w, F1))
-            sc.append(E(k - 2, 0))
-            sc.append((relu_z1, *U[k]))
-            sc.append(E(k - 2, 1))
-            sc.append((relu_z2, *U[k]))
+                pe += [(mul_z2, *U[k - 1]), (mul_z1, *U[k]), (mul_f, *U[k - 1]), T(k - 2, 0), T(k - 2, 1)]
+            else:
+                pe += [(mul_z2, *U[k - 1]), T(k - 2, 0), (mul_z1, *U[k]), (mul_f, *U[k - 1]), T(k - 2, 1)]
+            if k + 1 in gates:
+                pe.append((turn_x, *gates[k + 1]))
+            if k == 2:
+                ve += [(gate_x, *gt, 0), (gate_x, *gt, 1), (gain_z1, *U[k]), (quant_x, *gt, 0), (quant_x, *gt, 1), (quant_w, D0), (quant_u, *U[k]), (quant_w, D1), (fuse, *U[k - 1], 0), (fuse, *U[k - 1], 1)]
+                sc += [(group_w, D0, "s")]
+            elif k == 3:
+                ve += [(gate_x, *gt, 0), (gate_x, *gt, 1), (gain_z1, *U[k]), (quant_w, F1), (quant_x, *gt, 0), (quant_x, *gt, 1), (quant_u, *U[k]), (fuse, *U[k - 1], 0), (fuse, *U[k - 1], 1)]
+            else:
+                ve += [(gate_x, *gt, 0), (gate_x, *gt, 1), (quant_x, *gt, 0), (quant_x, *gt, 1), (gain_z1, *U[k]), (fuse, *U[k - 1], 0), (quant_u, *U[k]), (fuse, *U[k - 1], 1)]
+            sc += [(relu_z2, *U[k - 1]), E(k - 2, 0), (weigh_o1, *U[k - 1], "s"), (relu_z1, *U[k]), E(k - 2, 1)]
         a4, a5, a6, a7 = U[4:]
-        pe += [(mul_z1, *a6), (mul_f, *a5), (mul_z1, *a7), T(4, 0), (mul_z2, *a6), (mul_f, *a6), T(4, 1), (mul_z2, *a7), T(5, 0), (mul_f, *a7), T(5, 1), T(6, 0), T(6, 1), (open_out, *a7), (close_out, *a7, 0), (close_out, *a7, 1)]
+        pe += [(mul_z2, *a5), (mul_z1, *a6), (mul_f, *a5), T(4, 0), (mul_z1, *a7), (mul_z2, *a6), T(4, 1), (mul_f, *a6), (mul_z2, *a7), T(5, 0), (mul_f, *a7), T(5, 1), T(6, 0), T(6, 1), (open_out, *a7), (close_out, *a7, 0), (close_out, *a7, 1)]
         ve += [(gain_z1, *a6), (fuse, *a5, 0), (quant_u, *a6), (fuse, *a5, 1), (gain_z1, *a7)] + ([(merge, *a5)] if 5 in MERGED else []) + [(quant_u, *a7), (fuse, *a6, 0), (fuse, *a6, 1)] + ([(merge, *a6)] if 6 in MERGED else []) + [(fuse, *a7, 0), (fuse, *a7, 1), E(6, 1, "v"), E(7, 1, "v")]
-        sc += ([] if 5 in MERGED else [(weigh_o1, *a5, "s")]) + [(relu_z1, *a6), E(4, 0), (relu_z1, *a7), (relu_z2, *a6), E(4, 1), (relu_z2, *a7)] + ([] if 6 in MERGED else [(weigh_o1, *a6, "s")]) + [(weigh_o1, *a7, "s"), E(5, 0), E(5, 1), E(6, 0), E(7, 0)]
+        sc += [(relu_z2, *a5)] + ([] if 5 in MERGED else [(weigh_o1, *a5, "s")]) + [(relu_z1, *a6), E(4, 0), (relu_z1, *a7), (relu_z2, *a6), E(4, 1), (relu_z2, *a7)] + ([] if 6 in MERGED else [(weigh_o1, *a6, "s")]) + [(weigh_o1, *a7, "s"), E(5, 0), E(5, 1), E(6, 0), E(7, 0)]
 
         def needs(fn, args):
+            if fn is widen_vectors:
+                return []
             if fn is gate_x:
                 return [(turn_x, args[:2])]
             if fn is quant_x:
@@ -405,7 +404,7 @@ def tile_finalmlptwostreamfusion_kernel(tc, x, s, w1, w2_bytes, w2_scale, r, wf,
             if fn is mul_z2:
                 return [(quant_w, (("w2", h, g),)) for g in range(PASSES)] + [(quant_x, (c, g, 1)) for g in range(PASSES)]
             if fn is gain_z1:
-                return [(mul_z1, (c, h))]
+                return [(mul_z1, (c, h)), (widen_vectors, ())]
             if fn is relu_z1:
                 return [(gain_z1, (c, h))]
             if fn is weigh_o1:

@@ -38,8 +38,8 @@ def tile_finalmlptwostreamfusion_kernel(tc, x, s, w1, w2_bytes, w2_scale, r, wf,
 
         s_bf = keep.tile([P, 2 * PASSES, 4], BF16, name="s_bf")
         ws = keep.tile([P, PASSES, 4], F32, name="ws")
-        r_bf = keep.tile([P, HEADS, 4], BF16, name="r_bf")
-        a_bf = keep.tile([P, 2 * HEADS, 4], BF16, name="a_bf")
+        r_bf = keep.tile([P, HEADS, 8], BF16, name="r_bf")
+        a_bf = keep.tile([P, 2 * HEADS, 8], BF16, name="a_bf")
         x_raw = {}
         w1_raw = {}
         w2_raw = {}
@@ -67,23 +67,28 @@ def tile_finalmlptwostreamfusion_kernel(tc, x, s, w1, w2_bytes, w2_scale, r, wf,
 
         def load_wf(h):
             wf_raw[h] = keep.tile([P, 4, W], BF16, name="wf_raw%d" % h)
-            nc.sync.dma_start(out=wf_raw[h][:], in_=wf[h].rearrange("(p j) n -> p j n", j=4))
+            rows = wf[h].rearrange("(m t e) n -> e m t n", t=4, e=2)
+            for e in range(2):
+                nc.sync.dma_start(out=wf_raw[h][e::2, :, :], in_=rows[e])
 
         nc.scalar.dma_start(out=s_bf[:], in_=s.rearrange("k (g p t) -> p (k g) t", p=P, t=4))
         load_x(0, 0)
         load_w1(0, 0)
         nc.scalar.dma_start(out=ws[:], in_=w2_scale.rearrange("(g p t) o -> p g (t o)", p=P, t=4))
-        load_w2(0)
         load_x(0, 1)
-        load_w1(0, 1)
+        load_w2(0)
         load_x(1, 0)
-        load_x(1, 1)
+        load_w1(0, 1)
         load_w2(1)
+        load_x(1, 1)
         load_w1(1, 1)
+        for e in range(2):
+            nc.sync.dma_start(out=r_bf[e::2, :, 0:7], in_=r.rearrange("(h m c) -> m h c", h=HEADS, c=8)[:, :, e : e + 7])
+            nc.sync.dma_start(
+                out=a_bf[e::2, :, 0:7], in_=a.rearrange("k (h m c) -> m (k h) c", h=HEADS, c=8)[:, :, e : e + 7]
+            )
         load_wf(0)
         load_w1(1, 0)
-        nc.sync.dma_start(out=r_bf[:], in_=r.rearrange("(h p t) -> p h t", p=P, t=4))
-        nc.sync.dma_start(out=a_bf[:], in_=a.rearrange("k (h p t) -> p (k h) t", p=P, t=4))
         load_x(2, 0)
         load_wf(1)
         load_x(2, 1)
@@ -100,8 +105,8 @@ def tile_finalmlptwostreamfusion_kernel(tc, x, s, w1, w2_bytes, w2_scale, r, wf,
         a_f = keep.tile([P, 2 * HEADS, 4], F32, name="a_f")
 
         def widen_vectors():
-            nc.scalar.copy(out=r_f[:], in_=r_bf[:])
-            nc.scalar.copy(out=a_f[:], in_=a_bf[:])
+            nc.scalar.copy(out=r_f[:], in_=r_bf[:, :, 0:7:2])
+            nc.scalar.copy(out=a_f[:], in_=a_bf[:, :, 0:7:2])
 
         def planes(shape, name):
             codes = keep.tile([P] + shape, U32, name=name + "_c", align_bytes=64)
@@ -137,7 +142,7 @@ def tile_finalmlptwostreamfusion_kernel(tc, x, s, w1, w2_bytes, w2_scale, r, wf,
                     nc.tensor.transpose(xt[c, g][:, u, i * P : (i + 1) * P], words[:, u::2], ident[:])
 
         def gate_x(c, g, k):
-            xg[c, g, k] = work.tile([P, TB, 4], BF16, name="xg", bufs=4, align_bytes=64)
+            xg[c, g, k] = work.tile([P, TB, 4], BF16, name="xg", bufs=8, align_bytes=64)
             src = xt[c, g][:].bitcast(BF16).rearrange("p u (n e) -> p n u e", e=2)
             factor = gate[:, PASSES * k + g, :].rearrange("p (u e) -> p u e", e=2).unsqueeze(1)
             nc.vector.tensor_tensor(
@@ -180,23 +185,23 @@ def tile_finalmlptwostreamfusion_kernel(tc, x, s, w1, w2_bytes, w2_scale, r, wf,
 
         def take_w(key):
             wg[key] = work.tile([P, 4 * W], BF16, name="wg", bufs=4, align_bytes=64)
-            dst = wg[key][:].bitcast(F32).rearrange("p (t m v) -> p t m v", t=4, v=2)
+            dst = wg[key][:].bitcast(F32).rearrange("p (t m v) -> p t m v", t=4, v=4)
             for half in range(2):
                 src = mixed[key, half][:].rearrange("p a n j -> p (a n j)").bitcast(F32)
                 nc.scalar.copy(
-                    out=dst[:, :, 64 * half : 64 * (half + 1), :], in_=src.rearrange("p (m t v) -> p t m v", t=4, v=2)
+                    out=dst[:, :, 32 * half : 32 * (half + 1), :], in_=src.rearrange("p (m t v) -> p t m v", t=4, v=4)
                 )
 
-        def group_w(key, eng):
+        def group_w(key, eng, slot=0):
             if eng == "g":
-                wg[key] = work.tile([P, 4 * W], BF16, name="wg_pool", bufs=1, align_bytes=64)
-                dst = wg[key][:].rearrange("p (t m j) -> p m t j", t=4, j=4)
-                src = rows4[key][:].rearrange("p j (m t) -> p m t j", t=4)
+                wg[key] = work.tile([P, 4 * W], BF16, name="wg_pool%d" % slot, bufs=1, align_bytes=64)
+                dst = wg[key][:].rearrange("p (t m e j) -> p m t e j", t=4, e=2, j=4)
+                src = rows4[key][:].rearrange("p j (m t e) -> p m t e j", t=4, e=2)
                 nc.gpsimd.tensor_scalar(out=dst, in0=src, scalar1=1.0, scalar2=0.0, op0=ALU.mult, op1=ALU.add)
                 return
             wg[key] = work.tile([P, 4 * W], BF16, name="wg", bufs=4, align_bytes=64)
             dst = wg[key][:].rearrange("p (t m e j) -> p m t j e", t=4, e=2, j=4)
-            src = rows4[key][:].rearrange("p j (m e t) -> p m t j e", e=2, t=4)
+            src = rows4[key][:].rearrange("p j (m t e) -> p m t j e", e=2, t=4)
             if eng == "v":
                 nc.vector.tensor_copy(out=dst, in_=src)
             else:
@@ -336,8 +341,8 @@ def tile_finalmlptwostreamfusion_kernel(tc, x, s, w1, w2_bytes, w2_scale, r, wf,
         def store(c, h, tiles, eng="s"):
             for i in tiles:
                 rows = work.tile([P, W], F32, name="rows", bufs=6)
-                dst = rows[:].rearrange("n (m t) -> n m t", t=4)
-                src = tr[c, h, i][:].rearrange("n t m -> n m t")
+                dst = rows[:].rearrange("n (m t e) -> n m t e", t=4, e=2)
+                src = tr[c, h, i][:].rearrange("n t (m e) -> n m t e", e=2)
                 if eng == "v":
                     nc.vector.tensor_copy(out=dst, in_=src)
                 else:
@@ -348,7 +353,7 @@ def tile_finalmlptwostreamfusion_kernel(tc, x, s, w1, w2_bytes, w2_scale, r, wf,
         U = [(0, 0), (1, 0), (0, 1), (1, 1), (2, 0), (2, 1), (3, 0), (3, 1)]
         A0, A1, B0, B1, F0 = ("w1", 0, 0), ("w1", 0, 1), ("w2", 0, 0), ("w2", 0, 1), ("wf", 0, 0)
         C0, C1, D0, D1, F1 = ("w1", 1, 0), ("w1", 1, 1), ("w2", 1, 0), ("w2", 1, 1), ("wf", 1, 0)
-        MIXED = (A1, B0, B1, C0)
+        MIXED = (B0, B1, C0)
         last = len(U) - 1
         def terms(k):
             return (fused,) if k in MERGED else (o1, fused)
@@ -357,13 +362,14 @@ def tile_finalmlptwostreamfusion_kernel(tc, x, s, w1, w2_bytes, w2_scale, r, wf,
         def E(k, i, e="s"):
             return (store, *U[k], (i,), e)
         gates = {2: (2, 0), 3: (2, 1), 4: (3, 0), 5: (3, 1)}
-        pe = [(turn_x, 0, 0), (turn_x, 0, 1), (mix_w, A1), (turn_x, 1, 0), (turn_x, 1, 1), (mix_w, B0), (mul_z1, 0, 0), (mix_w, B1), (mix_w, C0), (mul_z1, 1, 0), (mul_z2, 0, 0), (mul_f, 0, 0), (turn_x, 2, 0)]
-        sc = [(widen_w2, 0, 0, "s"), (widen_w2, 1, 0, "s"), (take_w, A1), (widen_w2, 0, 1, "s"), (widen_vectors,), (take_w, B0), (group_w, F0, "s"), (take_w, B1), (relu_z1, 0, 0), (take_w, C0), (widen_w2, 1, 1, "s"), (relu_z2, 0, 0), (relu_z1, 1, 0), (weigh_o1, 0, 0, "s")]
-        ve = [(gate_x, 0, 0, 0), (gate_x, 0, 0, 1), (gate_x, 0, 1, 0), (gate_x, 0, 1, 1), (quant_x, 0, 0, 0), (quant_x, 0, 1, 0), (quant_x, 0, 0, 1), (quant_x, 0, 1, 1), (gate_x, 1, 0, 0), (quant_w, A1), (quant_w, A0),
-              (gate_x, 1, 1, 0), (gate_x, 1, 0, 1), (gate_x, 1, 1, 1), (gain_z1, 0, 0),
-              (quant_x, 1, 0, 0), (quant_x, 1, 1, 0), (quant_w, B0), (quant_u, 0, 0), (quant_w, B1), (quant_w, F0), (quant_x, 1, 0, 1), (quant_x, 1, 1, 1), (gain_z1, 1, 0), (quant_w, C0), (quant_u, 1, 0), (quant_w, C1),
+        pe = [(turn_x, 0, 0), (turn_x, 0, 1), (turn_x, 1, 0), (mix_w, B0), (turn_x, 1, 1), (mul_z1, 0, 0), (mix_w, B1), (mix_w, C0), (mul_z1, 1, 0), (mul_z2, 0, 0), (mul_f, 0, 0), (turn_x, 2, 0)]
+        sc = [(widen_w2, 0, 0, "s"), (widen_w2, 1, 0, "s"), (widen_w2, 0, 1, "s"), (take_w, B0), (widen_vectors,), (group_w, F0, "s"), (take_w, B1), (relu_z1, 0, 0), (take_w, C0), (widen_w2, 1, 1, "s"), (relu_z2, 0, 0), (relu_z1, 1, 0), (weigh_o1, 0, 0, "s")]
+        ve = [(gate_x, 0, 0, 0), (gate_x, 0, 0, 1), (gate_x, 0, 1, 0), (gate_x, 0, 1, 1), (gate_x, 1, 0, 0), (gate_x, 1, 0, 1),
+              (quant_x, 0, 0, 0), (quant_x, 0, 1, 0), (quant_w, A1), (quant_w, A0),
+              (gate_x, 1, 1, 0), (gate_x, 1, 1, 1), (gain_z1, 0, 0),
+              (quant_x, 1, 0, 0), (quant_x, 1, 1, 0), (quant_u, 0, 0), (quant_w, B0), (quant_x, 0, 0, 1), (quant_x, 0, 1, 1), (quant_w, B1), (quant_w, F0), (quant_x, 1, 0, 1), (quant_x, 1, 1, 1), (gain_z1, 1, 0), (quant_w, C0), (quant_u, 1, 0), (quant_w, C1),
               (fuse, 0, 0, 0), (fuse, 0, 0, 1)]
-        gp = [(group_w, A0, "g"), (group_w, C1, "g"), (group_w, D1, "g"), (group_w, F1, "g")]
+        gp = [(group_w, A0, "g"), (group_w, A1, "g", 1), (group_w, C1, "g"), (group_w, D1, "g"), (group_w, F1, "g")]
         for k in range(2, last - 1):
             gt = gates[k]
             if k == 2:
@@ -376,7 +382,7 @@ def tile_finalmlptwostreamfusion_kernel(tc, x, s, w1, w2_bytes, w2_scale, r, wf,
                 ve += [(gate_x, *gt, 0), (gate_x, *gt, 1), (gain_z1, *U[k]), (quant_x, *gt, 0), (quant_x, *gt, 1), (quant_w, D0), (quant_u, *U[k]), (quant_w, D1), (fuse, *U[k - 1], 0), (fuse, *U[k - 1], 1)]
                 sc += [(group_w, D0, "s")]
             elif k == 3:
-                ve += [(gate_x, *gt, 0), (gate_x, *gt, 1), (gain_z1, *U[k]), (quant_w, F1), (quant_x, *gt, 0), (quant_x, *gt, 1), (quant_u, *U[k]), (fuse, *U[k - 1], 0), (fuse, *U[k - 1], 1)]
+                ve += [(gate_x, *gt, 0), (gate_x, *gt, 1), (quant_w, F1), (quant_x, *gt, 0), (gain_z1, *U[k]), (quant_x, *gt, 1), (fuse, *U[k - 1], 0), (quant_u, *U[k]), (fuse, *U[k - 1], 1)]
             else:
                 ve += [(gate_x, *gt, 0), (gate_x, *gt, 1), (quant_x, *gt, 0), (quant_x, *gt, 1), (gain_z1, *U[k]), (fuse, *U[k - 1], 0), (quant_u, *U[k]), (fuse, *U[k - 1], 1)]
             sc += [(relu_z2, *U[k - 1]), E(k - 2, 0), (weigh_o1, *U[k - 1], "s"), (relu_z1, *U[k]), E(k - 2, 1)]

@@ -59,10 +59,11 @@ def tile_finalmlptwostreamfusion_kernel(tc, x, s, w1, w2_bytes, w2_scale, r, wf,
                 in_=w1[g * 512 : (g + 1) * 512, h * W : (h + 1) * W].rearrange("(p j) n -> p j n", j=4),
             )
 
-        def load_w2(g):
-            w2_raw[g] = keep.tile([P, 4, H], U8, name="w2_raw%d" % g)
+        def load_w2(h, g):
+            w2_raw[h, g] = keep.tile([P, 4, W], U8, name="w2_raw%d_%d" % (h, g))
             nc.sync.dma_start(
-                out=w2_raw[g][:], in_=w2_bytes[g * 512 : (g + 1) * 512, :].rearrange("(p j) n -> p j n", j=4)
+                out=w2_raw[h, g][:],
+                in_=w2_bytes[g * 512 : (g + 1) * 512, h * W : (h + 1) * W].rearrange("(p j) n -> p j n", j=4),
             )
 
         def load_wf(h):
@@ -73,25 +74,28 @@ def tile_finalmlptwostreamfusion_kernel(tc, x, s, w1, w2_bytes, w2_scale, r, wf,
 
         nc.scalar.dma_start(out=s_bf[:], in_=s.rearrange("k (g p t) -> p (k g) t", p=P, t=4))
         load_x(0, 0)
-        load_w1(0, 0)
         nc.scalar.dma_start(out=ws[:], in_=w2_scale.rearrange("(g p t) o -> p g (t o)", p=P, t=4))
+        load_w2(0, 0)
         load_x(0, 1)
-        load_w2(0)
+        load_w1(0, 0)
         load_x(1, 0)
+        load_w2(0, 1)
         load_w1(0, 1)
-        load_w2(1)
         load_x(1, 1)
+        load_w2(1, 0)
         load_w1(1, 1)
         for e in range(2):
             nc.sync.dma_start(out=r_bf[e::2, :, 0:7], in_=r.rearrange("(h m c) -> m h c", h=HEADS, c=8)[:, :, e : e + 7])
+        load_x(2, 0)
+        load_w2(1, 1)
+        load_w1(1, 0)
+        load_wf(0)
+        for e in range(2):
             nc.sync.dma_start(
                 out=a_bf[e::2, :, 0:7], in_=a.rearrange("k (h m c) -> m (k h) c", h=HEADS, c=8)[:, :, e : e + 7]
             )
-        load_wf(0)
-        load_w1(1, 0)
-        load_x(2, 0)
-        load_wf(1)
         load_x(2, 1)
+        load_wf(1)
         load_x(3, 0)
         load_x(3, 1)
 
@@ -104,8 +108,10 @@ def tile_finalmlptwostreamfusion_kernel(tc, x, s, w1, w2_bytes, w2_scale, r, wf,
         r_f = keep.tile([P, HEADS, 4], F32, name="r_f")
         a_f = keep.tile([P, 2 * HEADS, 4], F32, name="a_f")
 
-        def widen_vectors():
+        def widen_r():
             nc.scalar.copy(out=r_f[:], in_=r_bf[:, :, 0:7:2])
+
+        def widen_a():
             nc.scalar.copy(out=a_f[:], in_=a_bf[:, :, 0:7:2])
 
         def planes(shape, name):
@@ -142,7 +148,7 @@ def tile_finalmlptwostreamfusion_kernel(tc, x, s, w1, w2_bytes, w2_scale, r, wf,
                     nc.tensor.transpose(xt[c, g][:, u, i * P : (i + 1) * P], words[:, u::2], ident[:])
 
         def gate_x(c, g, k):
-            xg[c, g, k] = work.tile([P, TB, 4], BF16, name="xg", bufs=8, align_bytes=64)
+            xg[c, g, k] = work.tile([P, TB, 4], BF16, name="xg", bufs=10, align_bytes=64)
             src = xt[c, g][:].bitcast(BF16).rearrange("p u (n e) -> p n u e", e=2)
             factor = gate[:, PASSES * k + g, :].rearrange("p (u e) -> p u e", e=2).unsqueeze(1)
             nc.vector.tensor_tensor(
@@ -165,7 +171,7 @@ def tile_finalmlptwostreamfusion_kernel(tc, x, s, w1, w2_bytes, w2_scale, r, wf,
             wide = work.tile([P, 4, W], BF16, name="wide", bufs=3)
             rows4["w2", h, g] = wide
             for j in range(4):
-                src = w2_raw[g][:, j, h * W : (h + 1) * W].bitcast(FP8)
+                src = w2_raw[h, g][:, j, :].bitcast(FP8)
                 if eng == "v":
                     nc.vector.tensor_scalar(
                         out=wide[:, j, :], in0=src, scalar1=ws[:, g, j : j + 1], scalar2=None, op0=ALU.mult
@@ -353,7 +359,7 @@ def tile_finalmlptwostreamfusion_kernel(tc, x, s, w1, w2_bytes, w2_scale, r, wf,
         U = [(0, 0), (1, 0), (0, 1), (1, 1), (2, 0), (2, 1), (3, 0), (3, 1)]
         A0, A1, B0, B1, F0 = ("w1", 0, 0), ("w1", 0, 1), ("w2", 0, 0), ("w2", 0, 1), ("wf", 0, 0)
         C0, C1, D0, D1, F1 = ("w1", 1, 0), ("w1", 1, 1), ("w2", 1, 0), ("w2", 1, 1), ("wf", 1, 0)
-        MIXED = (B0, B1, C0)
+        MIXED = (B1, C0, D0)
         last = len(U) - 1
         def terms(k):
             return (fused,) if k in MERGED else (o1, fused)
@@ -362,25 +368,29 @@ def tile_finalmlptwostreamfusion_kernel(tc, x, s, w1, w2_bytes, w2_scale, r, wf,
         def E(k, i, e="s"):
             return (store, *U[k], (i,), e)
         gates = {2: (2, 0), 3: (2, 1), 4: (3, 0), 5: (3, 1)}
-        pe = [(turn_x, 0, 0), (turn_x, 0, 1), (turn_x, 1, 0), (mix_w, B0), (turn_x, 1, 1), (mul_z1, 0, 0), (mix_w, B1), (mix_w, C0), (mul_z1, 1, 0), (mul_z2, 0, 0), (mul_f, 0, 0), (turn_x, 2, 0)]
-        sc = [(widen_w2, 0, 0, "s"), (widen_w2, 1, 0, "s"), (widen_w2, 0, 1, "s"), (take_w, B0), (widen_vectors,), (group_w, F0, "s"), (take_w, B1), (relu_z1, 0, 0), (take_w, C0), (widen_w2, 1, 1, "s"), (relu_z2, 0, 0), (relu_z1, 1, 0), (weigh_o1, 0, 0, "s")]
-        ve = [(gate_x, 0, 0, 0), (gate_x, 0, 0, 1), (gate_x, 0, 1, 0), (gate_x, 0, 1, 1), (gate_x, 1, 0, 0), (gate_x, 1, 0, 1),
-              (quant_x, 0, 0, 0), (quant_x, 0, 1, 0), (quant_w, A1), (quant_w, A0),
-              (gate_x, 1, 1, 0), (gate_x, 1, 1, 1), (gain_z1, 0, 0),
-              (quant_x, 1, 0, 0), (quant_x, 1, 1, 0), (quant_u, 0, 0), (quant_w, B0), (quant_x, 0, 0, 1), (quant_x, 0, 1, 1), (quant_w, B1), (quant_w, F0), (quant_x, 1, 0, 1), (quant_x, 1, 1, 1), (gain_z1, 1, 0), (quant_w, C0), (quant_u, 1, 0), (quant_w, C1),
-              (fuse, 0, 0, 0), (fuse, 0, 0, 1)]
-        gp = [(group_w, A0, "g"), (group_w, A1, "g", 1), (group_w, C1, "g"), (group_w, D1, "g"), (group_w, F1, "g")]
+        pe = [(turn_x, 0, 0), (turn_x, 0, 1), (turn_x, 1, 0), (turn_x, 1, 1), (mix_w, B1), (turn_x, 2, 0), (mul_z1, 0, 0), (mix_w, C0), (mul_z1, 1, 0), (mul_z2, 0, 0), (mix_w, D0), (mul_f, 0, 0)]
+        sc = [(widen_w2, 0, 0, "s"), (widen_w2, 0, 1, "s"), (group_w, B0, "s"), (widen_w2, 1, 0, "s"), (take_w, B1), (widen_r,), (widen_w2, 1, 1, "s"), (group_w, F0, "s"), (take_w, C0), (relu_z1, 0, 0), (widen_a,), (relu_z2, 0, 0), (relu_z1, 1, 0), (weigh_o1, 0, 0, "s")]
+        ve = [(gate_x, 0, 0, 0), (gate_x, 0, 0, 1), (gate_x, 0, 1, 0), (gate_x, 0, 1, 1), (gate_x, 1, 0, 0), (gate_x, 1, 0, 1), (gate_x, 1, 1, 0),
+              (quant_x, 0, 0, 0), (quant_x, 0, 1, 0), (quant_w, A0), (quant_w, A1),
+              (gate_x, 1, 1, 1), (gate_x, 2, 0, 0), (gain_z1, 0, 0),
+              (quant_x, 1, 0, 0), (quant_x, 1, 1, 0), (quant_w, B0), (quant_u, 0, 0), (quant_x, 0, 0, 1), (quant_x, 0, 1, 1), (quant_w, B1), (quant_x, 1, 0, 1), (quant_x, 1, 1, 1), (gain_z1, 1, 0), (quant_w, F0), (quant_w, C0), (quant_u, 1, 0), (quant_x, 2, 0, 0), (quant_w, C1),
+              (gate_x, 2, 0, 1), (fuse, 0, 0, 0), (fuse, 0, 0, 1)]
+        gp = [(group_w, A0, "g", 1), (group_w, A1, "g"), (group_w, C1, "g"), (group_w, D1, "g"), (group_w, F1, "g")]
         for k in range(2, last - 1):
             gt = gates[k]
             if k == 2:
                 pe += [(mul_z2, *U[k - 1]), (mul_z1, *U[k]), (mul_f, *U[k - 1]), T(k - 2, 0), T(k - 2, 1)]
+            elif k == 3:
+                pe += [(mul_z2, *U[k - 1]), T(k - 2, 0), (mul_z1, *U[k]), T(k - 2, 1)]
             else:
                 pe += [(mul_z2, *U[k - 1]), T(k - 2, 0), (mul_z1, *U[k]), (mul_f, *U[k - 1]), T(k - 2, 1)]
             if k + 1 in gates:
                 pe.append((turn_x, *gates[k + 1]))
+            if k == 3:
+                pe.append((mul_f, *U[k - 1]))
             if k == 2:
-                ve += [(gate_x, *gt, 0), (gate_x, *gt, 1), (gain_z1, *U[k]), (quant_x, *gt, 0), (quant_x, *gt, 1), (quant_w, D0), (quant_u, *U[k]), (quant_w, D1), (fuse, *U[k - 1], 0), (fuse, *U[k - 1], 1)]
-                sc += [(group_w, D0, "s")]
+                ve += [(gain_z1, *U[k]), (quant_x, *gt, 1), (quant_w, D0), (quant_u, *U[k]), (quant_w, D1), (fuse, *U[k - 1], 0), (fuse, *U[k - 1], 1)]
+                sc += [(take_w, D0)]
             elif k == 3:
                 ve += [(gate_x, *gt, 0), (gate_x, *gt, 1), (quant_w, F1), (quant_x, *gt, 0), (gain_z1, *U[k]), (quant_x, *gt, 1), (fuse, *U[k - 1], 0), (quant_u, *U[k]), (fuse, *U[k - 1], 1)]
             else:
@@ -392,7 +402,7 @@ def tile_finalmlptwostreamfusion_kernel(tc, x, s, w1, w2_bytes, w2_scale, r, wf,
         sc += [(relu_z2, *a5)] + ([] if 5 in MERGED else [(weigh_o1, *a5, "s")]) + [(relu_z1, *a6), E(4, 0), (relu_z1, *a7), (relu_z2, *a6), E(4, 1), (relu_z2, *a7)] + ([] if 6 in MERGED else [(weigh_o1, *a6, "s")]) + [(weigh_o1, *a7, "s"), E(5, 0), E(5, 1), E(6, 0), E(7, 0)]
 
         def needs(fn, args):
-            if fn is widen_vectors:
+            if fn in (widen_r, widen_a):
                 return []
             if fn is gate_x:
                 return [(turn_x, args[:2])]
@@ -410,11 +420,11 @@ def tile_finalmlptwostreamfusion_kernel(tc, x, s, w1, w2_bytes, w2_scale, r, wf,
             if fn is mul_z2:
                 return [(quant_w, (("w2", h, g),)) for g in range(PASSES)] + [(quant_x, (c, g, 1)) for g in range(PASSES)]
             if fn is gain_z1:
-                return [(mul_z1, (c, h)), (widen_vectors, ())]
+                return [(mul_z1, (c, h)), (widen_r, ())]
             if fn is relu_z1:
                 return [(gain_z1, (c, h))]
             if fn is weigh_o1:
-                return [(relu_z1, (c, h))]
+                return [(relu_z1, (c, h)), (widen_a, ())]
             if fn is quant_u:
                 return [(gain_z1, (c, h))]
             if fn is relu_z2:
@@ -422,7 +432,7 @@ def tile_finalmlptwostreamfusion_kernel(tc, x, s, w1, w2_bytes, w2_scale, r, wf,
             if fn is mul_f:
                 return [(quant_u, (c, h)), (quant_w, (("wf", h, 0),))]
             if fn is fuse:
-                return [(mul_f, (c, h)), (relu_z2, (c, h))]
+                return [(mul_f, (c, h)), (relu_z2, (c, h)), (widen_a, ())]
             if fn is merge:
                 return [(fuse, (c, h, 1)), (relu_z1, (c, h))]
             if fn is turn_out:

@@ -316,11 +316,11 @@ def tile_finalmlptwostreamfusion_kernel(tc, x, s, w1, w2_bytes, w2_scale, r, wf,
 
         def turn_out(c, h, terms, tiles):
             for i in tiles:
-                bank = psum.tile([P, 4, P], F32, name="bank")
+                bank = psum.tile([P, 64, 4, 2], F32, name="bank")
                 for t in range(4):
                     for j, term in enumerate(terms):
                         nc.tensor.matmul(
-                            bank[:, t, :],
+                            bank[:, :, t, :],
                             lhsT=term[c, h][:, t, i * P : (i + 1) * P],
                             rhs=ident[:],
                             start=j == 0,
@@ -331,24 +331,24 @@ def tile_finalmlptwostreamfusion_kernel(tc, x, s, w1, w2_bytes, w2_scale, r, wf,
 
         def open_out(c, h):
             for i in range(TT):
-                tr[c, h, i] = psum.tile([P, 4, P], F32, name="bank")
+                tr[c, h, i] = psum.tile([P, 64, 4, 2], F32, name="bank")
                 for t in range(4):
                     nc.tensor.matmul(
-                        tr[c, h, i][:, t, :], lhsT=o1[c, h][:, t, i * P : (i + 1) * P], rhs=ident[:], start=t == 0, stop=False, is_transpose=True
+                        tr[c, h, i][:, :, t, :], lhsT=o1[c, h][:, t, i * P : (i + 1) * P], rhs=ident[:], start=t == 0, stop=False, is_transpose=True
                     )
 
         def close_out(c, h, pair):
             for t in (2 * pair, 2 * pair + 1):
                 for i in range(TT):
                     nc.tensor.matmul(
-                        tr[c, h, i][:, t, :], lhsT=fused[c, h][:, t, i * P : (i + 1) * P], rhs=ident[:], start=False, stop=t == 3, is_transpose=True
+                        tr[c, h, i][:, :, t, :], lhsT=fused[c, h][:, t, i * P : (i + 1) * P], rhs=ident[:], start=False, stop=t == 3, is_transpose=True
                     )
 
         def store(c, h, tiles, eng="s"):
             for i in tiles:
                 rows = work.tile([P, W], F32, name="rows", bufs=6)
-                dst = rows[:].rearrange("n (m t e) -> n m t e", t=4, e=2)
-                src = tr[c, h, i][:].rearrange("n t (m e) -> n m t e", e=2)
+                dst = rows[:]
+                src = tr[c, h, i][:].rearrange("n m t e -> n (m t e)")
                 if eng == "v":
                     nc.vector.tensor_copy(out=dst, in_=src)
                 else:

@@ -17,11 +17,17 @@ H = HEADS * W
 FLOPS = 2 * (2 * B * D * H + HEADS * B * W * W)
 
 P = 128
-PASSES = D // 512
+KP = 4 * P
+PASSES = D // KP
 TB = 256
-NB = B // TB
 TT = TB // P
-MERGED = (5, 6)
+M = P // 2
+
+UNITS = [(0, 0), (1, 0), (0, 1), (1, 1), (2, 0), (2, 1), (3, 0), (3, 1)]
+LAST = len(UNITS) - 1
+MERGED = (LAST - 2, LAST - 1)
+
+XG_BUFS, WIDE_BUFS, WG_BUFS, UG_BUFS, O_BUFS, FUSED_BUFS, ROW_BUFS = 10, 3, 4, 3, 4, 3, 6
 
 
 def tile_finalmlptwostreamfusion_kernel(tc, x, s, w1, w2_bytes, w2_scale, r, wf, a, out):
@@ -40,40 +46,49 @@ def tile_finalmlptwostreamfusion_kernel(tc, x, s, w1, w2_bytes, w2_scale, r, wf,
         ws = keep.tile([P, PASSES, 4], F32, name="ws")
         r_bf = keep.tile([P, HEADS, 8], BF16, name="r_bf")
         a_bf = keep.tile([P, 2 * HEADS, 8], BF16, name="a_bf")
+        x_first = {}
         x_raw = {}
-        w1_raw = {}
         w2_raw = {}
-        wf_raw = {}
+        rows4 = {}
+
+        def load_x_first():
+            for i in range(TT):
+                x_first[i] = keep.tile([P, KP], BF16, name="x_first%d" % i)
+                nc.sync.dma_start(out=x_first[i][:], in_=x[i * P : (i + 1) * P, 0:KP])
 
         def load_x(c, g):
-            x_raw[c, g] = keep.tile([P, TT, 512], BF16, name="x_raw%d_%d" % (c, g))
+            x_raw[c, g] = keep.tile([P, TT, KP], BF16, name="x_raw%d_%d" % (c, g))
             nc.sync.dma_start(
                 out=x_raw[c, g][:],
-                in_=x[c * TB : (c + 1) * TB, g * 512 : (g + 1) * 512].rearrange("(i p) k -> p i k", p=P),
+                in_=x[c * TB : (c + 1) * TB, g * KP : (g + 1) * KP].rearrange("(i p) k -> p i k", p=P),
             )
 
         def load_w1(h, g):
-            w1_raw[h, g] = keep.tile([P, 4, W], BF16, name="w1_raw%d_%d" % (h, g))
+            rows4["w1", h, g] = keep.tile([P, 4, W], BF16, name="w1_raw%d_%d" % (h, g))
             nc.sync.dma_start(
-                out=w1_raw[h, g][:],
-                in_=w1[g * 512 : (g + 1) * 512, h * W : (h + 1) * W].rearrange("(p j) n -> p j n", j=4),
+                out=rows4["w1", h, g][:],
+                in_=w1[g * KP : (g + 1) * KP, h * W : (h + 1) * W].rearrange("(p j) n -> p j n", j=4),
             )
 
         def load_w2(h, g):
             w2_raw[h, g] = keep.tile([P, 4, W], U8, name="w2_raw%d_%d" % (h, g))
             nc.sync.dma_start(
                 out=w2_raw[h, g][:],
-                in_=w2_bytes[g * 512 : (g + 1) * 512, h * W : (h + 1) * W].rearrange("(p j) n -> p j n", j=4),
+                in_=w2_bytes[g * KP : (g + 1) * KP, h * W : (h + 1) * W].rearrange("(p j) n -> p j n", j=4),
             )
 
         def load_wf(h):
-            wf_raw[h] = keep.tile([P, 4, W], BF16, name="wf_raw%d" % h)
+            rows4["wf", h, 0] = keep.tile([P, 4, W], BF16, name="wf_raw%d" % h)
             rows = wf[h].rearrange("(m t e) n -> e m t n", t=4, e=2)
             for e in range(2):
-                nc.sync.dma_start(out=wf_raw[h][e::2, :, :], in_=rows[e])
+                nc.sync.dma_start(out=rows4["wf", h, 0][e::2, :, :], in_=rows[e])
+
+        def load_channels(dst, src):
+            for e in range(2):
+                nc.sync.dma_start(out=dst[e::2, :, 0:7], in_=src[:, :, e : e + 7])
 
         nc.scalar.dma_start(out=s_bf[:], in_=s.rearrange("k (g p t) -> p (k g) t", p=P, t=4))
-        load_x(0, 0)
+        load_x_first()
         nc.scalar.dma_start(out=ws[:], in_=w2_scale.rearrange("(g p t) o -> p g (t o)", p=P, t=4))
         load_w2(0, 0)
         load_x(0, 1)
@@ -84,16 +99,12 @@ def tile_finalmlptwostreamfusion_kernel(tc, x, s, w1, w2_bytes, w2_scale, r, wf,
         load_x(1, 1)
         load_w2(1, 0)
         load_w1(1, 1)
-        for e in range(2):
-            nc.sync.dma_start(out=r_bf[e::2, :, 0:7], in_=r.rearrange("(h m c) -> m h c", h=HEADS, c=8)[:, :, e : e + 7])
+        load_channels(r_bf, r.rearrange("(h m c) -> m h c", h=HEADS, c=8))
         load_x(2, 0)
         load_w2(1, 1)
         load_w1(1, 0)
         load_wf(0)
-        for e in range(2):
-            nc.sync.dma_start(
-                out=a_bf[e::2, :, 0:7], in_=a.rearrange("k (h m c) -> m (k h) c", h=HEADS, c=8)[:, :, e : e + 7]
-            )
+        load_channels(a_bf, a.rearrange("k (h m c) -> m (k h) c", h=HEADS, c=8))
         load_x(2, 1)
         load_wf(1)
         load_x(3, 0)
@@ -114,128 +125,127 @@ def tile_finalmlptwostreamfusion_kernel(tc, x, s, w1, w2_bytes, w2_scale, r, wf,
         def widen_a():
             nc.scalar.copy(out=a_f[:], in_=a_bf[:, :, 0:7:2])
 
-        def planes(shape, name):
-            codes = keep.tile([P] + shape, U32, name=name + "_c", align_bytes=64)
-            scales = keep.tile([P] + shape, U8, name=name + "_s", align_bytes=64)
+        def quantize(grouped, columns, name):
+            codes = keep.tile([P, columns], U32, name=name + "_c", align_bytes=64)
+            scales = keep.tile([P, columns], U8, name=name + "_s", align_bytes=64)
+            nc.vector.quantize_mx(out=codes[:].bitcast(X4), scales=scales[:], in_=grouped)
             return codes, scales
 
-        w_q = {}
-        g_q = {}
-        u_q = {}
-
-        def quantize(q, grouped):
-            nc.vector.quantize_mx(out=q[0].bitcast(X4), scales=q[1], in_=grouped)
-
-        def mx(dst, lq, l0, rq, r0, n, start, stop):
+        def mx(dst, weight, t, moving, n0, n, start, stop):
             nc.tensor.matmul_mx(
                 out=dst,
-                lhsT=lq[0][:, l0 : l0 + P].bitcast(X4),
-                lhsT_scale=lq[1][:, l0 : l0 + P],
-                rhs=rq[0][:, r0 : r0 + n].bitcast(X4),
-                rhs_scale=rq[1][:, r0 : r0 + n],
+                lhsT=weight[0][:, t * P : (t + 1) * P].bitcast(X4),
+                lhsT_scale=weight[1][:, t * P : (t + 1) * P],
+                rhs=moving[0][:, n0 : n0 + n].bitcast(X4),
+                rhs_scale=moving[1][:, n0 : n0 + n],
                 start=start,
                 stop=stop,
             )
 
         xt = {}
         xg = {}
+        g_q = {}
 
         def turn_x(c, g):
-            xt[c, g] = psum.tile([P, 2, TB], F32, name="bank")
+            if (c, g) == (0, 0):
+                xt[c, g] = []
+                for i in range(TT):
+                    bank = psum.tile([P, 2, P], F32, name="bank")
+                    for u in range(2):
+                        nc.tensor.transpose(bank[:, u, :], x_first[i][:].bitcast(F32)[:, u::2], ident[:])
+                    xt[c, g].append((i * P, P, bank))
+                return
+            bank = psum.tile([P, 2, TB], F32, name="bank")
             for u in range(2):
                 for i in range(TT):
                     words = x_raw[c, g][:, i, :].bitcast(F32)
-                    nc.tensor.transpose(xt[c, g][:, u, i * P : (i + 1) * P], words[:, u::2], ident[:])
+                    nc.tensor.transpose(bank[:, u, i * P : (i + 1) * P], words[:, u::2], ident[:])
+            xt[c, g] = [(0, TB, bank)]
 
-        def gate_x(c, g, k):
-            xg[c, g, k] = work.tile([P, TB, 4], BF16, name="xg", bufs=10, align_bytes=64)
-            src = xt[c, g][:].bitcast(BF16).rearrange("p u (n e) -> p n u e", e=2)
-            factor = gate[:, PASSES * k + g, :].rearrange("p (u e) -> p u e", e=2).unsqueeze(1)
-            nc.vector.tensor_tensor(
-                out=xg[c, g, k][:].rearrange("p n (u e) -> p n u e", e=2),
-                in0=src,
-                in1=factor.to_broadcast([P, TB, 2, 2]),
-                op=ALU.mult,
-            )
+        def gate_x(c, g, stream):
+            xg[c, g, stream] = work.tile([P, TB, 4], BF16, name="xg", bufs=XG_BUFS, align_bytes=64)
+            factor = gate[:, PASSES * stream + g, :].rearrange("p (u e) -> p u e", e=2).unsqueeze(1)
+            for n0, n, bank in xt[c, g]:
+                nc.vector.tensor_tensor(
+                    out=xg[c, g, stream][:, n0 : n0 + n, :].rearrange("p n (u e) -> p n u e", e=2),
+                    in0=bank[:].bitcast(BF16).rearrange("p u (n e) -> p n u e", e=2),
+                    in1=factor.to_broadcast([P, n, 2, 2]),
+                    op=ALU.mult,
+                )
 
-        def quant_x(c, g, k):
-            codes, scales = planes([TB], "g%dq%d_%d" % (k, c, g))
-            g_q[c, g, k] = (codes, scales)
-            quantize((codes[:], scales[:]), xg[c, g, k][:].rearrange("p n t -> p (n t)"))
+        def quant_x(c, g, stream):
+            grouped = xg[c, g, stream][:].rearrange("p n j -> p (n j)")
+            g_q[c, g, stream] = quantize(grouped, TB, "g%dq%d_%d" % (stream, c, g))
 
-        rows4 = {}
         mixed = {}
         wg = {}
+        w_q = {}
 
-        def widen_w2(h, g, eng):
-            wide = work.tile([P, 4, W], BF16, name="wide", bufs=3)
-            rows4["w2", h, g] = wide
+        def widen_w2(h, g):
+            rows4["w2", h, g] = work.tile([P, 4, W], BF16, name="wide", bufs=WIDE_BUFS)
             for j in range(4):
-                src = w2_raw[h, g][:, j, :].bitcast(FP8)
-                if eng == "v":
-                    nc.vector.tensor_scalar(
-                        out=wide[:, j, :], in0=src, scalar1=ws[:, g, j : j + 1], scalar2=None, op0=ALU.mult
-                    )
-                else:
-                    nc.scalar.activation(out=wide[:, j, :], in_=src, func=ACT.Copy, scale=ws[:, g, j : j + 1])
+                nc.scalar.activation(
+                    out=rows4["w2", h, g][:, j, :],
+                    in_=w2_raw[h, g][:, j, :].bitcast(FP8),
+                    func=ACT.Copy,
+                    scale=ws[:, g, j : j + 1],
+                )
 
-        def mix_w(key):
-            src = rows4[key]
+        def mix_w(piece):
             for half in range(2):
                 bank = psum.tile([P, 2, P, 4], BF16, name="bank")
                 for v in range(2):
                     n0 = (2 * half + v) * P
                     dst = bank[:, v, :, :].rearrange("p n j -> p j n")
-                    nc.tensor.matmul(dst, lhsT=ident_bf[:], rhs=src[:, :, n0 : n0 + P], start=True, stop=True)
-                mixed[key, half] = bank
+                    nc.tensor.matmul(dst, lhsT=ident_bf[:], rhs=rows4[piece][:, :, n0 : n0 + P], start=True, stop=True)
+                mixed[piece, half] = bank
 
-        def take_w(key):
-            wg[key] = work.tile([P, 4 * W], BF16, name="wg", bufs=4, align_bytes=64)
-            dst = wg[key][:].bitcast(F32).rearrange("p (t m v) -> p t m v", t=4, v=4)
+        def take_w(piece):
+            wg[piece] = work.tile([P, 4 * W], BF16, name="wg", bufs=WG_BUFS, align_bytes=64)
+            dst = wg[piece][:].bitcast(F32).rearrange("p (t m v) -> p t m v", t=4, v=4)
             for half in range(2):
-                src = mixed[key, half][:].rearrange("p a n j -> p (a n j)").bitcast(F32)
+                src = mixed[piece, half][:].rearrange("p a n j -> p (a n j)").bitcast(F32)
                 nc.scalar.copy(
-                    out=dst[:, :, 32 * half : 32 * (half + 1), :], in_=src.rearrange("p (m t v) -> p t m v", t=4, v=4)
+                    out=dst[:, :, half * M // 2 : (half + 1) * M // 2, :],
+                    in_=src.rearrange("p (m t v) -> p t m v", t=4, v=4),
                 )
 
-        def group_w(key, eng, slot=0):
-            if eng == "g":
-                wg[key] = work.tile([P, 4 * W], BF16, name="wg_pool%d" % slot, bufs=1, align_bytes=64)
-                dst = wg[key][:].rearrange("p (t m e j) -> p m t e j", t=4, e=2, j=4)
-                src = rows4[key][:].rearrange("p j (m t e) -> p m t e j", t=4, e=2)
-                nc.gpsimd.tensor_scalar(out=dst, in0=src, scalar1=1.0, scalar2=0.0, op0=ALU.mult, op1=ALU.add)
-                return
-            wg[key] = work.tile([P, 4 * W], BF16, name="wg", bufs=4, align_bytes=64)
-            dst = wg[key][:].rearrange("p (t m e j) -> p m t j e", t=4, e=2, j=4)
-            src = rows4[key][:].rearrange("p j (m t e) -> p m t j e", e=2, t=4)
-            if eng == "v":
-                nc.vector.tensor_copy(out=dst, in_=src)
-            else:
-                nc.scalar.copy(out=dst, in_=src)
+        def group_scalar(piece):
+            wg[piece] = work.tile([P, 4 * W], BF16, name="wg", bufs=WG_BUFS, align_bytes=64)
+            nc.scalar.copy(
+                out=wg[piece][:].rearrange("p (t m e j) -> p m t j e", t=4, e=2, j=4),
+                in_=rows4[piece][:].rearrange("p j (m t e) -> p m t j e", e=2, t=4),
+            )
 
-        def quant_w(key):
-            codes, scales = planes([W], "%sq%d_%d" % key)
-            w_q[key] = (codes, scales)
-            quantize((codes[:], scales[:]), wg[key][:])
+        def group_pool(piece):
+            name = "wg_pool1" if piece == POOLED[0] else "wg_pool0"
+            wg[piece] = work.tile([P, 4 * W], BF16, name=name, bufs=1, align_bytes=64)
+            nc.gpsimd.tensor_scalar(
+                out=wg[piece][:].rearrange("p (t m e j) -> p m t e j", t=4, e=2, j=4),
+                in0=rows4[piece][:].rearrange("p j (m t e) -> p m t e j", t=4, e=2),
+                scalar1=1.0,
+                scalar2=0.0,
+                op0=ALU.mult,
+                op1=ALU.add,
+            )
 
-        for h in range(HEADS):
-            rows4["wf", h, 0] = wf_raw[h]
-            for g in range(PASSES):
-                rows4["w1", h, g] = w1_raw[h, g]
+        def quant_w(piece):
+            w_q[piece] = quantize(wg[piece][:], W, "%sq%d_%d" % piece)
 
         z1 = {}
         ug = {}
         o1 = {}
+        u_q = {}
 
         def mul_z1(c, h):
             for i in range(TT):
                 z1[c, h, i] = psum.tile([P, 4, P], F32, name="bank")
                 for t in range(4):
                     for g in range(PASSES):
-                        mx(z1[c, h, i][:, t, :], w_q["w1", h, g], t * P, g_q[c, g, 0], i * P, P, g == 0, g == PASSES - 1)
+                        mx(z1[c, h, i][:, t, :], w_q["w1", h, g], t, g_q[c, g, 0], i * P, P, g == 0, g == PASSES - 1)
 
         def gain_z1(c, h):
-            ug[c, h] = work.tile([P, TT, P, 4], BF16, name="ug", bufs=3, align_bytes=64)
+            ug[c, h] = work.tile([P, TT, P, 4], BF16, name="ug", bufs=UG_BUFS, align_bytes=64)
             for i in range(TT):
                 nc.vector.scalar_tensor_tensor(
                     out=ug[c, h][:, i, :, :],
@@ -247,56 +257,50 @@ def tile_finalmlptwostreamfusion_kernel(tc, x, s, w1, w2_bytes, w2_scale, r, wf,
                 )
 
         def relu_z1(c, h):
-            o1[c, h] = work.tile([P, 4, TB], F32, name="o1", bufs=4)
+            o1[c, h] = work.tile([P, 4, TB], F32, name="o1", bufs=O_BUFS)
             for i in range(TT):
                 nc.scalar.activation(out=o1[c, h][:, :, i * P : (i + 1) * P], in_=z1[c, h, i][:], func=ACT.Relu)
 
-        def weigh_o1(c, h, eng):
+        def weigh_o1(c, h):
             for t in range(4):
                 part = o1[c, h][:, t, :]
-                if eng == "v":
-                    nc.vector.tensor_scalar(out=part, in0=part, scalar1=a_f[:, h, t : t + 1], scalar2=None, op0=ALU.mult)
-                else:
-                    nc.scalar.activation(out=part, in_=part, func=ACT.Copy, scale=a_f[:, h, t : t + 1])
+                nc.scalar.activation(out=part, in_=part, func=ACT.Copy, scale=a_f[:, h, t : t + 1])
 
         def quant_u(c, h):
-            codes, scales = planes([TB], "uq%d_%d" % (c, h))
-            u_q[c, h] = (codes, scales)
-            quantize((codes[:], scales[:]), ug[c, h][:].rearrange("p i n t -> p (i n t)"))
+            u_q[c, h] = quantize(ug[c, h][:].rearrange("p i n t -> p (i n t)"), TB, "uq%d_%d" % (c, h))
 
         z2 = {}
         o2 = {}
+        fb = {}
+        fused = {}
 
         def mul_z2(c, h):
             for pair in range(2):
                 z2[c, h, pair] = psum.tile([P, 2, TB], F32, name="bank")
                 for v in range(2):
                     for g in range(PASSES):
-                        t = 2 * pair + v
-                        mx(z2[c, h, pair][:, v, :], w_q["w2", h, g], t * P, g_q[c, g, 1], 0, TB, g == 0, g == PASSES - 1)
+                        dst = z2[c, h, pair][:, v, :]
+                        mx(dst, w_q["w2", h, g], 2 * pair + v, g_q[c, g, 1], 0, TB, g == 0, g == PASSES - 1)
 
         def relu_z2(c, h):
-            o2[c, h] = work.tile([P, 4, TB], F32, name="o2", bufs=4)
+            o2[c, h] = work.tile([P, 4, TB], F32, name="o2", bufs=O_BUFS)
             for pair in range(2):
                 nc.scalar.activation(out=o2[c, h][:, 2 * pair : 2 * pair + 2, :], in_=z2[c, h, pair][:], func=ACT.Relu)
-
-        fb = {}
-        fused = {}
-        tr = {}
 
         def mul_f(c, h):
             for pair in range(2):
                 fb[c, h, pair] = psum.tile([P, 2, TB], F32, name="bank")
                 for v in range(2):
-                    mx(fb[c, h, pair][:, v, :], w_q["wf", h, 0], (2 * pair + v) * P, u_q[c, h], 0, TB, True, True)
+                    mx(fb[c, h, pair][:, v, :], w_q["wf", h, 0], 2 * pair + v, u_q[c, h], 0, TB, True, True)
 
         def fuse(c, h, pair):
             if pair == 0:
-                fused[c, h] = work.tile([P, 4, TB], F32, name="fused", bufs=3)
-            for t in (2 * pair, 2 * pair + 1):
+                fused[c, h] = work.tile([P, 4, TB], F32, name="fused", bufs=FUSED_BUFS)
+            for v in range(2):
+                t = 2 * pair + v
                 nc.vector.scalar_tensor_tensor(
                     out=fused[c, h][:, t, :],
-                    in0=fb[c, h, t // 2][:, t % 2, :],
+                    in0=fb[c, h, pair][:, v, :],
                     scalar=a_f[:, HEADS + h, t : t + 1],
                     in1=o2[c, h][:, t, :],
                     op0=ALU.add,
@@ -314,154 +318,161 @@ def tile_finalmlptwostreamfusion_kernel(tc, x, s, w1, w2_bytes, w2_scale, r, wf,
                     op1=ALU.add,
                 )
 
-        def turn_out(c, h, terms, tiles):
-            for i in tiles:
-                bank = psum.tile([P, 64, 4, 2], F32, name="bank")
-                for t in range(4):
-                    for j, term in enumerate(terms):
-                        nc.tensor.matmul(
-                            bank[:, :, t, :],
-                            lhsT=term[c, h][:, t, i * P : (i + 1) * P],
-                            rhs=ident[:],
-                            start=j == 0,
-                            stop=j == len(terms) - 1,
-                            is_transpose=True,
-                        )
-                tr[c, h, i] = bank
+        tr = {}
+
+        def turn_tile(term, c, h, i, t, start, stop):
+            nc.tensor.matmul(
+                tr[c, h, i][:, :, t, :],
+                lhsT=term[c, h][:, t, i * P : (i + 1) * P],
+                rhs=ident[:],
+                start=start,
+                stop=stop,
+                is_transpose=True,
+            )
+
+        def turn_out(c, h, i):
+            terms = (fused,) if UNITS.index((c, h)) in MERGED else (o1, fused)
+            tr[c, h, i] = psum.tile([P, M, 4, 2], F32, name="bank")
+            for t in range(4):
+                for n, term in enumerate(terms):
+                    turn_tile(term, c, h, i, t, n == 0, n == len(terms) - 1)
 
         def open_out(c, h):
             for i in range(TT):
-                tr[c, h, i] = psum.tile([P, 64, 4, 2], F32, name="bank")
+                tr[c, h, i] = psum.tile([P, M, 4, 2], F32, name="bank")
                 for t in range(4):
-                    nc.tensor.matmul(
-                        tr[c, h, i][:, :, t, :], lhsT=o1[c, h][:, t, i * P : (i + 1) * P], rhs=ident[:], start=t == 0, stop=False, is_transpose=True
-                    )
+                    turn_tile(o1, c, h, i, t, t == 0, False)
 
         def close_out(c, h, pair):
             for t in (2 * pair, 2 * pair + 1):
                 for i in range(TT):
-                    nc.tensor.matmul(
-                        tr[c, h, i][:, :, t, :], lhsT=fused[c, h][:, t, i * P : (i + 1) * P], rhs=ident[:], start=False, stop=t == 3, is_transpose=True
-                    )
+                    turn_tile(fused, c, h, i, t, False, t == 3)
 
-        def store(c, h, tiles, eng="s"):
-            for i in tiles:
-                rows = work.tile([P, W], F32, name="rows", bufs=6)
-                dst = rows[:]
-                src = tr[c, h, i][:].rearrange("n m t e -> n (m t e)")
-                if eng == "v":
-                    nc.vector.tensor_copy(out=dst, in_=src)
-                else:
-                    nc.scalar.copy(out=dst, in_=src)
-                n0 = c * TB + i * P
-                nc.sync.dma_start(out=out[n0 : n0 + P, h * W : (h + 1) * W], in_=rows[:])
+        def store(c, h, i, copy):
+            rows = work.tile([P, W], F32, name="rows", bufs=ROW_BUFS)
+            copy(out=rows[:], in_=tr[c, h, i][:].rearrange("n m t e -> n (m t e)"))
+            n0 = c * TB + i * P
+            nc.sync.dma_start(out=out[n0 : n0 + P, h * W : (h + 1) * W], in_=rows[:])
 
-        U = [(0, 0), (1, 0), (0, 1), (1, 1), (2, 0), (2, 1), (3, 0), (3, 1)]
-        A0, A1, B0, B1, F0 = ("w1", 0, 0), ("w1", 0, 1), ("w2", 0, 0), ("w2", 0, 1), ("wf", 0, 0)
-        C0, C1, D0, D1, F1 = ("w1", 1, 0), ("w1", 1, 1), ("w2", 1, 0), ("w2", 1, 1), ("wf", 1, 0)
-        MIXED = (B1, C0, D0)
-        last = len(U) - 1
-        def terms(k):
-            return (fused,) if k in MERGED else (o1, fused)
-        def T(k, i):
-            return (turn_out, *U[k], terms(k), (i,))
-        def E(k, i, e="s"):
-            return (store, *U[k], (i,), e)
-        gates = {2: (2, 0), 3: (2, 1), 4: (3, 0), 5: (3, 1)}
-        pe = [(turn_x, 0, 0), (turn_x, 0, 1), (turn_x, 1, 0), (turn_x, 1, 1), (mix_w, B1), (turn_x, 2, 0), (mul_z1, 0, 0), (mix_w, C0), (mul_z1, 1, 0), (mul_z2, 0, 0), (mix_w, D0), (mul_f, 0, 0)]
-        sc = [(widen_w2, 0, 0, "s"), (widen_w2, 0, 1, "s"), (group_w, B0, "s"), (widen_w2, 1, 0, "s"), (take_w, B1), (widen_r,), (widen_w2, 1, 1, "s"), (group_w, F0, "s"), (take_w, C0), (relu_z1, 0, 0), (widen_a,), (relu_z2, 0, 0), (relu_z1, 1, 0), (weigh_o1, 0, 0, "s")]
-        ve = [(gate_x, 0, 0, 0), (gate_x, 0, 0, 1), (gate_x, 0, 1, 0), (gate_x, 0, 1, 1), (gate_x, 1, 0, 0), (gate_x, 1, 0, 1), (gate_x, 1, 1, 0),
-              (quant_x, 0, 0, 0), (quant_x, 0, 1, 0), (quant_w, A0), (quant_w, A1),
-              (gate_x, 1, 1, 1), (gate_x, 2, 0, 0), (gain_z1, 0, 0),
-              (quant_x, 1, 0, 0), (quant_x, 1, 1, 0), (quant_w, B0), (quant_u, 0, 0), (quant_x, 0, 0, 1), (quant_x, 0, 1, 1), (quant_w, B1), (quant_x, 1, 0, 1), (quant_x, 1, 1, 1), (gain_z1, 1, 0), (quant_w, F0), (quant_w, C0), (quant_u, 1, 0), (quant_x, 2, 0, 0), (quant_w, C1),
-              (gate_x, 2, 0, 1), (fuse, 0, 0, 0), (fuse, 0, 0, 1)]
-        gp = [(group_w, A0, "g", 1), (group_w, A1, "g"), (group_w, C1, "g"), (group_w, D1, "g"), (group_w, F1, "g")]
-        for k in range(2, last - 1):
-            gt = gates[k]
+        def store_scalar(c, h, i):
+            store(c, h, i, nc.scalar.copy)
+
+        def store_vector(c, h, i):
+            store(c, h, i, nc.vector.tensor_copy)
+
+        W1 = {(h, g): ("w1", h, g) for h in range(HEADS) for g in range(PASSES)}
+        W2 = {(h, g): ("w2", h, g) for h in range(HEADS) for g in range(PASSES)}
+        WF = {h: ("wf", h, 0) for h in range(HEADS)}
+        MIXED = (W2[0, 1], W1[1, 0], W2[1, 0])
+        POOLED = (W1[0, 0], W1[0, 1], W1[1, 1], W2[1, 1], WF[1])
+
+        def unit(fn, k, *rest):
+            return (fn, *UNITS[k], *rest)
+
+        def both(fn, k):
+            return [unit(fn, k, 0), unit(fn, k, 1)]
+
+        tensor = [(turn_x, c, g) for c in range(2) for g in range(PASSES)]
+        tensor += [(mix_w, W2[0, 1]), (turn_x, 2, 0), unit(mul_z1, 0), (mix_w, W1[1, 0]), unit(mul_z1, 1)]
+        tensor += [unit(mul_z2, 0), (mix_w, W2[1, 0]), unit(mul_f, 0)]
+
+        scalar = [(widen_w2, 0, 0), (widen_w2, 0, 1), (group_scalar, W2[0, 0]), (widen_w2, 1, 0), (take_w, W2[0, 1])]
+        scalar += [(widen_r,), (widen_w2, 1, 1), (group_scalar, WF[0]), (take_w, W1[1, 0]), unit(relu_z1, 0)]
+        scalar += [(widen_a,), unit(relu_z2, 0), unit(relu_z1, 1), unit(weigh_o1, 0)]
+
+        first_gates = [(gate_x, c, g, stream) for c in range(2) for g in range(PASSES) for stream in range(2)]
+        vector = first_gates[:-1]
+        vector += [(quant_x, 0, 0, 0), (quant_x, 0, 1, 0), (quant_w, W1[0, 0]), (quant_w, W1[0, 1])]
+        vector += [first_gates[-1], (gate_x, 2, 0, 0), unit(gain_z1, 0)]
+        vector += [(quant_x, 1, 0, 0), (quant_x, 1, 1, 0), (quant_w, W2[0, 0]), unit(quant_u, 0)]
+        vector += [(quant_x, 0, 0, 1), (quant_x, 0, 1, 1), (quant_w, W2[0, 1]), (quant_x, 1, 0, 1), (quant_x, 1, 1, 1)]
+        vector += [unit(gain_z1, 1), (quant_w, WF[0]), (quant_w, W1[1, 0]), unit(quant_u, 1), (quant_x, 2, 0, 0)]
+        vector += [(quant_w, W1[1, 1])]
+        vector += [(gate_x, 2, 0, 1)] + both(fuse, 0)
+
+        pool = [(group_pool, piece) for piece in POOLED]
+
+        gated_in = {2: (2, 0), 3: (2, 1), 4: (3, 0), 5: (3, 1)}
+        for k, cg in gated_in.items():
+            next_x = [(turn_x, *gated_in[k + 1])] if k + 1 in gated_in else []
+            gates = [(gate_x, *cg, 0), (gate_x, *cg, 1)]
             if k == 2:
-                pe += [(mul_z2, *U[k - 1]), (mul_z1, *U[k]), (mul_f, *U[k - 1]), T(k - 2, 0), T(k - 2, 1)]
+                tensor += [unit(mul_z2, 1), unit(mul_z1, 2), unit(mul_f, 1)] + both(turn_out, 0) + next_x
+                vector += [unit(gain_z1, 2), (quant_x, *cg, 1), (quant_w, W2[1, 0]), unit(quant_u, 2)]
+                vector += [(quant_w, W2[1, 1])] + both(fuse, 1)
+                scalar += [(take_w, W2[1, 0])]
             elif k == 3:
-                pe += [(mul_z2, *U[k - 1]), T(k - 2, 0), (mul_z1, *U[k]), T(k - 2, 1)]
+                tensor += [unit(mul_z2, 2), unit(turn_out, 1, 0), unit(mul_z1, 3), unit(turn_out, 1, 1)]
+                tensor += next_x + [unit(mul_f, 2)]
+                vector += gates + [(quant_w, WF[1]), (quant_x, *cg, 0), unit(gain_z1, 3), (quant_x, *cg, 1)]
+                vector += [unit(fuse, 2, 0), unit(quant_u, 3), unit(fuse, 2, 1)]
             else:
-                pe += [(mul_z2, *U[k - 1]), T(k - 2, 0), (mul_z1, *U[k]), (mul_f, *U[k - 1]), T(k - 2, 1)]
-            if k + 1 in gates:
-                pe.append((turn_x, *gates[k + 1]))
-            if k == 3:
-                pe.append((mul_f, *U[k - 1]))
-            if k == 2:
-                ve += [(gain_z1, *U[k]), (quant_x, *gt, 1), (quant_w, D0), (quant_u, *U[k]), (quant_w, D1), (fuse, *U[k - 1], 0), (fuse, *U[k - 1], 1)]
-                sc += [(take_w, D0)]
-            elif k == 3:
-                ve += [(gate_x, *gt, 0), (gate_x, *gt, 1), (quant_w, F1), (quant_x, *gt, 0), (gain_z1, *U[k]), (quant_x, *gt, 1), (fuse, *U[k - 1], 0), (quant_u, *U[k]), (fuse, *U[k - 1], 1)]
-            else:
-                ve += [(gate_x, *gt, 0), (gate_x, *gt, 1), (quant_x, *gt, 0), (quant_x, *gt, 1), (gain_z1, *U[k]), (fuse, *U[k - 1], 0), (quant_u, *U[k]), (fuse, *U[k - 1], 1)]
-            sc += [(relu_z2, *U[k - 1]), E(k - 2, 0), (weigh_o1, *U[k - 1], "s"), (relu_z1, *U[k]), E(k - 2, 1)]
-        a4, a5, a6, a7 = U[4:]
-        pe += [(mul_z2, *a5), (mul_z1, *a6), (mul_f, *a5), T(4, 0), (mul_z1, *a7), (mul_z2, *a6), T(4, 1), (mul_f, *a6), (mul_z2, *a7), T(5, 0), (mul_f, *a7), T(5, 1), T(6, 0), T(6, 1), (open_out, *a7), (close_out, *a7, 0), (close_out, *a7, 1)]
-        ve += [(gain_z1, *a6), (fuse, *a5, 0), (quant_u, *a6), (fuse, *a5, 1), (gain_z1, *a7)] + ([(merge, *a5)] if 5 in MERGED else []) + [(quant_u, *a7), (fuse, *a6, 0), (fuse, *a6, 1)] + ([(merge, *a6)] if 6 in MERGED else []) + [(fuse, *a7, 0), (fuse, *a7, 1), E(6, 1, "v"), E(7, 1, "v")]
-        sc += [(relu_z2, *a5)] + ([] if 5 in MERGED else [(weigh_o1, *a5, "s")]) + [(relu_z1, *a6), E(4, 0), (relu_z1, *a7), (relu_z2, *a6), E(4, 1), (relu_z2, *a7)] + ([] if 6 in MERGED else [(weigh_o1, *a6, "s")]) + [(weigh_o1, *a7, "s"), E(5, 0), E(5, 1), E(6, 0), E(7, 0)]
+                tensor += [unit(mul_z2, k - 1), unit(turn_out, k - 2, 0), unit(mul_z1, k), unit(mul_f, k - 1)]
+                tensor += [unit(turn_out, k - 2, 1)] + next_x
+                vector += gates + [(quant_x, *cg, 0), (quant_x, *cg, 1), unit(gain_z1, k)]
+                vector += [unit(fuse, k - 1, 0), unit(quant_u, k), unit(fuse, k - 1, 1)]
+            scalar += [unit(relu_z2, k - 1), unit(store_scalar, k - 2, 0), unit(weigh_o1, k - 1)]
+            scalar += [unit(relu_z1, k), unit(store_scalar, k - 2, 1)]
 
-        def needs(fn, args):
-            if fn in (widen_r, widen_a):
+        k4, k5, k6, k7 = range(LAST - 3, LAST + 1)
+        tensor += [unit(mul_z2, k5), unit(mul_z1, k6), unit(mul_f, k5), unit(turn_out, k4, 0), unit(mul_z1, k7)]
+        tensor += [unit(mul_z2, k6), unit(turn_out, k4, 1), unit(mul_f, k6), unit(mul_z2, k7), unit(turn_out, k5, 0)]
+        tensor += [unit(mul_f, k7), unit(turn_out, k5, 1)] + both(turn_out, k6)
+        tensor += [unit(open_out, k7)] + both(close_out, k7)
+        vector += [unit(gain_z1, k6), unit(fuse, k5, 0), unit(quant_u, k6), unit(fuse, k5, 1), unit(gain_z1, k7)]
+        vector += [unit(merge, k5), unit(quant_u, k7)] + both(fuse, k6) + [unit(merge, k6)] + both(fuse, k7)
+        vector += [unit(store_vector, k6, 1), unit(store_vector, k7, 1)]
+        scalar += [unit(relu_z2, k5), unit(relu_z1, k6), unit(store_scalar, k4, 0), unit(relu_z1, k7)]
+        scalar += [unit(relu_z2, k6), unit(store_scalar, k4, 1), unit(relu_z2, k7), unit(weigh_o1, k7)]
+        scalar += both(store_scalar, k5) + [unit(store_scalar, k6, 0), unit(store_scalar, k7, 0)]
+
+        def needs(fn, *args):
+            if fn in (turn_x, widen_w2, widen_r, widen_a):
                 return []
             if fn is gate_x:
-                return [(turn_x, args[:2])]
+                return [(turn_x, *args[:2])]
             if fn is quant_x:
-                return [(gate_x, args)]
-            if fn in (mix_w, group_w):
-                return [(widen_w2, args[0][1:])] if args[0][0] == "w2" else []
+                return [(gate_x, *args)]
+            if fn in (mix_w, group_scalar, group_pool):
+                return [(widen_w2, *args[0][1:])] if args[0][0] == "w2" else []
             if fn is take_w:
-                return [(mix_w, args)]
+                return [(mix_w, *args)]
             if fn is quant_w:
-                return [(take_w, args)] if args[0] in MIXED else [(group_w, args)]
+                return [(take_w if args[0] in MIXED else group_pool if args[0] in POOLED else group_scalar, *args)]
             c, h = args[:2]
             if fn is mul_z1:
-                return [(quant_w, (("w1", h, g),)) for g in range(PASSES)] + [(quant_x, (c, g, 0)) for g in range(PASSES)]
+                return [(quant_w, W1[h, g]) for g in range(PASSES)] + [(quant_x, c, g, 0) for g in range(PASSES)]
             if fn is mul_z2:
-                return [(quant_w, (("w2", h, g),)) for g in range(PASSES)] + [(quant_x, (c, g, 1)) for g in range(PASSES)]
+                return [(quant_w, W2[h, g]) for g in range(PASSES)] + [(quant_x, c, g, 1) for g in range(PASSES)]
             if fn is gain_z1:
-                return [(mul_z1, (c, h)), (widen_r, ())]
-            if fn is relu_z1:
-                return [(gain_z1, (c, h))]
+                return [(mul_z1, c, h), (widen_r,)]
+            if fn in (relu_z1, quant_u):
+                return [(gain_z1, c, h)]
             if fn is weigh_o1:
-                return [(relu_z1, (c, h)), (widen_a, ())]
-            if fn is quant_u:
-                return [(gain_z1, (c, h))]
+                return [(relu_z1, c, h), (widen_a,)]
             if fn is relu_z2:
-                return [(mul_z2, (c, h))]
+                return [(mul_z2, c, h)]
             if fn is mul_f:
-                return [(quant_u, (c, h)), (quant_w, (("wf", h, 0),))]
+                return [(quant_u, c, h), (quant_w, WF[h])]
             if fn is fuse:
-                return [(mul_f, (c, h)), (relu_z2, (c, h)), (widen_a, ())]
+                return [(mul_f, c, h), (relu_z2, c, h), (widen_a,)]
             if fn is merge:
-                return [(fuse, (c, h, 1)), (relu_z1, (c, h))]
+                return [(fuse, c, h, 1), (relu_z1, c, h)]
             if fn is turn_out:
-                return [(merge, (c, h))] if len(args[2]) == 1 else [(fuse, (c, h, 1)), (weigh_o1, (c, h))]
+                return [(merge, c, h)] if UNITS.index((c, h)) in MERGED else [(fuse, c, h, 1), (weigh_o1, c, h)]
             if fn is open_out:
-                return [(weigh_o1, (c, h))]
+                return [(weigh_o1, c, h)]
             if fn is close_out:
-                return [(fuse, args), (open_out, (c, h))]
-            if fn is store:
-                return [(close_out, (c, h, 1))] if (c, h) == U[last] else [(turn_out, (c, h, args[2]))]
-            return []
-
-        def name_of(fn, args):
-            if fn in (widen_w2, weigh_o1):
-                return (fn, args[:2])
-            if fn is group_w:
-                return (fn, args[:1])
-            if fn is turn_out:
-                return (fn, (args[0], args[1], args[3]))
-            return (fn, args)
+                return [(fuse, *args), (open_out, c, h)]
+            return [(close_out, c, h, 1)] if (c, h) == UNITS[LAST] else [(turn_out, *args)]
 
         done = set()
-        queues = [list(pe), list(ve), list(sc), list(gp)]
-        while any(queues):
-            moved = False
-            for queue in queues:
-                while queue and all(n in done for n in needs(queue[0][0], queue[0][1:])):
-                    item = queue.pop(0)
-                    item[0](*item[1:])
-                    done.add(name_of(item[0], item[1:]))
-                    moved = True
-            assert moved
+        programs = [tensor, vector, scalar, pool]
+        while any(programs):
+            before = len(done)
+            for program in programs:
+                while program and all(stage in done for stage in needs(*program[0])):
+                    stage = program.pop(0)
+                    stage[0](*stage[1:])
+                    done.add(stage)
+            assert len(done) > before

@@ -25,9 +25,9 @@ M = P // 2
 
 UNITS = [(0, 0), (1, 0), (0, 1), (1, 1), (2, 0), (2, 1), (3, 0), (3, 1)]
 LAST = len(UNITS) - 1
-MERGED = (LAST - 2, LAST - 1)
+MERGED = (3, 4, 5)
 
-XG_BUFS, WIDE_BUFS, WG_BUFS, UG_BUFS, O_BUFS, FUSED_BUFS, ROW_BUFS = 10, 3, 4, 3, 4, 3, 6
+XG_BUFS, WIDE_BUFS, WG_BUFS, UG_BUFS, O_BUFS, FUSED_BUFS, ROW_BUFS = 9, 3, 4, 3, 5, 4, 6
 
 
 def tile_finalmlptwostreamfusion_kernel(tc, x, s, w1, w2_bytes, w2_scale, r, wf, a, out):
@@ -77,6 +77,12 @@ def tile_finalmlptwostreamfusion_kernel(tc, x, s, w1, w2_bytes, w2_scale, r, wf,
                 in_=w2_bytes[g * KP : (g + 1) * KP, h * W : (h + 1) * W].rearrange("(p j) n -> p j n", j=4),
             )
 
+        def load_w2_wide(g):
+            raw = keep.tile([P, 4, H], U8, name="w2_wide%d" % g)
+            nc.sync.dma_start(out=raw[:], in_=w2_bytes[g * KP : (g + 1) * KP, :].rearrange("(p j) n -> p j n", j=4))
+            for h in range(HEADS):
+                w2_raw[h, g] = raw[:, :, h * W : (h + 1) * W]
+
         def load_wf(h):
             rows4["wf", h, 0] = keep.tile([P, 4, W], BF16, name="wf_raw%d" % h)
             rows = wf[h].rearrange("(m t e) n -> e m t n", t=4, e=2)
@@ -99,11 +105,11 @@ def tile_finalmlptwostreamfusion_kernel(tc, x, s, w1, w2_bytes, w2_scale, r, wf,
         load_x(1, 1)
         load_w2(1, 0)
         load_w1(1, 1)
-        load_channels(r_bf, r.rearrange("(h m c) -> m h c", h=HEADS, c=8))
         load_x(2, 0)
-        load_w2(1, 1)
-        load_w1(1, 0)
+        load_channels(r_bf, r.rearrange("(h m c) -> m h c", h=HEADS, c=8))
         load_wf(0)
+        load_w1(1, 0)
+        load_w2(1, 1)
         load_channels(a_bf, a.rearrange("k (h m c) -> m (k h) c", h=HEADS, c=8))
         load_x(2, 1)
         load_wf(1)
@@ -181,9 +187,10 @@ def tile_finalmlptwostreamfusion_kernel(tc, x, s, w1, w2_bytes, w2_scale, r, wf,
         wg = {}
         w_q = {}
 
-        def widen_w2(h, g):
-            rows4["w2", h, g] = work.tile([P, 4, W], BF16, name="wide", bufs=WIDE_BUFS)
-            for j in range(4):
+        def widen_w2(h, g, half):
+            if half == 0:
+                rows4["w2", h, g] = work.tile([P, 4, W], BF16, name="wide", bufs=WIDE_BUFS)
+            for j in (2 * half, 2 * half + 1):
                 nc.scalar.activation(
                     out=rows4["w2", h, g][:, j, :],
                     in_=w2_raw[h, g][:, j, :].bitcast(FP8),
@@ -210,11 +217,13 @@ def tile_finalmlptwostreamfusion_kernel(tc, x, s, w1, w2_bytes, w2_scale, r, wf,
                     in_=src.rearrange("p (m t v) -> p t m v", t=4, v=4),
                 )
 
-        def group_scalar(piece):
-            wg[piece] = work.tile([P, 4 * W], BF16, name="wg", bufs=WG_BUFS, align_bytes=64)
+        def group_scalar(piece, half):
+            if half == 0:
+                wg[piece] = work.tile([P, 4 * W], BF16, name="wg", bufs=WG_BUFS, align_bytes=64)
+            pairs = slice(half * M // 2, (half + 1) * M // 2)
             nc.scalar.copy(
-                out=wg[piece][:].rearrange("p (t m e j) -> p m t j e", t=4, e=2, j=4),
-                in_=rows4[piece][:].rearrange("p j (m t e) -> p m t j e", e=2, t=4),
+                out=wg[piece][:].rearrange("p (t m e j) -> p m t j e", t=4, e=2, j=4)[:, pairs],
+                in_=rows4[piece][:].rearrange("p j (m t e) -> p m t j e", e=2, t=4)[:, pairs],
             )
 
         def group_pool(piece):
@@ -236,13 +245,35 @@ def tile_finalmlptwostreamfusion_kernel(tc, x, s, w1, w2_bytes, w2_scale, r, wf,
         ug = {}
         o1 = {}
         u_q = {}
+        weighed = {}
 
-        def mul_z1(c, h):
-            for i in range(TT):
-                z1[c, h, i] = psum.tile([P, 4, P], F32, name="bank")
-                for t in range(4):
+        def mul_z1_wide(c, h):
+            for pair in range(2):
+                z1[c, h, pair] = psum.tile([P, 2, TB], F32, name="bank")
+                for v in range(2):
                     for g in range(PASSES):
-                        mx(z1[c, h, i][:, t, :], w_q["w1", h, g], t, g_q[c, g, 0], i * P, P, g == 0, g == PASSES - 1)
+                        dst = z1[c, h, pair][:, v, :]
+                        mx(dst, w_q["w1", h, g], 2 * pair + v, g_q[c, g, 0], 0, TB, g == 0, g == PASSES - 1)
+
+        def relu_z1_wide(c, h):
+            o1[c, h] = work.tile([P, 4, TB], F32, name="o1", bufs=O_BUFS)
+            for pair in range(2):
+                nc.scalar.activation(out=o1[c, h][:, 2 * pair : 2 * pair + 2, :], in_=z1[c, h, pair][:], func=ACT.Relu)
+
+        def gain_pool(c, h):
+            ug[c, h] = work.tile([P, TT, P, 4], BF16, name="wg_pool0", bufs=1, align_bytes=64)
+            nc.gpsimd.tensor_tensor(
+                out=ug[c, h][:].rearrange("p i n t -> p (i n) t"),
+                in0=o1[c, h][:].rearrange("p t n -> p n t"),
+                in1=r_f[:, h, :].unsqueeze(1).to_broadcast([P, TB, 4]),
+                op=ALU.mult,
+            )
+
+        def mul_z1(c, h, i):
+            z1[c, h, i] = psum.tile([P, 4, P], F32, name="bank")
+            for t in range(4):
+                for g in range(PASSES):
+                    mx(z1[c, h, i][:, t, :], w_q["w1", h, g], t, g_q[c, g, 0], i * P, P, g == 0, g == PASSES - 1)
 
         def gain_z1(c, h):
             ug[c, h] = work.tile([P, TT, P, 4], BF16, name="ug", bufs=UG_BUFS, align_bytes=64)
@@ -262,9 +293,13 @@ def tile_finalmlptwostreamfusion_kernel(tc, x, s, w1, w2_bytes, w2_scale, r, wf,
                 nc.scalar.activation(out=o1[c, h][:, :, i * P : (i + 1) * P], in_=z1[c, h, i][:], func=ACT.Relu)
 
         def weigh_o1(c, h):
+            weighed[c, h] = o1[c, h]
+            if UNITS.index((c, h)) in POOL_GAINED:
+                weighed[c, h] = work.tile([P, 4, TB], F32, name="weighed", bufs=1)
             for t in range(4):
-                part = o1[c, h][:, t, :]
-                nc.scalar.activation(out=part, in_=part, func=ACT.Copy, scale=a_f[:, h, t : t + 1])
+                nc.scalar.activation(
+                    out=weighed[c, h][:, t, :], in_=o1[c, h][:, t, :], func=ACT.Copy, scale=a_f[:, h, t : t + 1]
+                )
 
         def quant_u(c, h):
             u_q[c, h] = quantize(ug[c, h][:].rearrange("p i n t -> p (i n t)"), TB, "uq%d_%d" % (c, h))
@@ -331,7 +366,7 @@ def tile_finalmlptwostreamfusion_kernel(tc, x, s, w1, w2_bytes, w2_scale, r, wf,
             )
 
         def turn_out(c, h, i):
-            terms = (fused,) if UNITS.index((c, h)) in MERGED else (o1, fused)
+            terms = (fused,) if UNITS.index((c, h)) in MERGED else (weighed, fused)
             tr[c, h, i] = psum.tile([P, M, 4, 2], F32, name="bank")
             for t in range(4):
                 for n, term in enumerate(terms):
@@ -341,30 +376,32 @@ def tile_finalmlptwostreamfusion_kernel(tc, x, s, w1, w2_bytes, w2_scale, r, wf,
             for i in range(TT):
                 tr[c, h, i] = psum.tile([P, M, 4, 2], F32, name="bank")
                 for t in range(4):
-                    turn_tile(o1, c, h, i, t, t == 0, False)
+                    turn_tile(weighed, c, h, i, t, t == 0, False)
 
         def close_out(c, h, pair):
             for t in (2 * pair, 2 * pair + 1):
                 for i in range(TT):
                     turn_tile(fused, c, h, i, t, False, t == 3)
 
-        def store(c, h, i, copy):
-            rows = work.tile([P, W], F32, name="rows", bufs=ROW_BUFS)
-            copy(out=rows[:], in_=tr[c, h, i][:].rearrange("n m t e -> n (m t e)"))
+        rows = {}
+
+        def copy_out(c, h, i, copy):
+            rows[c, h, i] = work.tile([P, W], F32, name="rows", bufs=ROW_BUFS)
+            copy(out=rows[c, h, i][:], in_=tr[c, h, i][:].rearrange("n m t e -> n (m t e)"))
+
+        def copy_scalar(c, h, i):
+            copy_out(c, h, i, nc.scalar.copy)
+
+        def copy_vector(c, h, i):
+            copy_out(c, h, i, nc.vector.tensor_copy)
+
+        def store(c, h, i):
             n0 = c * TB + i * P
-            nc.sync.dma_start(out=out[n0 : n0 + P, h * W : (h + 1) * W], in_=rows[:])
-
-        def store_scalar(c, h, i):
-            store(c, h, i, nc.scalar.copy)
-
-        def store_vector(c, h, i):
-            store(c, h, i, nc.vector.tensor_copy)
+            nc.sync.dma_start(out=out[n0 : n0 + P, h * W : (h + 1) * W], in_=rows[c, h, i][:])
 
         W1 = {(h, g): ("w1", h, g) for h in range(HEADS) for g in range(PASSES)}
         W2 = {(h, g): ("w2", h, g) for h in range(HEADS) for g in range(PASSES)}
         WF = {h: ("wf", h, 0) for h in range(HEADS)}
-        MIXED = (W2[0, 1], W1[1, 0], W2[1, 0])
-        POOLED = (W1[0, 0], W1[0, 1], W1[1, 1], W2[1, 1], WF[1])
 
         def unit(fn, k, *rest):
             return (fn, *UNITS[k], *rest)
@@ -372,59 +409,61 @@ def tile_finalmlptwostreamfusion_kernel(tc, x, s, w1, w2_bytes, w2_scale, r, wf,
         def both(fn, k):
             return [unit(fn, k, 0), unit(fn, k, 1)]
 
-        tensor = [(turn_x, c, g) for c in range(2) for g in range(PASSES)]
-        tensor += [(mix_w, W2[0, 1]), (turn_x, 2, 0), unit(mul_z1, 0), (mix_w, W1[1, 0]), unit(mul_z1, 1)]
-        tensor += [unit(mul_z2, 0), (mix_w, W2[1, 0]), unit(mul_f, 0)]
+        def gates(c, g):
+            return [(gate_x, c, g, 0), (gate_x, c, g, 1)]
 
-        scalar = [(widen_w2, 0, 0), (widen_w2, 0, 1), (group_scalar, W2[0, 0]), (widen_w2, 1, 0), (take_w, W2[0, 1])]
-        scalar += [(widen_r,), (widen_w2, 1, 1), (group_scalar, WF[0]), (take_w, W1[1, 0]), unit(relu_z1, 0)]
-        scalar += [(widen_a,), unit(relu_z2, 0), unit(relu_z1, 1), unit(weigh_o1, 0)]
+        def quants(c, g):
+            return [(quant_x, c, g, 0), (quant_x, c, g, 1)]
+
+        def grouped(piece):
+            return [(group_scalar, piece, 0), (group_scalar, piece, 1)]
+
+        def widened(h, g):
+            return [(widen_w2, h, g, 0), (widen_w2, h, g, 1)]
+
+        MIXED = (W2[0, 1], W1[1, 0])
+        POOLED = (W1[0, 0], W1[0, 1], W1[1, 1], W2[1, 0], W2[1, 1], WF[1])
+        POOL_GAINED = (4, 5, 6)
+
+        tensor = [(turn_x, c, g) for c in range(2) for g in range(PASSES)]
+        tensor += [(mix_w, W2[0, 1]), (turn_x, 2, 0)] + both(mul_z1, 0) + [(mix_w, W1[1, 0])] + both(mul_z1, 1)
+        tensor += [unit(mul_z2, 0), unit(mul_f, 0), unit(mul_z2, 1)] + both(mul_z1, 2) + [(turn_x, 2, 1), unit(turn_out, 0, 0)]
+        tensor += [unit(mul_f, 1), unit(turn_out, 0, 1), unit(mul_z1, 3, 0), (turn_x, 3, 0), unit(turn_out, 1, 0), unit(mul_z1, 3, 1), unit(turn_out, 1, 1)]
+        tensor += [unit(mul_z1_wide, 4), unit(mul_z2, 2), unit(mul_z2, 3), (turn_x, 3, 1), unit(mul_z1_wide, 5), unit(mul_f, 2), unit(mul_z2, 4), unit(mul_f, 3)]
+        tensor += [unit(mul_z2, 5)] + both(turn_out, 2) + [unit(mul_f, 4), unit(mul_z1_wide, 6)]
+        tensor += both(mul_z1, 7) + [unit(mul_z2, 6), unit(mul_f, 5)] + both(turn_out, 3) + [unit(mul_z2, 7), unit(mul_f, 6), unit(mul_f, 7)]
+        tensor += both(turn_out, 4) + both(turn_out, 5) + [unit(open_out, 7)] + both(turn_out, 6)
+        tensor += both(close_out, 7)
 
         first_gates = [(gate_x, c, g, stream) for c in range(2) for g in range(PASSES) for stream in range(2)]
         vector = first_gates[:-1]
         vector += [(quant_x, 0, 0, 0), (quant_x, 0, 1, 0), (quant_w, W1[0, 0]), (quant_w, W1[0, 1])]
         vector += [first_gates[-1], (gate_x, 2, 0, 0), unit(gain_z1, 0)]
-        vector += [(quant_x, 1, 0, 0), (quant_x, 1, 1, 0), (quant_w, W2[0, 0]), unit(quant_u, 0)]
-        vector += [(quant_x, 0, 0, 1), (quant_x, 0, 1, 1), (quant_w, W2[0, 1]), (quant_x, 1, 0, 1), (quant_x, 1, 1, 1)]
-        vector += [unit(gain_z1, 1), (quant_w, WF[0]), (quant_w, W1[1, 0]), unit(quant_u, 1), (quant_x, 2, 0, 0)]
-        vector += [(quant_w, W1[1, 1])]
-        vector += [(gate_x, 2, 0, 1)] + both(fuse, 0)
+        vector += [(quant_x, 1, 0, 0), (quant_x, 1, 1, 0), (quant_w, W2[0, 0]), (quant_x, 0, 0, 1), (quant_x, 0, 1, 1), (quant_w, W2[0, 1])]
+        vector += [unit(quant_u, 0), (quant_w, WF[0]), (quant_x, 1, 0, 1), (quant_x, 1, 1, 1), (quant_w, W1[1, 0]), (quant_w, W1[1, 1])]
+        vector += [unit(gain_z1, 1)] + both(fuse, 0) + [(gate_x, 2, 0, 1)]
+        vector += [unit(quant_u, 1)] + quants(2, 0) + [(quant_w, W2[1, 0])]
+        vector += both(fuse, 1) + [unit(gain_z1, 2), (gate_x, 2, 1, 0)]
+        vector += [(quant_x, 2, 1, 0), unit(quant_u, 2), (quant_w, W2[1, 1])]
+        vector += [unit(gain_z1, 3), (gate_x, 2, 1, 1), (gate_x, 3, 0, 0)]
+        vector += [unit(quant_u, 3), (quant_x, 2, 1, 1), (quant_w, WF[1])]
+        vector += [(gate_x, 3, 0, 1), (gate_x, 3, 1, 0)] + both(fuse, 2)
+        vector += quants(3, 0) + [(quant_x, 3, 1, 0), unit(quant_u, 4)]
+        vector += both(fuse, 3) + [(gate_x, 3, 1, 1)] + both(fuse, 4)
+        vector += [(quant_x, 3, 1, 1), unit(merge, 3), unit(quant_u, 5), unit(gain_z1, 7)] + both(fuse, 5)
+        vector += [unit(quant_u, 6), unit(quant_u, 7), unit(merge, 4), unit(merge, 5)] + both(fuse, 6) + both(fuse, 7)
+        vector += [unit(copy_vector, 6, 1), unit(copy_vector, 7, 1)]
 
-        pool = [(group_pool, piece) for piece in POOLED]
+        scalar = widened(0, 0) + [(group_scalar, W2[0, 0], 0)] + widened(0, 1) + [(group_scalar, W2[0, 0], 1)] + widened(1, 0)
+        scalar += [(widen_r,), (take_w, W2[0, 1])] + grouped(WF[0]) + [unit(relu_z1, 0), (take_w, W1[1, 0]), (widen_a,)]
+        scalar += [(widen_w2, 1, 1, 0), unit(relu_z2, 0), unit(weigh_o1, 0), unit(relu_z1, 1), unit(relu_z2, 1), (widen_w2, 1, 1, 1)]
+        scalar += [unit(copy_scalar, 0, 0), unit(weigh_o1, 1), unit(copy_scalar, 0, 1), unit(relu_z1, 2), unit(copy_scalar, 1, 0), unit(weigh_o1, 2)]
+        scalar += [unit(copy_scalar, 1, 1), unit(relu_z1_wide, 4), unit(relu_z1, 3), unit(relu_z2, 2), unit(relu_z2, 3)]
+        scalar += [unit(relu_z1_wide, 5), unit(relu_z2, 4), unit(relu_z2, 5), unit(copy_scalar, 2, 0), unit(copy_scalar, 2, 1), unit(relu_z1_wide, 6), unit(weigh_o1, 6)]
+        scalar += [unit(relu_z2, 6), unit(relu_z1, 7)] + both(copy_scalar, 3) + [unit(relu_z2, 7), unit(weigh_o1, 7)] + both(copy_scalar, 4)
+        scalar += both(copy_scalar, 5) + [unit(copy_scalar, 6, 0), unit(copy_scalar, 7, 0)]
 
-        gated_in = {2: (2, 0), 3: (2, 1), 4: (3, 0), 5: (3, 1)}
-        for k, cg in gated_in.items():
-            next_x = [(turn_x, *gated_in[k + 1])] if k + 1 in gated_in else []
-            gates = [(gate_x, *cg, 0), (gate_x, *cg, 1)]
-            if k == 2:
-                tensor += [unit(mul_z2, 1), unit(mul_z1, 2), unit(mul_f, 1)] + both(turn_out, 0) + next_x
-                vector += [unit(gain_z1, 2), (quant_x, *cg, 1), (quant_w, W2[1, 0]), unit(quant_u, 2)]
-                vector += [(quant_w, W2[1, 1])] + both(fuse, 1)
-                scalar += [(take_w, W2[1, 0])]
-            elif k == 3:
-                tensor += [unit(mul_z2, 2), unit(turn_out, 1, 0), unit(mul_z1, 3), unit(turn_out, 1, 1)]
-                tensor += next_x + [unit(mul_f, 2)]
-                vector += gates + [(quant_w, WF[1]), (quant_x, *cg, 0), unit(gain_z1, 3), (quant_x, *cg, 1)]
-                vector += [unit(fuse, 2, 0), unit(quant_u, 3), unit(fuse, 2, 1)]
-            else:
-                tensor += [unit(mul_z2, k - 1), unit(turn_out, k - 2, 0), unit(mul_z1, k), unit(mul_f, k - 1)]
-                tensor += [unit(turn_out, k - 2, 1)] + next_x
-                vector += gates + [(quant_x, *cg, 0), (quant_x, *cg, 1), unit(gain_z1, k)]
-                vector += [unit(fuse, k - 1, 0), unit(quant_u, k), unit(fuse, k - 1, 1)]
-            scalar += [unit(relu_z2, k - 1), unit(store_scalar, k - 2, 0), unit(weigh_o1, k - 1)]
-            scalar += [unit(relu_z1, k), unit(store_scalar, k - 2, 1)]
-
-        k4, k5, k6, k7 = range(LAST - 3, LAST + 1)
-        tensor += [unit(mul_z2, k5), unit(mul_z1, k6), unit(mul_f, k5), unit(turn_out, k4, 0), unit(mul_z1, k7)]
-        tensor += [unit(mul_z2, k6), unit(turn_out, k4, 1), unit(mul_f, k6), unit(mul_z2, k7), unit(turn_out, k5, 0)]
-        tensor += [unit(mul_f, k7), unit(turn_out, k5, 1)] + both(turn_out, k6)
-        tensor += [unit(open_out, k7)] + both(close_out, k7)
-        vector += [unit(gain_z1, k6), unit(fuse, k5, 0), unit(quant_u, k6), unit(fuse, k5, 1), unit(gain_z1, k7)]
-        vector += [unit(merge, k5), unit(quant_u, k7)] + both(fuse, k6) + [unit(merge, k6)] + both(fuse, k7)
-        vector += [unit(store_vector, k6, 1), unit(store_vector, k7, 1)]
-        scalar += [unit(relu_z2, k5), unit(relu_z1, k6), unit(store_scalar, k4, 0), unit(relu_z1, k7)]
-        scalar += [unit(relu_z2, k6), unit(store_scalar, k4, 1), unit(relu_z2, k7), unit(weigh_o1, k7)]
-        scalar += both(store_scalar, k5) + [unit(store_scalar, k6, 0), unit(store_scalar, k7, 0)]
+        pool = [(group_pool, piece) for piece in POOLED] + [unit(gain_pool, k) for k in POOL_GAINED]
 
         def needs(fn, *args):
             if fn in (turn_x, widen_w2, widen_r, widen_a):
@@ -434,22 +473,29 @@ def tile_finalmlptwostreamfusion_kernel(tc, x, s, w1, w2_bytes, w2_scale, r, wf,
             if fn is quant_x:
                 return [(gate_x, *args)]
             if fn in (mix_w, group_scalar, group_pool):
-                return [(widen_w2, *args[0][1:])] if args[0][0] == "w2" else []
+                return [(widen_w2, *args[0][1:], 1)] if args[0][0] == "w2" else []
             if fn is take_w:
                 return [(mix_w, *args)]
             if fn is quant_w:
-                return [(take_w if args[0] in MIXED else group_pool if args[0] in POOLED else group_scalar, *args)]
+                if args[0] in MIXED or args[0] in POOLED:
+                    return [(take_w if args[0] in MIXED else group_pool, *args)]
+                return [(group_scalar, *args, 1)]
             c, h = args[:2]
-            if fn is mul_z1:
+            k = UNITS.index((c, h))
+            if fn in (mul_z1, mul_z1_wide):
                 return [(quant_w, W1[h, g]) for g in range(PASSES)] + [(quant_x, c, g, 0) for g in range(PASSES)]
             if fn is mul_z2:
                 return [(quant_w, W2[h, g]) for g in range(PASSES)] + [(quant_x, c, g, 1) for g in range(PASSES)]
             if fn is gain_z1:
-                return [(mul_z1, c, h), (widen_r,)]
+                return [(mul_z1, c, h, 1), (widen_r,)]
+            if fn is relu_z1_wide:
+                return [(mul_z1_wide, c, h)]
+            if fn is gain_pool:
+                return [(relu_z1_wide, c, h)]
             if fn in (relu_z1, quant_u):
-                return [(gain_z1, c, h)]
+                return [(gain_pool if k in POOL_GAINED else gain_z1, c, h)]
             if fn is weigh_o1:
-                return [(relu_z1, c, h), (widen_a,)]
+                return [(relu_z1_wide if k in POOL_GAINED else relu_z1, c, h), (widen_a,)]
             if fn is relu_z2:
                 return [(mul_z2, c, h)]
             if fn is mul_f:
@@ -457,21 +503,32 @@ def tile_finalmlptwostreamfusion_kernel(tc, x, s, w1, w2_bytes, w2_scale, r, wf,
             if fn is fuse:
                 return [(mul_f, c, h), (relu_z2, c, h), (widen_a,)]
             if fn is merge:
-                return [(fuse, c, h, 1), (relu_z1, c, h)]
+                return [(fuse, c, h, 1), (relu_z1_wide if k in POOL_GAINED else relu_z1, c, h)]
             if fn is turn_out:
                 return [(merge, c, h)] if UNITS.index((c, h)) in MERGED else [(fuse, c, h, 1), (weigh_o1, c, h)]
             if fn is open_out:
                 return [(weigh_o1, c, h)]
             if fn is close_out:
                 return [(fuse, *args), (open_out, c, h)]
+            if fn is store:
+                return [(copy_vector if (copy_vector, *args) in by_vector else copy_scalar, *args)]
             return [(close_out, c, h, 1)] if (c, h) == UNITS[LAST] else [(turn_out, *args)]
 
+        def waits(stage):
+            if stage in chain[1:]:
+                before = chain[chain.index(stage) - 1]
+                return [(quant_w if before[0] is group_pool else quant_u, *before[1:])]
+            return []
+
+        chain = pool[1:]
+        by_vector = [stage for stage in vector if stage[0] is copy_vector]
+        sync = [stage for k in range(LAST + 1) for stage in both(store, k)]
         done = set()
-        programs = [tensor, vector, scalar, pool]
+        programs = [tensor, vector, scalar, pool, sync]
         while any(programs):
             before = len(done)
             for program in programs:
-                while program and all(stage in done for stage in needs(*program[0])):
+                while program and all(stage in done for stage in needs(*program[0]) + waits(program[0])):
                     stage = program.pop(0)
                     stage[0](*stage[1:])
                     done.add(stage)

@@ -25,9 +25,10 @@ M = P // 2
 
 UNITS = [(0, 0), (1, 0), (0, 1), (1, 1), (2, 0), (2, 1), (3, 0), (3, 1)]
 LAST = len(UNITS) - 1
-MERGED = (3, 4, 5)
+MERGED = (3, 4)
+OPENED = (6, 7)
 
-XG_BUFS, WIDE_BUFS, WG_BUFS, UG_BUFS, O_BUFS, FUSED_BUFS, ROW_BUFS = 9, 3, 4, 3, 5, 4, 6
+XG_BUFS, WIDE_BUFS, WG_BUFS, UG_BUFS, O_BUFS, FUSED_BUFS, ROW_BUFS = 8, 3, 4, 2, 5, 4, 6
 
 
 def tile_finalmlptwostreamfusion_kernel(tc, x, s, w1, w2_bytes, w2_scale, r, wf, a, out):
@@ -46,22 +47,36 @@ def tile_finalmlptwostreamfusion_kernel(tc, x, s, w1, w2_bytes, w2_scale, r, wf,
         ws = keep.tile([P, PASSES, 4], F32, name="ws")
         r_bf = keep.tile([P, HEADS, 8], BF16, name="r_bf")
         a_bf = keep.tile([P, 2 * HEADS, 8], BF16, name="a_bf")
-        x_first = {}
         x_raw = {}
+        x_part = {}
         w2_raw = {}
         rows4 = {}
 
         def load_x_first():
             for i in range(TT):
-                x_first[i] = keep.tile([P, KP], BF16, name="x_first%d" % i)
-                nc.sync.dma_start(out=x_first[i][:], in_=x[i * P : (i + 1) * P, 0:KP])
+                x_raw[0, i] = keep.tile([P, D], BF16, name="x_first%d" % i)
+                nc.sync.dma_start(out=x_raw[0, i][:], in_=x[i * P : (i + 1) * P, :])
+                for g in range(PASSES):
+                    x_part[0, i, g] = x_raw[0, i][:, g * KP : (g + 1) * KP]
 
-        def load_x(c, g):
-            x_raw[c, g] = keep.tile([P, TT, KP], BF16, name="x_raw%d_%d" % (c, g))
+        def load_x(c):
+            rows_c = keep.tile([P, TT * D], BF16, name="x_raw%d" % c)
             nc.sync.dma_start(
-                out=x_raw[c, g][:],
+                out=rows_c[:].rearrange("p (i k) -> p i k", i=TT),
+                in_=x[c * TB : (c + 1) * TB, :].rearrange("(i p) k -> p i k", p=P),
+            )
+            for i in range(TT):
+                for g in range(PASSES):
+                    x_part[c, i, g] = rows_c[:, i * D + g * KP : i * D + (g + 1) * KP]
+
+        def load_x_pass(c, g):
+            rows_cg = keep.tile([P, TT * KP], BF16, name="x_raw%d_%d" % (c, g))
+            nc.sync.dma_start(
+                out=rows_cg[:].rearrange("p (i k) -> p i k", i=TT),
                 in_=x[c * TB : (c + 1) * TB, g * KP : (g + 1) * KP].rearrange("(i p) k -> p i k", p=P),
             )
+            for i in range(TT):
+                x_part[c, i, g] = rows_cg[:, i * KP : (i + 1) * KP]
 
         def load_w1(h, g):
             rows4["w1", h, g] = keep.tile([P, 4, W], BF16, name="w1_raw%d_%d" % (h, g))
@@ -77,12 +92,6 @@ def tile_finalmlptwostreamfusion_kernel(tc, x, s, w1, w2_bytes, w2_scale, r, wf,
                 in_=w2_bytes[g * KP : (g + 1) * KP, h * W : (h + 1) * W].rearrange("(p j) n -> p j n", j=4),
             )
 
-        def load_w2_wide(g):
-            raw = keep.tile([P, 4, H], U8, name="w2_wide%d" % g)
-            nc.sync.dma_start(out=raw[:], in_=w2_bytes[g * KP : (g + 1) * KP, :].rearrange("(p j) n -> p j n", j=4))
-            for h in range(HEADS):
-                w2_raw[h, g] = raw[:, :, h * W : (h + 1) * W]
-
         def load_wf(h):
             rows4["wf", h, 0] = keep.tile([P, 4, W], BF16, name="wf_raw%d" % h)
             rows = wf[h].rearrange("(m t e) n -> e m t n", t=4, e=2)
@@ -97,24 +106,22 @@ def tile_finalmlptwostreamfusion_kernel(tc, x, s, w1, w2_bytes, w2_scale, r, wf,
         load_x_first()
         nc.scalar.dma_start(out=ws[:], in_=w2_scale.rearrange("(g p t) o -> p g (t o)", p=P, t=4))
         load_w2(0, 0)
-        load_x(0, 1)
         load_w1(0, 0)
-        load_x(1, 0)
+        load_x_pass(1, 0)
         load_w2(0, 1)
         load_w1(0, 1)
-        load_x(1, 1)
+        load_x_pass(1, 1)
         load_w2(1, 0)
-        load_w1(1, 1)
-        load_x(2, 0)
-        load_channels(r_bf, r.rearrange("(h m c) -> m h c", h=HEADS, c=8))
+        load_x_pass(2, 0)
         load_wf(0)
+        load_w1(1, 1)
+        load_channels(r_bf, r.rearrange("(h m c) -> m h c", h=HEADS, c=8))
         load_w1(1, 0)
         load_w2(1, 1)
         load_channels(a_bf, a.rearrange("k (h m c) -> m (k h) c", h=HEADS, c=8))
-        load_x(2, 1)
+        load_x_pass(2, 1)
         load_wf(1)
-        load_x(3, 0)
-        load_x(3, 1)
+        load_x(3)
 
         sig = keep.tile([P, 2 * PASSES, 4], F32, name="sig")
         nc.scalar.activation(out=sig[:], in_=s_bf[:], func=ACT.Sigmoid)
@@ -158,13 +165,13 @@ def tile_finalmlptwostreamfusion_kernel(tc, x, s, w1, w2_bytes, w2_scale, r, wf,
                 for i in range(TT):
                     bank = psum.tile([P, 2, P], F32, name="bank")
                     for u in range(2):
-                        nc.tensor.transpose(bank[:, u, :], x_first[i][:].bitcast(F32)[:, u::2], ident[:])
+                        nc.tensor.transpose(bank[:, u, :], x_part[c, i, g].bitcast(F32)[:, u::2], ident[:])
                     xt[c, g].append((i * P, P, bank))
                 return
             bank = psum.tile([P, 2, TB], F32, name="bank")
             for u in range(2):
                 for i in range(TT):
-                    words = x_raw[c, g][:, i, :].bitcast(F32)
+                    words = x_part[c, i, g].bitcast(F32)
                     nc.tensor.transpose(bank[:, u, i * P : (i + 1) * P], words[:, u::2], ident[:])
             xt[c, g] = [(0, TB, bank)]
 
@@ -198,31 +205,36 @@ def tile_finalmlptwostreamfusion_kernel(tc, x, s, w1, w2_bytes, w2_scale, r, wf,
                     scale=ws[:, g, j : j + 1],
                 )
 
-        def mix_w(piece):
-            for half in range(2):
-                bank = psum.tile([P, 2, P, 4], BF16, name="bank")
-                for v in range(2):
-                    n0 = (2 * half + v) * P
-                    dst = bank[:, v, :, :].rearrange("p n j -> p j n")
-                    nc.tensor.matmul(dst, lhsT=ident_bf[:], rhs=rows4[piece][:, :, n0 : n0 + P], start=True, stop=True)
-                mixed[piece, half] = bank
+        def mix_w(piece, half):
+            bank = psum.tile([P, 2, P, 4], BF16, name="bank")
+            for v in range(2):
+                n0 = (2 * half + v) * P
+                dst = bank[:, v, :, :].rearrange("p n j -> p j n")
+                nc.tensor.matmul(dst, lhsT=ident_bf[:], rhs=rows4[piece][:, :, n0 : n0 + P], start=True, stop=True)
+            mixed[piece, half] = bank
 
-        def take_w(piece):
-            wg[piece] = work.tile([P, 4 * W], BF16, name="wg", bufs=WG_BUFS, align_bytes=64)
-            dst = wg[piece][:].bitcast(F32).rearrange("p (t m v) -> p t m v", t=4, v=4)
-            for half in range(2):
-                src = mixed[piece, half][:].rearrange("p a n j -> p (a n j)").bitcast(F32)
-                nc.scalar.copy(
-                    out=dst[:, :, half * M // 2 : (half + 1) * M // 2, :],
-                    in_=src.rearrange("p (m t v) -> p t m v", t=4, v=4),
-                )
+        def warm_up(count):
+            bank = psum.tile([P, W], F32, name="bank")
+            for n in range(count):
+                nc.tensor.matmul(bank[:], lhsT=ident_bf[:], rhs=x_part[0, 0, 0], start=True, stop=True)
+
+        def staged(piece):
+            if piece not in wg:
+                wg[piece] = work.tile([P, 4 * W], BF16, name="wg", bufs=WG_BUFS, align_bytes=64)
+            return wg[piece][:]
+
+        def take_w(piece, half):
+            dst = staged(piece).bitcast(F32).rearrange("p (t m v) -> p t m v", t=4, v=4)
+            src = mixed[piece, half][:].rearrange("p a n j -> p (a n j)").bitcast(F32)
+            nc.scalar.copy(
+                out=dst[:, :, half * M // 2 : (half + 1) * M // 2, :],
+                in_=src.rearrange("p (m t v) -> p t m v", t=4, v=4),
+            )
 
         def group_scalar(piece, half):
-            if half == 0:
-                wg[piece] = work.tile([P, 4 * W], BF16, name="wg", bufs=WG_BUFS, align_bytes=64)
             pairs = slice(half * M // 2, (half + 1) * M // 2)
             nc.scalar.copy(
-                out=wg[piece][:].rearrange("p (t m e j) -> p m t j e", t=4, e=2, j=4)[:, pairs],
+                out=staged(piece).rearrange("p (t m e j) -> p m t j e", t=4, e=2, j=4)[:, pairs],
                 in_=rows4[piece][:].rearrange("p j (m t e) -> p m t j e", e=2, t=4)[:, pairs],
             )
 
@@ -295,10 +307,22 @@ def tile_finalmlptwostreamfusion_kernel(tc, x, s, w1, w2_bytes, w2_scale, r, wf,
         def weigh_o1(c, h):
             weighed[c, h] = o1[c, h]
             if UNITS.index((c, h)) in POOL_GAINED:
-                weighed[c, h] = work.tile([P, 4, TB], F32, name="weighed", bufs=1)
+                weighed[c, h] = work.tile([P, 4, TB], F32, name="weighed", bufs=2)
             for t in range(4):
                 nc.scalar.activation(
                     out=weighed[c, h][:, t, :], in_=o1[c, h][:, t, :], func=ACT.Copy, scale=a_f[:, h, t : t + 1]
+                )
+
+        def weigh_z1(c, h):
+            weighed[c, h] = work.tile([P, 4, TB], F32, name="o1", bufs=O_BUFS)
+            for i in range(TT):
+                nc.vector.scalar_tensor_tensor(
+                    out=weighed[c, h][:, :, i * P : (i + 1) * P],
+                    in0=z1[c, h, i][:],
+                    scalar=0.0,
+                    in1=a_f[:, h, :].unsqueeze(2).to_broadcast([P, 4, P]),
+                    op0=ALU.max,
+                    op1=ALU.mult,
                 )
 
         def quant_u(c, h):
@@ -342,6 +366,20 @@ def tile_finalmlptwostreamfusion_kernel(tc, x, s, w1, w2_bytes, w2_scale, r, wf,
                     op1=ALU.mult,
                 )
 
+        def fuse_rows(c, h, i):
+            if i == 0:
+                fused[c, h] = work.tile([P, 4, TB], F32, name="fused", bufs=FUSED_BUFS)
+            tokens = slice(i * P, (i + 1) * P)
+            for t in range(4):
+                nc.vector.scalar_tensor_tensor(
+                    out=fused[c, h][:, t, tokens],
+                    in0=fb[c, h, t // 2][:, t % 2, tokens],
+                    scalar=a_f[:, HEADS + h, t : t + 1],
+                    in1=o2[c, h][:, t, tokens],
+                    op0=ALU.add,
+                    op1=ALU.mult,
+                )
+
         def merge(c, h):
             for t in range(4):
                 nc.vector.scalar_tensor_tensor(
@@ -378,10 +416,9 @@ def tile_finalmlptwostreamfusion_kernel(tc, x, s, w1, w2_bytes, w2_scale, r, wf,
                 for t in range(4):
                     turn_tile(weighed, c, h, i, t, t == 0, False)
 
-        def close_out(c, h, pair):
-            for t in (2 * pair, 2 * pair + 1):
-                for i in range(TT):
-                    turn_tile(fused, c, h, i, t, False, t == 3)
+        def close_out(c, h, i):
+            for t in range(4):
+                turn_tile(fused, c, h, i, t, False, t == 3)
 
         rows = {}
 
@@ -415,25 +452,29 @@ def tile_finalmlptwostreamfusion_kernel(tc, x, s, w1, w2_bytes, w2_scale, r, wf,
         def quants(c, g):
             return [(quant_x, c, g, 0), (quant_x, c, g, 1)]
 
-        def grouped(piece):
-            return [(group_scalar, piece, 0), (group_scalar, piece, 1)]
-
         def widened(h, g):
             return [(widen_w2, h, g, 0), (widen_w2, h, g, 1)]
 
-        MIXED = (W2[0, 1], W1[1, 0])
+        def mixes(piece):
+            return [(mix_w, piece, 0), (mix_w, piece, 1)]
+
+        def taken(piece):
+            return [(take_w, piece, 0), (take_w, piece, 1)]
+
+        MIXED = [(piece, half) for piece in (W2[0, 0], W2[0, 1], WF[0]) for half in range(2)]
         POOLED = (W1[0, 0], W1[0, 1], W1[1, 1], W2[1, 0], W2[1, 1], WF[1])
         POOL_GAINED = (4, 5, 6)
+        VECTOR_WEIGHED = (7,)
+        BY_ROWS = (6, 7)
 
-        tensor = [(turn_x, c, g) for c in range(2) for g in range(PASSES)]
-        tensor += [(mix_w, W2[0, 1]), (turn_x, 2, 0)] + both(mul_z1, 0) + [(mix_w, W1[1, 0])] + both(mul_z1, 1)
-        tensor += [unit(mul_z2, 0), unit(mul_f, 0), unit(mul_z2, 1)] + both(mul_z1, 2) + [(turn_x, 2, 1), unit(turn_out, 0, 0)]
-        tensor += [unit(mul_f, 1), unit(turn_out, 0, 1), unit(mul_z1, 3, 0), (turn_x, 3, 0), unit(turn_out, 1, 0), unit(mul_z1, 3, 1), unit(turn_out, 1, 1)]
-        tensor += [unit(mul_z1_wide, 4), unit(mul_z2, 2), unit(mul_z2, 3), (turn_x, 3, 1), unit(mul_z1_wide, 5), unit(mul_f, 2), unit(mul_z2, 4), unit(mul_f, 3)]
-        tensor += [unit(mul_z2, 5)] + both(turn_out, 2) + [unit(mul_f, 4), unit(mul_z1_wide, 6)]
-        tensor += both(mul_z1, 7) + [unit(mul_z2, 6), unit(mul_f, 5)] + both(turn_out, 3) + [unit(mul_z2, 7), unit(mul_f, 6), unit(mul_f, 7)]
-        tensor += both(turn_out, 4) + both(turn_out, 5) + [unit(open_out, 7)] + both(turn_out, 6)
-        tensor += both(close_out, 7)
+        tensor = [(turn_x, 0, 0), (turn_x, 0, 1), (warm_up, 3), (turn_x, 1, 0)] + mixes(W2[0, 0]) + [(turn_x, 1, 1)] + mixes(W2[0, 1])
+        tensor += [(turn_x, 2, 0), (mix_w, WF[0], 0)] + both(mul_z1, 0) + [(mix_w, WF[0], 1)] + both(mul_z1, 1)
+        tensor += [unit(mul_z2, 0), unit(mul_f, 0), (turn_x, 2, 1), unit(mul_z2, 1)] + both(mul_z1, 2) + both(turn_out, 0)
+        tensor += [unit(mul_f, 1), unit(mul_z1_wide, 4)] + both(mul_z1, 3) + both(turn_out, 1) + [(turn_x, 3, 0)]
+        tensor += [unit(mul_z2, 2), unit(mul_z2, 3), (turn_x, 3, 1), unit(mul_z1_wide, 5), unit(mul_f, 2), unit(mul_z2, 4), unit(mul_f, 3)]
+        tensor += [unit(mul_z2, 5)] + both(turn_out, 2) + [unit(mul_f, 4), unit(mul_z1_wide, 6)] + both(mul_z1, 7) + [unit(mul_z2, 6)]
+        tensor += both(turn_out, 3) + [unit(mul_z2, 7), unit(mul_f, 5)] + both(turn_out, 4) + both(turn_out, 5) + [unit(mul_f, 6), unit(mul_f, 7)]
+        tensor += [unit(open_out, 6)] + both(close_out, 6) + [unit(open_out, 7)] + both(close_out, 7)
 
         first_gates = [(gate_x, c, g, stream) for c in range(2) for g in range(PASSES) for stream in range(2)]
         vector = first_gates[:-1]
@@ -441,32 +482,32 @@ def tile_finalmlptwostreamfusion_kernel(tc, x, s, w1, w2_bytes, w2_scale, r, wf,
         vector += [first_gates[-1], (gate_x, 2, 0, 0), unit(gain_z1, 0)]
         vector += [(quant_x, 1, 0, 0), (quant_x, 1, 1, 0), (quant_w, W2[0, 0]), (quant_x, 0, 0, 1), (quant_x, 0, 1, 1), (quant_w, W2[0, 1])]
         vector += [unit(quant_u, 0), (quant_w, WF[0]), (quant_x, 1, 0, 1), (quant_x, 1, 1, 1), (quant_w, W1[1, 0]), (quant_w, W1[1, 1])]
-        vector += [unit(gain_z1, 1)] + both(fuse, 0) + [(gate_x, 2, 0, 1)]
-        vector += [unit(quant_u, 1)] + quants(2, 0) + [(quant_w, W2[1, 0])]
-        vector += both(fuse, 1) + [unit(gain_z1, 2), (gate_x, 2, 1, 0)]
-        vector += [(quant_x, 2, 1, 0), unit(quant_u, 2), (quant_w, W2[1, 1])]
+        vector += both(fuse, 0) + [unit(gain_z1, 1), (gate_x, 2, 1, 0)]
+        vector += [unit(quant_u, 1), (quant_x, 2, 0, 0), (quant_x, 2, 1, 0), (quant_w, W2[1, 0])]
+        vector += both(fuse, 1) + [unit(gain_z1, 2), (gate_x, 2, 0, 1)]
+        vector += [unit(quant_u, 2), (quant_x, 2, 0, 1), (quant_w, W2[1, 1])]
         vector += [unit(gain_z1, 3), (gate_x, 2, 1, 1), (gate_x, 3, 0, 0)]
         vector += [unit(quant_u, 3), (quant_x, 2, 1, 1), (quant_w, WF[1])]
         vector += [(gate_x, 3, 0, 1), (gate_x, 3, 1, 0)] + both(fuse, 2)
         vector += quants(3, 0) + [(quant_x, 3, 1, 0), unit(quant_u, 4)]
         vector += both(fuse, 3) + [(gate_x, 3, 1, 1)] + both(fuse, 4)
-        vector += [(quant_x, 3, 1, 1), unit(merge, 3), unit(quant_u, 5), unit(gain_z1, 7)] + both(fuse, 5)
-        vector += [unit(quant_u, 6), unit(quant_u, 7), unit(merge, 4), unit(merge, 5)] + both(fuse, 6) + both(fuse, 7)
-        vector += [unit(copy_vector, 6, 1), unit(copy_vector, 7, 1)]
+        vector += [(quant_x, 3, 1, 1), unit(merge, 3), unit(merge, 4), unit(quant_u, 5), unit(gain_z1, 7)] + both(fuse, 5)
+        vector += [unit(quant_u, 6), unit(quant_u, 7), unit(weigh_z1, 7)] + both(fuse_rows, 6) + both(fuse_rows, 7)
+        vector += [unit(copy_vector, 7, 1)]
 
-        scalar = widened(0, 0) + [(group_scalar, W2[0, 0], 0)] + widened(0, 1) + [(group_scalar, W2[0, 0], 1)] + widened(1, 0)
-        scalar += [(widen_r,), (take_w, W2[0, 1])] + grouped(WF[0]) + [unit(relu_z1, 0), (take_w, W1[1, 0]), (widen_a,)]
-        scalar += [(widen_w2, 1, 1, 0), unit(relu_z2, 0), unit(weigh_o1, 0), unit(relu_z1, 1), unit(relu_z2, 1), (widen_w2, 1, 1, 1)]
-        scalar += [unit(copy_scalar, 0, 0), unit(weigh_o1, 1), unit(copy_scalar, 0, 1), unit(relu_z1, 2), unit(copy_scalar, 1, 0), unit(weigh_o1, 2)]
-        scalar += [unit(copy_scalar, 1, 1), unit(relu_z1_wide, 4), unit(relu_z1, 3), unit(relu_z2, 2), unit(relu_z2, 3)]
-        scalar += [unit(relu_z1_wide, 5), unit(relu_z2, 4), unit(relu_z2, 5), unit(copy_scalar, 2, 0), unit(copy_scalar, 2, 1), unit(relu_z1_wide, 6), unit(weigh_o1, 6)]
-        scalar += [unit(relu_z2, 6), unit(relu_z1, 7)] + both(copy_scalar, 3) + [unit(relu_z2, 7), unit(weigh_o1, 7)] + both(copy_scalar, 4)
-        scalar += both(copy_scalar, 5) + [unit(copy_scalar, 6, 0), unit(copy_scalar, 7, 0)]
+        scalar = widened(0, 0) + widened(0, 1) + taken(W2[0, 0]) + widened(1, 0) + taken(W2[0, 1]) + [(widen_r,), (take_w, WF[0], 0)]
+        scalar += [(group_scalar, W1[1, 0], 0), (take_w, WF[0], 1), unit(relu_z1, 0), (group_scalar, W1[1, 0], 1), (widen_a,)]
+        scalar += [unit(relu_z2, 0), (widen_w2, 1, 1, 0), unit(weigh_o1, 0), unit(relu_z2, 1), unit(relu_z1, 1), (widen_w2, 1, 1, 1)]
+        scalar += both(copy_scalar, 0) + [unit(weigh_o1, 1), unit(relu_z1, 2), unit(relu_z1_wide, 4)] + both(copy_scalar, 1)
+        scalar += [unit(weigh_o1, 2), unit(relu_z1, 3), unit(relu_z2, 2), unit(relu_z2, 3)]
+        scalar += [unit(relu_z1_wide, 5), unit(relu_z2, 4), unit(weigh_o1, 5), unit(relu_z2, 5)] + both(copy_scalar, 2) + [unit(relu_z1_wide, 6)]
+        scalar += [unit(weigh_o1, 6), unit(relu_z2, 6)] + both(copy_scalar, 3) + [unit(relu_z2, 7)] + both(copy_scalar, 4)
+        scalar += both(copy_scalar, 5) + both(copy_scalar, 6) + [unit(copy_scalar, 7, 0)]
 
         pool = [(group_pool, piece) for piece in POOLED] + [unit(gain_pool, k) for k in POOL_GAINED]
 
         def needs(fn, *args):
-            if fn in (turn_x, widen_w2, widen_r, widen_a):
+            if fn in (turn_x, warm_up, widen_w2, widen_r, widen_a):
                 return []
             if fn is gate_x:
                 return [(turn_x, *args[:2])]
@@ -477,9 +518,9 @@ def tile_finalmlptwostreamfusion_kernel(tc, x, s, w1, w2_bytes, w2_scale, r, wf,
             if fn is take_w:
                 return [(mix_w, *args)]
             if fn is quant_w:
-                if args[0] in MIXED or args[0] in POOLED:
-                    return [(take_w if args[0] in MIXED else group_pool, *args)]
-                return [(group_scalar, *args, 1)]
+                if args[0] in POOLED:
+                    return [(group_pool, *args)]
+                return [(take_w if (*args, half) in MIXED else group_scalar, *args, half) for half in range(2)]
             c, h = args[:2]
             k = UNITS.index((c, h))
             if fn in (mul_z1, mul_z1_wide):
@@ -488,6 +529,9 @@ def tile_finalmlptwostreamfusion_kernel(tc, x, s, w1, w2_bytes, w2_scale, r, wf,
                 return [(quant_w, W2[h, g]) for g in range(PASSES)] + [(quant_x, c, g, 1) for g in range(PASSES)]
             if fn is gain_z1:
                 return [(mul_z1, c, h, 1), (widen_r,)]
+            weigh = weigh_z1 if k in VECTOR_WEIGHED else weigh_o1
+            if fn is weigh_z1:
+                return [(gain_z1, c, h), (widen_a,)]
             if fn is relu_z1_wide:
                 return [(mul_z1_wide, c, h)]
             if fn is gain_pool:
@@ -500,19 +544,19 @@ def tile_finalmlptwostreamfusion_kernel(tc, x, s, w1, w2_bytes, w2_scale, r, wf,
                 return [(mul_z2, c, h)]
             if fn is mul_f:
                 return [(quant_u, c, h), (quant_w, WF[h])]
-            if fn is fuse:
+            if fn in (fuse, fuse_rows):
                 return [(mul_f, c, h), (relu_z2, c, h), (widen_a,)]
             if fn is merge:
                 return [(fuse, c, h, 1), (relu_z1_wide if k in POOL_GAINED else relu_z1, c, h)]
             if fn is turn_out:
-                return [(merge, c, h)] if UNITS.index((c, h)) in MERGED else [(fuse, c, h, 1), (weigh_o1, c, h)]
+                return [(merge, c, h)] if UNITS.index((c, h)) in MERGED else [(fuse_rows, *args) if k in BY_ROWS else (fuse, c, h, 1), (weigh, c, h)]
             if fn is open_out:
-                return [(weigh_o1, c, h)]
+                return [(weigh, c, h)]
             if fn is close_out:
-                return [(fuse, *args), (open_out, c, h)]
+                return [(fuse_rows, *args), (open_out, c, h)]
             if fn is store:
                 return [(copy_vector if (copy_vector, *args) in by_vector else copy_scalar, *args)]
-            return [(close_out, c, h, 1)] if (c, h) == UNITS[LAST] else [(turn_out, *args)]
+            return [(close_out, *args)] if k in OPENED else [(turn_out, *args)]
 
         def waits(stage):
             if stage in chain[1:]:

@@ -213,11 +213,6 @@ def tile_finalmlptwostreamfusion_kernel(tc, x, s, w1, w2_bytes, w2_scale, r, wf,
                 nc.tensor.matmul(dst, lhsT=ident_bf[:], rhs=rows4[piece][:, :, n0 : n0 + P], start=True, stop=True)
             mixed[piece, half] = bank
 
-        def warm_up(count):
-            bank = psum.tile([P, W], F32, name="bank")
-            for n in range(count):
-                nc.tensor.matmul(bank[:], lhsT=ident_bf[:], rhs=x_part[0, 0, 0], start=True, stop=True)
-
         def staged(piece):
             if piece not in wg:
                 wg[piece] = work.tile([P, 4 * W], BF16, name="wg", bufs=WG_BUFS, align_bytes=64)
@@ -467,7 +462,7 @@ def tile_finalmlptwostreamfusion_kernel(tc, x, s, w1, w2_bytes, w2_scale, r, wf,
         VECTOR_WEIGHED = (7,)
         BY_ROWS = (6, 7)
 
-        tensor = [(turn_x, 0, 0), (turn_x, 0, 1), (warm_up, 3), (turn_x, 1, 0)] + mixes(W2[0, 0]) + [(turn_x, 1, 1)] + mixes(W2[0, 1])
+        tensor = [(turn_x, 0, 0), (turn_x, 0, 1), (turn_x, 1, 0)] + mixes(W2[0, 0]) + [(turn_x, 1, 1)] + mixes(W2[0, 1])
         tensor += [(turn_x, 2, 0), (mix_w, WF[0], 0)] + both(mul_z1, 0) + [(mix_w, WF[0], 1)] + both(mul_z1, 1)
         tensor += [unit(mul_z2, 0), unit(mul_f, 0), (turn_x, 2, 1), unit(mul_z2, 1)] + both(mul_z1, 2) + both(turn_out, 0)
         tensor += [unit(mul_f, 1), unit(mul_z1_wide, 4)] + both(mul_z1, 3) + both(turn_out, 1) + [(turn_x, 3, 0)]
@@ -507,7 +502,7 @@ def tile_finalmlptwostreamfusion_kernel(tc, x, s, w1, w2_bytes, w2_scale, r, wf,
         pool = [(group_pool, piece) for piece in POOLED] + [unit(gain_pool, k) for k in POOL_GAINED]
 
         def needs(fn, *args):
-            if fn in (turn_x, warm_up, widen_w2, widen_r, widen_a):
+            if fn in (turn_x, widen_w2, widen_r, widen_a):
                 return []
             if fn is gate_x:
                 return [(turn_x, *args[:2])]

@@ -85,12 +85,11 @@ def tile_finalmlptwostreamfusion_kernel(tc, x, s, w1, w2_bytes, w2_scale, r, wf,
                 in_=w1[g * KP : (g + 1) * KP, h * W : (h + 1) * W].rearrange("(p j) n -> p j n", j=4),
             )
 
-        def load_w2(h, g):
-            w2_raw[h, g] = keep.tile([P, 4, W], U8, name="w2_raw%d_%d" % (h, g))
-            nc.sync.dma_start(
-                out=w2_raw[h, g][:],
-                in_=w2_bytes[g * KP : (g + 1) * KP, h * W : (h + 1) * W].rearrange("(p j) n -> p j n", j=4),
-            )
+        def load_w2(g):
+            raw = keep.tile([P, 4, H], U8, name="w2_raw%d" % g)
+            nc.sync.dma_start(out=raw[:], in_=w2_bytes[g * KP : (g + 1) * KP, :].rearrange("(p j) n -> p j n", j=4))
+            for h in range(HEADS):
+                w2_raw[h, g] = raw[:, :, h * W : (h + 1) * W]
 
         def load_wf(h):
             rows4["wf", h, 0] = keep.tile([P, 4, W], BF16, name="wf_raw%d" % h)
@@ -105,19 +104,17 @@ def tile_finalmlptwostreamfusion_kernel(tc, x, s, w1, w2_bytes, w2_scale, r, wf,
         nc.scalar.dma_start(out=s_bf[:], in_=s.rearrange("k (g p t) -> p (k g) t", p=P, t=4))
         load_x_first()
         nc.scalar.dma_start(out=ws[:], in_=w2_scale.rearrange("(g p t) o -> p g (t o)", p=P, t=4))
-        load_w2(0, 0)
+        load_w2(0)
         load_w1(0, 0)
         load_x_pass(1, 0)
-        load_w2(0, 1)
+        load_w2(1)
         load_w1(0, 1)
         load_x_pass(1, 1)
-        load_w2(1, 0)
         load_x_pass(2, 0)
         load_wf(0)
         load_w1(1, 1)
         load_channels(r_bf, r.rearrange("(h m c) -> m h c", h=HEADS, c=8))
         load_w1(1, 0)
-        load_w2(1, 1)
         load_channels(a_bf, a.rearrange("k (h m c) -> m (k h) c", h=HEADS, c=8))
         load_x_pass(2, 1)
         load_wf(1)
@@ -490,9 +487,9 @@ def tile_finalmlptwostreamfusion_kernel(tc, x, s, w1, w2_bytes, w2_scale, r, wf,
         vector += [unit(quant_u, 6), unit(quant_u, 7), unit(weigh_z1, 7)] + both(fuse_rows, 6) + both(fuse_rows, 7)
         vector += [unit(copy_vector, 7, 1)]
 
-        scalar = widened(0, 0) + widened(0, 1) + taken(W2[0, 0]) + widened(1, 0) + taken(W2[0, 1]) + [(widen_r,), (take_w, WF[0], 0)]
-        scalar += [(group_scalar, W1[1, 0], 0), (take_w, WF[0], 1), unit(relu_z1, 0), (group_scalar, W1[1, 0], 1), (widen_a,)]
-        scalar += [unit(relu_z2, 0), (widen_w2, 1, 1, 0), unit(weigh_o1, 0), unit(relu_z2, 1), unit(relu_z1, 1), (widen_w2, 1, 1, 1)]
+        scalar = widened(0, 0) + [(widen_w2, 1, 0, 0)] + widened(0, 1) + taken(W2[0, 0]) + [(widen_w2, 1, 0, 1), (widen_w2, 1, 1, 0)] + taken(W2[0, 1])
+        scalar += [(widen_r,), (take_w, WF[0], 0), (group_scalar, W1[1, 0], 0), (take_w, WF[0], 1), unit(relu_z1, 0), (group_scalar, W1[1, 0], 1), (widen_a,)]
+        scalar += [unit(relu_z2, 0), (widen_w2, 1, 1, 1), unit(weigh_o1, 0), unit(relu_z2, 1), unit(relu_z1, 1)]
         scalar += both(copy_scalar, 0) + [unit(weigh_o1, 1), unit(relu_z1, 2), unit(relu_z1_wide, 4)] + both(copy_scalar, 1)
         scalar += [unit(weigh_o1, 2), unit(relu_z1, 3), unit(relu_z2, 2), unit(relu_z2, 3)]
         scalar += [unit(relu_z1_wide, 5), unit(relu_z2, 4), unit(weigh_o1, 5), unit(relu_z2, 5)] + both(copy_scalar, 2) + [unit(relu_z1_wide, 6)]

@@ -24,7 +24,7 @@ TT = TB // P
 M = P // 2
 
 UNITS = [(0, 0), (1, 0), (0, 1), (1, 1), (2, 0), (2, 1), (3, 0), (3, 1)]
-LAST = len(UNITS) - 1
+BANKS = 8
 MERGED = (3, 4)
 OPENED = (6, 7)
 
@@ -36,7 +36,22 @@ def tile_finalmlptwostreamfusion_kernel(tc, x, s, w1, w2_bytes, w2_scale, r, wf,
     with ExitStack() as ctx:
         keep = ctx.enter_context(tc.tile_pool(name="keep", bufs=1))
         work = ctx.enter_context(tc.tile_pool(name="work", bufs=1))
-        psum = ctx.enter_context(tc.psum_pool(name="psum", bufs=8))
+        psum = ctx.enter_context(tc.psum_pool(name="psum", bufs=1))
+        free_banks = list(range(BANKS))
+        held = {}
+
+        def bank_for(key, shape, dtype):
+            held[key] = free_banks.pop(0)
+            return psum.tile(shape, dtype, name="bank%d" % held[key])
+
+        asked = {}
+
+        def buffer(name, shape, dtype, count):
+            asked[name] = asked.get(name, -1) + 1
+            return work.tile(shape, dtype, name="%s%d" % (name, asked[name] % count), bufs=1, align_bytes=64)
+
+        def give_back(key):
+            free_banks.append(held.pop(key))
 
         ident = keep.tile([P, P], F32, name="ident")
         make_identity(nc, ident[:])
@@ -108,8 +123,8 @@ def tile_finalmlptwostreamfusion_kernel(tc, x, s, w1, w2_bytes, w2_scale, r, wf,
         load_w1(0, 0)
         load_x_pass(1, 0)
         load_w2(1)
-        load_w1(0, 1)
         load_x_pass(1, 1)
+        load_w1(0, 1)
         load_x_pass(2, 0)
         load_wf(0)
         load_w1(1, 1)
@@ -154,18 +169,20 @@ def tile_finalmlptwostreamfusion_kernel(tc, x, s, w1, w2_bytes, w2_scale, r, wf,
 
         xt = {}
         xg = {}
+        free_gated = list(range(XG_BUFS))
+        gated_in = {}
         g_q = {}
 
         def turn_x(c, g):
             if (c, g) == (0, 0):
                 xt[c, g] = []
                 for i in range(TT):
-                    bank = psum.tile([P, 2, P], F32, name="bank")
+                    bank = bank_for(("x", c, g, i), [P, 2, P], F32)
                     for u in range(2):
                         nc.tensor.transpose(bank[:, u, :], x_part[c, i, g].bitcast(F32)[:, u::2], ident[:])
                     xt[c, g].append((i * P, P, bank))
                 return
-            bank = psum.tile([P, 2, TB], F32, name="bank")
+            bank = bank_for(("x", c, g, 0), [P, 2, TB], F32)
             for u in range(2):
                 for i in range(TT):
                     words = x_part[c, i, g].bitcast(F32)
@@ -173,7 +190,9 @@ def tile_finalmlptwostreamfusion_kernel(tc, x, s, w1, w2_bytes, w2_scale, r, wf,
             xt[c, g] = [(0, TB, bank)]
 
         def gate_x(c, g, stream):
-            xg[c, g, stream] = work.tile([P, TB, 4], BF16, name="xg", bufs=XG_BUFS, align_bytes=64)
+            gated_in[c, g, stream] = free_gated.pop(0)
+            name = "xg%d" % gated_in[c, g, stream]
+            xg[c, g, stream] = work.tile([P, TB, 4], BF16, name=name, bufs=1, align_bytes=64)
             factor = gate[:, PASSES * stream + g, :].rearrange("p (u e) -> p u e", e=2).unsqueeze(1)
             for n0, n, bank in xt[c, g]:
                 nc.vector.tensor_tensor(
@@ -182,10 +201,13 @@ def tile_finalmlptwostreamfusion_kernel(tc, x, s, w1, w2_bytes, w2_scale, r, wf,
                     in1=factor.to_broadcast([P, n, 2, 2]),
                     op=ALU.mult,
                 )
+                if (c, g, 1 - stream) in xg:
+                    give_back(("x", c, g, n0 // P))
 
         def quant_x(c, g, stream):
             grouped = xg[c, g, stream][:].rearrange("p n j -> p (n j)")
             g_q[c, g, stream] = quantize(grouped, TB, "g%dq%d_%d" % (stream, c, g))
+            free_gated.append(gated_in[c, g, stream])
 
         mixed = {}
         wg = {}
@@ -193,7 +215,7 @@ def tile_finalmlptwostreamfusion_kernel(tc, x, s, w1, w2_bytes, w2_scale, r, wf,
 
         def widen_w2(h, g, half):
             if half == 0:
-                rows4["w2", h, g] = work.tile([P, 4, W], BF16, name="wide", bufs=WIDE_BUFS)
+                rows4["w2", h, g] = buffer("wide", [P, 4, W], BF16, WIDE_BUFS)
             for j in (2 * half, 2 * half + 1):
                 nc.scalar.activation(
                     out=rows4["w2", h, g][:, j, :],
@@ -203,7 +225,7 @@ def tile_finalmlptwostreamfusion_kernel(tc, x, s, w1, w2_bytes, w2_scale, r, wf,
                 )
 
         def mix_w(piece, half):
-            bank = psum.tile([P, 2, P, 4], BF16, name="bank")
+            bank = bank_for(("mix", piece, half), [P, 2, P, 4], BF16)
             for v in range(2):
                 n0 = (2 * half + v) * P
                 dst = bank[:, v, :, :].rearrange("p n j -> p j n")
@@ -212,7 +234,7 @@ def tile_finalmlptwostreamfusion_kernel(tc, x, s, w1, w2_bytes, w2_scale, r, wf,
 
         def staged(piece):
             if piece not in wg:
-                wg[piece] = work.tile([P, 4 * W], BF16, name="wg", bufs=WG_BUFS, align_bytes=64)
+                wg[piece] = buffer("wg", [P, 4 * W], BF16, WG_BUFS)
             return wg[piece][:]
 
         def take_w(piece, half):
@@ -222,6 +244,7 @@ def tile_finalmlptwostreamfusion_kernel(tc, x, s, w1, w2_bytes, w2_scale, r, wf,
                 out=dst[:, :, half * M // 2 : (half + 1) * M // 2, :],
                 in_=src.rearrange("p (m t v) -> p t m v", t=4, v=4),
             )
+            give_back(("mix", piece, half))
 
         def group_scalar(piece, half):
             pairs = slice(half * M // 2, (half + 1) * M // 2)
@@ -233,9 +256,10 @@ def tile_finalmlptwostreamfusion_kernel(tc, x, s, w1, w2_bytes, w2_scale, r, wf,
         def group_pool(piece):
             name = "wg_pool1" if piece == POOLED[0] else "wg_pool0"
             wg[piece] = work.tile([P, 4 * W], BF16, name=name, bufs=1, align_bytes=64)
+            pairs = slice(0, M // 2 if (piece, 1) in MIXED else M)
             nc.gpsimd.tensor_scalar(
-                out=wg[piece][:].rearrange("p (t m e j) -> p m t e j", t=4, e=2, j=4),
-                in0=rows4[piece][:].rearrange("p j (m t e) -> p m t e j", t=4, e=2),
+                out=wg[piece][:].rearrange("p (t m e j) -> p m t e j", t=4, e=2, j=4)[:, pairs],
+                in0=rows4[piece][:].rearrange("p j (m t e) -> p m t e j", t=4, e=2)[:, pairs],
                 scalar1=1.0,
                 scalar2=0.0,
                 op0=ALU.mult,
@@ -251,18 +275,38 @@ def tile_finalmlptwostreamfusion_kernel(tc, x, s, w1, w2_bytes, w2_scale, r, wf,
         u_q = {}
         weighed = {}
 
-        def mul_z1_wide(c, h):
-            for pair in range(2):
-                z1[c, h, pair] = psum.tile([P, 2, TB], F32, name="bank")
-                for v in range(2):
-                    for g in range(PASSES):
-                        dst = z1[c, h, pair][:, v, :]
-                        mx(dst, w_q["w1", h, g], 2 * pair + v, g_q[c, g, 0], 0, TB, g == 0, g == PASSES - 1)
+        def pooled(c, h):
+            return UNITS.index((c, h)) in POOL_GAINED
 
-        def relu_z1_wide(c, h):
-            o1[c, h] = work.tile([P, 4, TB], F32, name="o1", bufs=O_BUFS)
-            for pair in range(2):
-                nc.scalar.activation(out=o1[c, h][:, 2 * pair : 2 * pair + 2, :], in_=z1[c, h, pair][:], func=ACT.Relu)
+        def mul_z1(c, h, n):
+            if pooled(c, h):
+                z1[c, h, n] = bank_for(("z1", c, h, n), [P, 2, TB], F32)
+                parts = [(z1[c, h, n][:, v, :], 2 * n + v, 0, TB) for v in range(2)]
+            else:
+                z1[c, h, n] = bank_for(("z1", c, h, n), [P, 4, P], F32)
+                parts = [(z1[c, h, n][:, t, :], t, n * P, P) for t in range(4)]
+            for dst, t, n0, tokens in parts:
+                for g in range(PASSES):
+                    mx(dst, w_q["w1", h, g], t, g_q[c, g, 0], n0, tokens, g == 0, g == PASSES - 1)
+
+        def gain_z1(c, h, i):
+            if i == 0:
+                ug[c, h] = buffer("ug", [P, TT, P, 4], BF16, UG_BUFS)
+            nc.vector.scalar_tensor_tensor(
+                out=ug[c, h][:, i, :, :],
+                in0=z1[c, h, i][:].rearrange("p t n -> p n t"),
+                scalar=0.0,
+                in1=r_f[:, h, :].unsqueeze(1).to_broadcast([P, P, 4]),
+                op0=ALU.max,
+                op1=ALU.mult,
+            )
+
+        def relu_z1(c, h, n):
+            if n == 0:
+                o1[c, h] = buffer("o1", [P, 4, TB], F32, O_BUFS)
+            dst = o1[c, h][:, 2 * n : 2 * n + 2, :] if pooled(c, h) else o1[c, h][:, :, n * P : (n + 1) * P]
+            nc.scalar.activation(out=dst, in_=z1[c, h, n][:], func=ACT.Relu)
+            give_back(("z1", c, h, n))
 
         def gain_pool(c, h):
             ug[c, h] = work.tile([P, TT, P, 4], BF16, name="wg_pool0", bufs=1, align_bytes=64)
@@ -273,49 +317,27 @@ def tile_finalmlptwostreamfusion_kernel(tc, x, s, w1, w2_bytes, w2_scale, r, wf,
                 op=ALU.mult,
             )
 
-        def mul_z1(c, h, i):
-            z1[c, h, i] = psum.tile([P, 4, P], F32, name="bank")
-            for t in range(4):
-                for g in range(PASSES):
-                    mx(z1[c, h, i][:, t, :], w_q["w1", h, g], t, g_q[c, g, 0], i * P, P, g == 0, g == PASSES - 1)
-
-        def gain_z1(c, h):
-            ug[c, h] = work.tile([P, TT, P, 4], BF16, name="ug", bufs=UG_BUFS, align_bytes=64)
-            for i in range(TT):
-                nc.vector.scalar_tensor_tensor(
-                    out=ug[c, h][:, i, :, :],
-                    in0=z1[c, h, i][:].rearrange("p t n -> p n t"),
-                    scalar=0.0,
-                    in1=r_f[:, h, :].unsqueeze(1).to_broadcast([P, P, 4]),
-                    op0=ALU.max,
-                    op1=ALU.mult,
-                )
-
-        def relu_z1(c, h):
-            o1[c, h] = work.tile([P, 4, TB], F32, name="o1", bufs=O_BUFS)
-            for i in range(TT):
-                nc.scalar.activation(out=o1[c, h][:, :, i * P : (i + 1) * P], in_=z1[c, h, i][:], func=ACT.Relu)
-
         def weigh_o1(c, h):
             weighed[c, h] = o1[c, h]
-            if UNITS.index((c, h)) in POOL_GAINED:
-                weighed[c, h] = work.tile([P, 4, TB], F32, name="weighed", bufs=2)
+            if pooled(c, h):
+                weighed[c, h] = buffer("weighed", [P, 4, TB], F32, 2)
             for t in range(4):
                 nc.scalar.activation(
                     out=weighed[c, h][:, t, :], in_=o1[c, h][:, t, :], func=ACT.Copy, scale=a_f[:, h, t : t + 1]
                 )
 
-        def weigh_z1(c, h):
-            weighed[c, h] = work.tile([P, 4, TB], F32, name="o1", bufs=O_BUFS)
-            for i in range(TT):
-                nc.vector.scalar_tensor_tensor(
-                    out=weighed[c, h][:, :, i * P : (i + 1) * P],
-                    in0=z1[c, h, i][:],
-                    scalar=0.0,
-                    in1=a_f[:, h, :].unsqueeze(2).to_broadcast([P, 4, P]),
-                    op0=ALU.max,
-                    op1=ALU.mult,
-                )
+        def weigh_z1(c, h, i):
+            if i == 0:
+                weighed[c, h] = buffer("o1", [P, 4, TB], F32, O_BUFS)
+            nc.vector.scalar_tensor_tensor(
+                out=weighed[c, h][:, :, i * P : (i + 1) * P],
+                in0=z1[c, h, i][:],
+                scalar=0.0,
+                in1=a_f[:, h, :].unsqueeze(2).to_broadcast([P, 4, P]),
+                op0=ALU.max,
+                op1=ALU.mult,
+            )
+            give_back(("z1", c, h, i))
 
         def quant_u(c, h):
             u_q[c, h] = quantize(ug[c, h][:].rearrange("p i n t -> p (i n t)"), TB, "uq%d_%d" % (c, h))
@@ -325,28 +347,27 @@ def tile_finalmlptwostreamfusion_kernel(tc, x, s, w1, w2_bytes, w2_scale, r, wf,
         fb = {}
         fused = {}
 
-        def mul_z2(c, h):
-            for pair in range(2):
-                z2[c, h, pair] = psum.tile([P, 2, TB], F32, name="bank")
-                for v in range(2):
-                    for g in range(PASSES):
-                        dst = z2[c, h, pair][:, v, :]
-                        mx(dst, w_q["w2", h, g], 2 * pair + v, g_q[c, g, 1], 0, TB, g == 0, g == PASSES - 1)
+        def mul_z2(c, h, pair):
+            z2[c, h, pair] = bank_for(("z2", c, h, pair), [P, 2, TB], F32)
+            for v in range(2):
+                for g in range(PASSES):
+                    dst = z2[c, h, pair][:, v, :]
+                    mx(dst, w_q["w2", h, g], 2 * pair + v, g_q[c, g, 1], 0, TB, g == 0, g == PASSES - 1)
 
-        def relu_z2(c, h):
-            o2[c, h] = work.tile([P, 4, TB], F32, name="o2", bufs=O_BUFS)
-            for pair in range(2):
-                nc.scalar.activation(out=o2[c, h][:, 2 * pair : 2 * pair + 2, :], in_=z2[c, h, pair][:], func=ACT.Relu)
+        def relu_z2(c, h, pair):
+            if pair == 0:
+                o2[c, h] = buffer("o2", [P, 4, TB], F32, O_BUFS)
+            nc.scalar.activation(out=o2[c, h][:, 2 * pair : 2 * pair + 2, :], in_=z2[c, h, pair][:], func=ACT.Relu)
+            give_back(("z2", c, h, pair))
 
-        def mul_f(c, h):
-            for pair in range(2):
-                fb[c, h, pair] = psum.tile([P, 2, TB], F32, name="bank")
-                for v in range(2):
-                    mx(fb[c, h, pair][:, v, :], w_q["wf", h, 0], 2 * pair + v, u_q[c, h], 0, TB, True, True)
+        def mul_f(c, h, pair):
+            fb[c, h, pair] = bank_for(("f", c, h, pair), [P, 2, TB], F32)
+            for v in range(2):
+                mx(fb[c, h, pair][:, v, :], w_q["wf", h, 0], 2 * pair + v, u_q[c, h], 0, TB, True, True)
 
         def fuse(c, h, pair):
             if pair == 0:
-                fused[c, h] = work.tile([P, 4, TB], F32, name="fused", bufs=FUSED_BUFS)
+                fused[c, h] = buffer("fused", [P, 4, TB], F32, FUSED_BUFS)
             for v in range(2):
                 t = 2 * pair + v
                 nc.vector.scalar_tensor_tensor(
@@ -357,10 +378,11 @@ def tile_finalmlptwostreamfusion_kernel(tc, x, s, w1, w2_bytes, w2_scale, r, wf,
                     op0=ALU.add,
                     op1=ALU.mult,
                 )
+            give_back(("f", c, h, pair))
 
         def fuse_rows(c, h, i):
             if i == 0:
-                fused[c, h] = work.tile([P, 4, TB], F32, name="fused", bufs=FUSED_BUFS)
+                fused[c, h] = buffer("fused", [P, 4, TB], F32, FUSED_BUFS)
             tokens = slice(i * P, (i + 1) * P)
             for t in range(4):
                 nc.vector.scalar_tensor_tensor(
@@ -371,6 +393,8 @@ def tile_finalmlptwostreamfusion_kernel(tc, x, s, w1, w2_bytes, w2_scale, r, wf,
                     op0=ALU.add,
                     op1=ALU.mult,
                 )
+                if i == TT - 1 and t % 2 == 1:
+                    give_back(("f", c, h, t // 2))
 
         def merge(c, h):
             for t in range(4):
@@ -397,16 +421,15 @@ def tile_finalmlptwostreamfusion_kernel(tc, x, s, w1, w2_bytes, w2_scale, r, wf,
 
         def turn_out(c, h, i):
             terms = (fused,) if UNITS.index((c, h)) in MERGED else (weighed, fused)
-            tr[c, h, i] = psum.tile([P, M, 4, 2], F32, name="bank")
+            tr[c, h, i] = bank_for(("out", c, h, i), [P, M, 4, 2], F32)
             for t in range(4):
                 for n, term in enumerate(terms):
                     turn_tile(term, c, h, i, t, n == 0, n == len(terms) - 1)
 
-        def open_out(c, h):
-            for i in range(TT):
-                tr[c, h, i] = psum.tile([P, M, 4, 2], F32, name="bank")
-                for t in range(4):
-                    turn_tile(weighed, c, h, i, t, t == 0, False)
+        def open_out(c, h, i):
+            tr[c, h, i] = bank_for(("out", c, h, i), [P, M, 4, 2], F32)
+            for t in range(4):
+                turn_tile(weighed, c, h, i, t, t == 0, False)
 
         def close_out(c, h, i):
             for t in range(4):
@@ -415,8 +438,9 @@ def tile_finalmlptwostreamfusion_kernel(tc, x, s, w1, w2_bytes, w2_scale, r, wf,
         rows = {}
 
         def copy_out(c, h, i, copy):
-            rows[c, h, i] = work.tile([P, W], F32, name="rows", bufs=ROW_BUFS)
+            rows[c, h, i] = buffer("rows", [P, W], F32, ROW_BUFS)
             copy(out=rows[c, h, i][:], in_=tr[c, h, i][:].rearrange("n m t e -> n (m t e)"))
+            give_back(("out", c, h, i))
 
         def copy_scalar(c, h, i):
             copy_out(c, h, i, nc.scalar.copy)
@@ -435,68 +459,115 @@ def tile_finalmlptwostreamfusion_kernel(tc, x, s, w1, w2_bytes, w2_scale, r, wf,
         def unit(fn, k, *rest):
             return (fn, *UNITS[k], *rest)
 
-        def both(fn, k):
-            return [unit(fn, k, 0), unit(fn, k, 1)]
-
-        def gates(c, g):
-            return [(gate_x, c, g, 0), (gate_x, c, g, 1)]
-
-        def quants(c, g):
-            return [(quant_x, c, g, 0), (quant_x, c, g, 1)]
+        def both(fn, *what):
+            args = UNITS[what[0]] if what[0] in range(len(UNITS)) else what
+            return [(fn, *args, 0), (fn, *args, 1)]
 
         def widened(h, g):
             return [(widen_w2, h, g, 0), (widen_w2, h, g, 1)]
 
-        def mixes(piece):
-            return [(mix_w, piece, 0), (mix_w, piece, 1)]
+        def on_x(fn, *parts):
+            return [(fn, *part) for part in parts]
 
-        def taken(piece):
-            return [(take_w, piece, 0), (take_w, piece, 1)]
-
-        MIXED = [(piece, half) for piece in (W2[0, 0], W2[0, 1], WF[0]) for half in range(2)]
+        MIXED = [(piece, half) for piece in (W2[0, 0], W2[0, 1], WF[0]) for half in range(2)] + [(W1[0, 1], 1)]
         POOLED = (W1[0, 0], W1[0, 1], W1[1, 1], W2[1, 0], W2[1, 1], WF[1])
         POOL_GAINED = (4, 5, 6)
         VECTOR_WEIGHED = (7,)
-        BY_ROWS = (6, 7)
+        stretches = []
 
-        tensor = [(turn_x, 0, 0), (turn_x, 0, 1), (turn_x, 1, 0)] + mixes(W2[0, 0]) + [(turn_x, 1, 1)] + mixes(W2[0, 1])
-        tensor += [(turn_x, 2, 0), (mix_w, WF[0], 0)] + both(mul_z1, 0) + [(mix_w, WF[0], 1)] + both(mul_z1, 1)
-        tensor += [unit(mul_z2, 0), unit(mul_f, 0), (turn_x, 2, 1), unit(mul_z2, 1)] + both(mul_z1, 2) + both(turn_out, 0)
-        tensor += [unit(mul_f, 1), unit(mul_z1_wide, 4)] + both(mul_z1, 3) + both(turn_out, 1) + [(turn_x, 3, 0)]
-        tensor += [unit(mul_z2, 2), unit(mul_z2, 3), (turn_x, 3, 1), unit(mul_z1_wide, 5), unit(mul_f, 2), unit(mul_z2, 4), unit(mul_f, 3)]
-        tensor += [unit(mul_z2, 5)] + both(turn_out, 2) + [unit(mul_f, 4), unit(mul_z1_wide, 6)] + both(mul_z1, 7) + [unit(mul_z2, 6)]
-        tensor += both(turn_out, 3) + [unit(mul_z2, 7), unit(mul_f, 5)] + both(turn_out, 4) + both(turn_out, 5) + [unit(mul_f, 6), unit(mul_f, 7)]
-        tensor += [unit(open_out, 6)] + both(close_out, 6) + [unit(open_out, 7)] + both(close_out, 7)
+        def stretch(vector, tensor, scalar, pool=()):
+            stretches.append([tensor, vector, scalar, list(pool)])
 
-        first_gates = [(gate_x, c, g, stream) for c in range(2) for g in range(PASSES) for stream in range(2)]
-        vector = first_gates[:-1]
-        vector += [(quant_x, 0, 0, 0), (quant_x, 0, 1, 0), (quant_w, W1[0, 0]), (quant_w, W1[0, 1])]
-        vector += [first_gates[-1], (gate_x, 2, 0, 0), unit(gain_z1, 0)]
-        vector += [(quant_x, 1, 0, 0), (quant_x, 1, 1, 0), (quant_w, W2[0, 0]), (quant_x, 0, 0, 1), (quant_x, 0, 1, 1), (quant_w, W2[0, 1])]
-        vector += [unit(quant_u, 0), (quant_w, WF[0]), (quant_x, 1, 0, 1), (quant_x, 1, 1, 1), (quant_w, W1[1, 0]), (quant_w, W1[1, 1])]
-        vector += both(fuse, 0) + [unit(gain_z1, 1), (gate_x, 2, 1, 0)]
-        vector += [unit(quant_u, 1), (quant_x, 2, 0, 0), (quant_x, 2, 1, 0), (quant_w, W2[1, 0])]
-        vector += both(fuse, 1) + [unit(gain_z1, 2), (gate_x, 2, 0, 1)]
-        vector += [unit(quant_u, 2), (quant_x, 2, 0, 1), (quant_w, W2[1, 1])]
-        vector += [unit(gain_z1, 3), (gate_x, 2, 1, 1), (gate_x, 3, 0, 0)]
-        vector += [unit(quant_u, 3), (quant_x, 2, 1, 1), (quant_w, WF[1])]
-        vector += [(gate_x, 3, 0, 1), (gate_x, 3, 1, 0)] + both(fuse, 2)
-        vector += quants(3, 0) + [(quant_x, 3, 1, 0), unit(quant_u, 4)]
-        vector += both(fuse, 3) + [(gate_x, 3, 1, 1)] + both(fuse, 4)
-        vector += [(quant_x, 3, 1, 1), unit(merge, 3), unit(merge, 4), unit(quant_u, 5), unit(gain_z1, 7)] + both(fuse, 5)
-        vector += [unit(quant_u, 6), unit(quant_u, 7), unit(weigh_z1, 7)] + both(fuse_rows, 6) + both(fuse_rows, 7)
-        vector += [unit(copy_vector, 7, 1)]
-
-        scalar = widened(0, 0) + [(widen_w2, 1, 0, 0)] + widened(0, 1) + taken(W2[0, 0]) + [(widen_w2, 1, 0, 1), (widen_w2, 1, 1, 0)] + taken(W2[0, 1])
-        scalar += [(widen_r,), (take_w, WF[0], 0), (group_scalar, W1[1, 0], 0), (take_w, WF[0], 1), unit(relu_z1, 0), (group_scalar, W1[1, 0], 1), (widen_a,)]
-        scalar += [unit(relu_z2, 0), (widen_w2, 1, 1, 1), unit(weigh_o1, 0), unit(relu_z2, 1), unit(relu_z1, 1)]
-        scalar += both(copy_scalar, 0) + [unit(weigh_o1, 1), unit(relu_z1, 2), unit(relu_z1_wide, 4)] + both(copy_scalar, 1)
-        scalar += [unit(weigh_o1, 2), unit(relu_z1, 3), unit(relu_z2, 2), unit(relu_z2, 3)]
-        scalar += [unit(relu_z1_wide, 5), unit(relu_z2, 4), unit(weigh_o1, 5), unit(relu_z2, 5)] + both(copy_scalar, 2) + [unit(relu_z1_wide, 6)]
-        scalar += [unit(weigh_o1, 6), unit(relu_z2, 6)] + both(copy_scalar, 3) + [unit(relu_z2, 7)] + both(copy_scalar, 4)
-        scalar += both(copy_scalar, 5) + both(copy_scalar, 6) + [unit(copy_scalar, 7, 0)]
-
-        pool = [(group_pool, piece) for piece in POOLED] + [unit(gain_pool, k) for k in POOL_GAINED]
+        stretch(
+            [(gate_x, c, g, stream) for c in range(2) for g in range(PASSES) for stream in range(2)],
+            on_x(turn_x, (0, 0), (0, 1), (1, 0)) + [(mix_w, W2[0, 0], 0), (turn_x, 1, 1), (mix_w, W2[0, 0], 1), (mix_w, W1[0, 1], 1), (turn_x, 2, 0)],
+            widened(0, 0) + [(widen_w2, 1, 0, 0)] + widened(0, 1) + both(take_w, W2[0, 0]) + [(widen_w2, 1, 0, 1)],
+            [(group_pool, W1[0, 0]), (group_pool, W1[0, 1])],
+        )
+        stretch(
+            on_x(quant_x, (0, 0, 0), (0, 1, 0)) + [(quant_w, W1[0, 0]), (quant_w, W1[0, 1])],
+            both(mix_w, W2[0, 1]),
+            [(take_w, W1[0, 1], 1), (widen_w2, 1, 1, 0)],
+        )
+        stretch(
+            on_x(gate_x, (2, 0, 0), (2, 0, 1)) + both(gain_z1, 0),
+            both(mul_z1, 0) + both(mix_w, WF[0]),
+            both(take_w, W2[0, 1]) + [(widen_r,), (group_scalar, W1[1, 0], 0), (take_w, WF[0], 0)],
+            [(group_pool, W1[1, 1])],
+        )
+        stretch(
+            on_x(quant_x, (1, 0, 0), (1, 1, 0)) + [(quant_w, W2[0, 0])] + on_x(quant_x, (0, 0, 1), (0, 1, 1))
+            + [(quant_w, W2[0, 1]), unit(quant_u, 0), (quant_w, WF[0])] + on_x(quant_x, (1, 0, 1), (1, 1, 1))
+            + [(quant_w, W1[1, 0]), (quant_w, W1[1, 1])],
+            both(mul_z1, 1) + both(mul_z2, 0) + both(mul_f, 0) + [(turn_x, 2, 1)] + both(mul_z2, 1),
+            [(group_scalar, W1[1, 0], 1), (take_w, WF[0], 1)] + both(relu_z1, 0) + [(widen_a,)] + both(relu_z2, 0) + [(widen_w2, 1, 1, 1)],
+        )
+        stretch(
+            both(fuse, 0) + both(gain_z1, 1) + [(gate_x, 2, 1, 0)],
+            both(mul_z1, 2) + both(turn_out, 0),
+            [unit(weigh_o1, 0)] + both(relu_z2, 1) + both(relu_z1, 1),
+            [(group_pool, W2[1, 0])],
+        )
+        stretch(
+            [unit(quant_u, 1)] + on_x(quant_x, (2, 0, 0), (2, 1, 0)) + [(quant_w, W2[1, 0])],
+            both(mul_f, 1) + both(mul_z1, 4),
+            both(copy_scalar, 0),
+        )
+        stretch(
+            both(fuse, 1) + both(gain_z1, 2) + [(gate_x, 2, 1, 1)],
+            both(mul_z1, 3) + both(turn_out, 1),
+            [unit(weigh_o1, 1)] + both(relu_z1, 4) + both(relu_z1, 2),
+            [(group_pool, W2[1, 1])],
+        )
+        stretch(
+            [unit(quant_u, 2)] + on_x(quant_x, (2, 0, 1), (2, 1, 1)) + [(quant_w, W2[1, 1])],
+            on_x(turn_x, (3, 0), (3, 1)) + both(mul_z2, 2),
+            both(copy_scalar, 1) + [unit(weigh_o1, 2)],
+        )
+        stretch(
+            both(gain_z1, 3) + on_x(gate_x, (3, 0, 0), (3, 1, 0)),
+            both(mul_z2, 3) + both(mul_z1, 5),
+            both(relu_z2, 2) + both(relu_z1, 3) + both(relu_z2, 3),
+            [(group_pool, WF[1])],
+        )
+        stretch(
+            [unit(quant_u, 3)] + on_x(quant_x, (3, 0, 0), (3, 1, 0)) + [(quant_w, WF[1])],
+            both(mul_z2, 4) + both(mul_z2, 5),
+            both(relu_z1, 5),
+        )
+        stretch(
+            on_x(gate_x, (3, 0, 1), (3, 1, 1)) + both(fuse, 2),
+            both(mul_f, 2) + both(mul_f, 3) + both(mul_z1, 7),
+            both(relu_z2, 4) + both(relu_z2, 5),
+            [unit(gain_pool, 4)],
+        )
+        stretch(
+            on_x(quant_x, (3, 0, 1), (3, 1, 1)) + [unit(quant_u, 4)],
+            both(turn_out, 2),
+            [unit(weigh_o1, 5)],
+        )
+        stretch(
+            both(fuse, 3) + both(gain_z1, 7) + both(fuse, 4),
+            both(mul_f, 4) + both(mul_z1, 6) + both(mul_z2, 7),
+            both(copy_scalar, 2) + both(relu_z1, 6) + both(relu_z2, 7),
+            [unit(gain_pool, 5)],
+        )
+        stretch(
+            [unit(merge, 3), unit(quant_u, 7), unit(merge, 4), unit(quant_u, 5)],
+            both(mul_z2, 6) + both(turn_out, 3) + both(mul_f, 7) + [unit(turn_out, 4, 0)],
+            both(relu_z2, 6) + both(copy_scalar, 3),
+        )
+        stretch(
+            both(weigh_z1, 7) + both(fuse, 5) + [unit(fuse_rows, 7, 0)],
+            both(mul_f, 5) + [unit(turn_out, 4, 1)] + both(open_out, 7) + both(turn_out, 5),
+            [unit(copy_scalar, 4, 0), unit(weigh_o1, 6), unit(copy_scalar, 4, 1)],
+            [unit(gain_pool, 6)],
+        )
+        stretch(
+            [unit(quant_u, 6), unit(fuse_rows, 7, 1)] + both(fuse_rows, 6) + [unit(copy_vector, 6, 1)],
+            both(mul_f, 6) + both(close_out, 7) + both(open_out, 6) + both(close_out, 6),
+            both(copy_scalar, 5) + both(copy_scalar, 7) + [unit(copy_scalar, 6, 0)],
+        )
 
         def needs(fn, *args):
             if fn in (turn_x, widen_w2, widen_r, widen_a):
@@ -508,64 +579,68 @@ def tile_finalmlptwostreamfusion_kernel(tc, x, s, w1, w2_bytes, w2_scale, r, wf,
             if fn in (mix_w, group_scalar, group_pool):
                 return [(widen_w2, *args[0][1:], 1)] if args[0][0] == "w2" else []
             if fn is take_w:
-                return [(mix_w, *args)]
+                return [(mix_w, *args)] + ([(group_pool, args[0])] if args[0] in POOLED else [])
             if fn is quant_w:
+                halves = [(take_w if (*args, half) in MIXED else group_scalar, *args, half) for half in range(2)]
                 if args[0] in POOLED:
-                    return [(group_pool, *args)]
-                return [(take_w if (*args, half) in MIXED else group_scalar, *args, half) for half in range(2)]
+                    return [(group_pool, *args)] + [stage for stage in halves if stage[0] is take_w]
+                return halves
             c, h = args[:2]
             k = UNITS.index((c, h))
-            if fn in (mul_z1, mul_z1_wide):
-                return [(quant_w, W1[h, g]) for g in range(PASSES)] + [(quant_x, c, g, 0) for g in range(PASSES)]
-            if fn is mul_z2:
-                return [(quant_w, W2[h, g]) for g in range(PASSES)] + [(quant_x, c, g, 1) for g in range(PASSES)]
+            weighs = both(weigh_z1, k) if k in VECTOR_WEIGHED else [unit(weigh_o1, k)]
+            if fn in (mul_z1, mul_z2):
+                weight, stream = (W1, 0) if fn is mul_z1 else (W2, 1)
+                return [(quant_w, weight[h, g]) for g in range(PASSES)] + [(quant_x, c, g, stream) for g in range(PASSES)]
             if fn is gain_z1:
-                return [(mul_z1, c, h, 1), (widen_r,)]
-            weigh = weigh_z1 if k in VECTOR_WEIGHED else weigh_o1
+                return [(mul_z1, *args), (widen_r,)]
+            if fn is relu_z1:
+                return [(mul_z1 if pooled(c, h) else gain_z1, *args)]
             if fn is weigh_z1:
-                return [(gain_z1, c, h), (widen_a,)]
-            if fn is relu_z1_wide:
-                return [(mul_z1_wide, c, h)]
-            if fn is gain_pool:
-                return [(relu_z1_wide, c, h)]
-            if fn in (relu_z1, quant_u):
-                return [(gain_pool if k in POOL_GAINED else gain_z1, c, h)]
-            if fn is weigh_o1:
-                return [(relu_z1_wide if k in POOL_GAINED else relu_z1, c, h), (widen_a,)]
+                return [(gain_z1, *args), (widen_a,)]
+            if fn in (gain_pool, weigh_o1):
+                return both(relu_z1, k) + [(widen_r,), (widen_a,)]
+            if fn is quant_u:
+                return [unit(gain_pool, k)] if pooled(c, h) else both(gain_z1, k)
             if fn is relu_z2:
-                return [(mul_z2, c, h)]
+                return [(mul_z2, *args)]
             if fn is mul_f:
-                return [(quant_u, c, h), (quant_w, WF[h])]
-            if fn in (fuse, fuse_rows):
-                return [(mul_f, c, h), (relu_z2, c, h), (widen_a,)]
+                return [unit(quant_u, k), (quant_w, WF[h])]
+            if fn is fuse:
+                return [(mul_f, *args), (relu_z2, *args), (widen_a,)]
+            if fn is fuse_rows:
+                return both(mul_f, k) + both(relu_z2, k)
             if fn is merge:
-                return [(fuse, c, h, 1), (relu_z1_wide if k in POOL_GAINED else relu_z1, c, h)]
+                return both(fuse, k) + both(relu_z1, k)
             if fn is turn_out:
-                return [(merge, c, h)] if UNITS.index((c, h)) in MERGED else [(fuse_rows, *args) if k in BY_ROWS else (fuse, c, h, 1), (weigh, c, h)]
+                return [unit(merge, k)] if k in MERGED else both(fuse, k) + weighs
             if fn is open_out:
-                return [(weigh, c, h)]
+                return weighs
             if fn is close_out:
-                return [(fuse_rows, *args), (open_out, c, h)]
-            if fn is store:
-                return [(copy_vector if (copy_vector, *args) in by_vector else copy_scalar, *args)]
-            return [(close_out, *args)] if k in OPENED else [(turn_out, *args)]
+                return [(fuse_rows, *args), (open_out, *args)]
+            return [(close_out if k in OPENED else turn_out, *args)]
 
-        def waits(stage):
-            if stage in chain[1:]:
-                before = chain[chain.index(stage) - 1]
-                return [(quant_w if before[0] is group_pool else quant_u, *before[1:])]
-            return []
+        def banks_wanted(fn, *args):
+            if (fn, *args) == (turn_x, 0, 0):
+                return TT
+            return 1 if fn in (turn_x, mix_w, mul_z1, mul_z2, mul_f, turn_out, open_out) else 0
 
-        chain = pool[1:]
-        by_vector = [stage for stage in vector if stage[0] is copy_vector]
-        sync = [stage for k in range(LAST + 1) for stage in both(store, k)]
+        long_stages = (gate_x, merge, widen_w2, group_scalar, weigh_o1, mix_w)
         done = set()
-        programs = [tensor, vector, scalar, pool, sync]
-        while any(programs):
-            before = len(done)
-            for program in programs:
-                while program and all(stage in done for stage in needs(*program[0]) + waits(program[0])):
+        rested = set()
+        for programs in stretches:
+            while any(programs):
+                before = len(done) + len(rested)
+                for program in programs:
+                    if not program or banks_wanted(*program[0]) > len(free_banks):
+                        continue
+                    if not all(stage in done for stage in needs(*program[0])):
+                        continue
+                    if program[0][0] in long_stages and program[0] not in rested:
+                        rested.add(program[0])
+                        continue
                     stage = program.pop(0)
                     stage[0](*stage[1:])
+                    if stage[0] in (copy_scalar, copy_vector):
+                        store(*stage[1:])
                     done.add(stage)
-            assert len(done) > before
+                assert len(done) + len(rested) > before

@@ -62,17 +62,19 @@ def tile_finalmlptwostreamfusion_kernel(tc, x, s, w1, w2_bytes, w2_scale, r, wf,
         ws = keep.tile([P, PASSES, 4], F32, name="ws")
         r_bf = keep.tile([P, HEADS, 8], BF16, name="r_bf")
         a_bf = keep.tile([P, 2 * HEADS, 8], BF16, name="a_bf")
-        x_raw = {}
         x_part = {}
         w2_raw = {}
         rows4 = {}
 
         def load_x_first():
-            for i in range(TT):
-                x_raw[0, i] = keep.tile([P, D], BF16, name="x_first%d" % i)
-                nc.sync.dma_start(out=x_raw[0, i][:], in_=x[i * P : (i + 1) * P, :])
-                for g in range(PASSES):
-                    x_part[0, i, g] = x_raw[0, i][:, g * KP : (g + 1) * KP]
+            for g in range(PASSES):
+                first = keep.tile([P, KP], BF16, name="x_first%d" % g)
+                nc.sync.dma_start(out=first[:], in_=x[0:P, g * KP : (g + 1) * KP])
+                x_part[0, 0, g] = first[:]
+            second = keep.tile([P, D], BF16, name="x_second")
+            nc.sync.dma_start(out=second[:], in_=x[P:TB, :])
+            for g in range(PASSES):
+                x_part[0, 1, g] = second[:, g * KP : (g + 1) * KP]
 
         def load_x(c):
             rows_c = keep.tile([P, TT * D], BF16, name="x_raw%d" % c)
@@ -120,10 +122,9 @@ def tile_finalmlptwostreamfusion_kernel(tc, x, s, w1, w2_bytes, w2_scale, r, wf,
         load_x_first()
         nc.scalar.dma_start(out=ws[:], in_=w2_scale.rearrange("(g p t) o -> p g (t o)", p=P, t=4))
         load_w2(0)
+        load_x(1)
         load_w1(0, 0)
-        load_x_pass(1, 0)
         load_w2(1)
-        load_x_pass(1, 1)
         load_w1(0, 1)
         load_x_pass(2, 0)
         load_wf(0)
@@ -137,8 +138,8 @@ def tile_finalmlptwostreamfusion_kernel(tc, x, s, w1, w2_bytes, w2_scale, r, wf,
 
         sig = keep.tile([P, 2 * PASSES, 4], F32, name="sig")
         nc.scalar.activation(out=sig[:], in_=s_bf[:], func=ACT.Sigmoid)
-        gate = keep.tile([P, 2 * PASSES, 4], F32, name="gate")
-        nc.vector.tensor_scalar(out=gate[:], in0=sig[:], scalar1=2.0, scalar2=None, op0=ALU.mult)
+        gates = keep.tile([P, 2 * PASSES, 4], F32, name="gates")
+        nc.vector.tensor_scalar(out=gates[:], in0=sig[:], scalar1=2.0, scalar2=None, op0=ALU.mult)
         ident_bf = keep.tile([P, P], BF16, name="ident_bf")
         nc.scalar.copy(out=ident_bf[:], in_=ident[:])
         r_f = keep.tile([P, HEADS, 4], F32, name="r_f")
@@ -174,35 +175,39 @@ def tile_finalmlptwostreamfusion_kernel(tc, x, s, w1, w2_bytes, w2_scale, r, wf,
         g_q = {}
 
         def turn_x(c, g):
-            if (c, g) == (0, 0):
-                xt[c, g] = []
-                for i in range(TT):
-                    bank = bank_for(("x", c, g, i), [P, 2, P], F32)
-                    for u in range(2):
-                        nc.tensor.transpose(bank[:, u, :], x_part[c, i, g].bitcast(F32)[:, u::2], ident[:])
-                    xt[c, g].append((i * P, P, bank))
-                return
-            bank = bank_for(("x", c, g, 0), [P, 2, TB], F32)
+            xt[c, g] = bank_for(("x", c, g), [P, 2, TB], F32)
             for u in range(2):
                 for i in range(TT):
                     words = x_part[c, i, g].bitcast(F32)
-                    nc.tensor.transpose(bank[:, u, i * P : (i + 1) * P], words[:, u::2], ident[:])
-            xt[c, g] = [(0, TB, bank)]
+                    nc.tensor.transpose(xt[c, g][:, u, i * P : (i + 1) * P], words[:, u::2], ident[:])
+
+        def turn_tile_x(i, g):
+            xt[0, g, i] = bank_for(("x", 0, g, i), [P, 2, P], F32)
+            for u in range(2):
+                nc.tensor.transpose(xt[0, g, i][:, u, :], x_part[0, i, g].bitcast(F32)[:, u::2], ident[:])
+
+        def gate(c, g, stream, bank, n0, n):
+            if (c, g, stream) not in xg:
+                gated_in[c, g, stream] = free_gated.pop(0)
+                name = "xg%d" % gated_in[c, g, stream]
+                xg[c, g, stream] = work.tile([P, TB, 4], BF16, name=name, bufs=1, align_bytes=64)
+            factor = gates[:, PASSES * stream + g, :].rearrange("p (u e) -> p u e", e=2).unsqueeze(1)
+            nc.vector.tensor_tensor(
+                out=xg[c, g, stream][:, n0 : n0 + n, :].rearrange("p n (u e) -> p n u e", e=2),
+                in0=bank[:].bitcast(BF16).rearrange("p u (n e) -> p n u e", e=2),
+                in1=factor.to_broadcast([P, n, 2, 2]),
+                op=ALU.mult,
+            )
 
         def gate_x(c, g, stream):
-            gated_in[c, g, stream] = free_gated.pop(0)
-            name = "xg%d" % gated_in[c, g, stream]
-            xg[c, g, stream] = work.tile([P, TB, 4], BF16, name=name, bufs=1, align_bytes=64)
-            factor = gate[:, PASSES * stream + g, :].rearrange("p (u e) -> p u e", e=2).unsqueeze(1)
-            for n0, n, bank in xt[c, g]:
-                nc.vector.tensor_tensor(
-                    out=xg[c, g, stream][:, n0 : n0 + n, :].rearrange("p n (u e) -> p n u e", e=2),
-                    in0=bank[:].bitcast(BF16).rearrange("p u (n e) -> p n u e", e=2),
-                    in1=factor.to_broadcast([P, n, 2, 2]),
-                    op=ALU.mult,
-                )
-                if (c, g, 1 - stream) in xg:
-                    give_back(("x", c, g, n0 // P))
+            gate(c, g, stream, xt[c, g], 0, TB)
+            if (c, g, 1 - stream) in xg:
+                give_back(("x", c, g))
+
+        def gate_tile_x(i, g):
+            for stream in range(2):
+                gate(0, g, stream, xt[0, g, i], i * P, P)
+            give_back(("x", 0, g, i))
 
         def quant_x(c, g, stream):
             grouped = xg[c, g, stream][:].rearrange("p n j -> p (n j)")
@@ -213,16 +218,15 @@ def tile_finalmlptwostreamfusion_kernel(tc, x, s, w1, w2_bytes, w2_scale, r, wf,
         wg = {}
         w_q = {}
 
-        def widen_w2(h, g, half):
-            if half == 0:
+        def widen_w2(h, g, j):
+            if j == 0:
                 rows4["w2", h, g] = buffer("wide", [P, 4, W], BF16, WIDE_BUFS)
-            for j in (2 * half, 2 * half + 1):
-                nc.scalar.activation(
-                    out=rows4["w2", h, g][:, j, :],
-                    in_=w2_raw[h, g][:, j, :].bitcast(FP8),
-                    func=ACT.Copy,
-                    scale=ws[:, g, j : j + 1],
-                )
+            nc.scalar.activation(
+                out=rows4["w2", h, g][:, j, :],
+                in_=w2_raw[h, g][:, j, :].bitcast(FP8),
+                func=ACT.Copy,
+                scale=ws[:, g, j : j + 1],
+            )
 
         def mix_w(piece, half):
             bank = bank_for(("mix", piece, half), [P, 2, P, 4], BF16)
@@ -463,8 +467,8 @@ def tile_finalmlptwostreamfusion_kernel(tc, x, s, w1, w2_bytes, w2_scale, r, wf,
             args = UNITS[what[0]] if what[0] in range(len(UNITS)) else what
             return [(fn, *args, 0), (fn, *args, 1)]
 
-        def widened(h, g):
-            return [(widen_w2, h, g, 0), (widen_w2, h, g, 1)]
+        def widened(h, g, first=0, last=3):
+            return [(widen_w2, h, g, j) for j in range(first, last + 1)]
 
         def on_x(fn, *parts):
             return [(fn, *part) for part in parts]
@@ -479,15 +483,15 @@ def tile_finalmlptwostreamfusion_kernel(tc, x, s, w1, w2_bytes, w2_scale, r, wf,
             stretches.append([tensor, vector, scalar, list(pool)])
 
         stretch(
-            [(gate_x, c, g, stream) for c in range(2) for g in range(PASSES) for stream in range(2)],
-            on_x(turn_x, (0, 0), (0, 1), (1, 0)) + [(mix_w, W2[0, 0], 0), (turn_x, 1, 1), (mix_w, W2[0, 0], 1), (mix_w, W1[0, 1], 1), (turn_x, 2, 0)],
-            widened(0, 0) + [(widen_w2, 1, 0, 0)] + widened(0, 1) + both(take_w, W2[0, 0]) + [(widen_w2, 1, 0, 1)],
+            [(gate_tile_x, i, g) for i in range(TT) for g in range(PASSES)] + [(gate_x, 1, g, stream) for g in range(PASSES) for stream in range(2)],
+            [(turn_tile_x, i, g) for i in range(TT) for g in range(PASSES)] + on_x(turn_x, (1, 0), (1, 1)) + both(mix_w, W2[0, 0]) + [(mix_w, W1[0, 1], 1), (turn_x, 2, 0)],
+            widened(0, 0) + widened(1, 0, 0, 2) + widened(0, 1) + [(take_w, W2[0, 0], 0), (take_w, W1[0, 1], 1)],
             [(group_pool, W1[0, 0]), (group_pool, W1[0, 1])],
         )
         stretch(
             on_x(quant_x, (0, 0, 0), (0, 1, 0)) + [(quant_w, W1[0, 0]), (quant_w, W1[0, 1])],
             both(mix_w, W2[0, 1]),
-            [(take_w, W1[0, 1], 1), (widen_w2, 1, 1, 0)],
+            [(take_w, W2[0, 0], 1)] + widened(1, 0, 3, 3) + widened(1, 1, 0, 1),
         )
         stretch(
             on_x(gate_x, (2, 0, 0), (2, 0, 1)) + both(gain_z1, 0),
@@ -500,7 +504,7 @@ def tile_finalmlptwostreamfusion_kernel(tc, x, s, w1, w2_bytes, w2_scale, r, wf,
             + [(quant_w, W2[0, 1]), unit(quant_u, 0), (quant_w, WF[0])] + on_x(quant_x, (1, 0, 1), (1, 1, 1))
             + [(quant_w, W1[1, 0]), (quant_w, W1[1, 1])],
             both(mul_z1, 1) + both(mul_z2, 0) + both(mul_f, 0) + [(turn_x, 2, 1)] + both(mul_z2, 1),
-            [(group_scalar, W1[1, 0], 1), (take_w, WF[0], 1)] + both(relu_z1, 0) + [(widen_a,)] + both(relu_z2, 0) + [(widen_w2, 1, 1, 1)],
+            [(group_scalar, W1[1, 0], 1), (take_w, WF[0], 1)] + both(relu_z1, 0) + [(widen_a,)] + both(relu_z2, 0) + widened(1, 1, 2, 3),
         )
         stretch(
             both(fuse, 0) + both(gain_z1, 1) + [(gate_x, 2, 1, 0)],
@@ -570,14 +574,16 @@ def tile_finalmlptwostreamfusion_kernel(tc, x, s, w1, w2_bytes, w2_scale, r, wf,
         )
 
         def needs(fn, *args):
-            if fn in (turn_x, widen_w2, widen_r, widen_a):
+            if fn in (turn_x, turn_tile_x, widen_w2, widen_r, widen_a):
                 return []
             if fn is gate_x:
                 return [(turn_x, *args[:2])]
+            if fn is gate_tile_x:
+                return [(turn_tile_x, *args)]
             if fn is quant_x:
-                return [(gate_x, *args)]
+                return [(gate_x, *args) if args[0] else (gate_tile_x, TT - 1, args[1])]
             if fn in (mix_w, group_scalar, group_pool):
-                return [(widen_w2, *args[0][1:], 1)] if args[0][0] == "w2" else []
+                return [(widen_w2, *args[0][1:], 3)] if args[0][0] == "w2" else []
             if fn is take_w:
                 return [(mix_w, *args)] + ([(group_pool, args[0])] if args[0] in POOLED else [])
             if fn is quant_w:
@@ -620,11 +626,9 @@ def tile_finalmlptwostreamfusion_kernel(tc, x, s, w1, w2_bytes, w2_scale, r, wf,
             return [(close_out if k in OPENED else turn_out, *args)]
 
         def banks_wanted(fn, *args):
-            if (fn, *args) == (turn_x, 0, 0):
-                return TT
-            return 1 if fn in (turn_x, mix_w, mul_z1, mul_z2, mul_f, turn_out, open_out) else 0
+            return 1 if fn in (turn_x, turn_tile_x, mix_w, mul_z1, mul_z2, mul_f, turn_out, open_out) else 0
 
-        long_stages = (gate_x, merge, widen_w2, group_scalar, weigh_o1, mix_w)
+        long_stages = (gate_x, gate_tile_x, merge, group_scalar, weigh_o1, mix_w)
         done = set()
         rested = set()
         for programs in stretches:

@@ -321,11 +321,10 @@ def tile_finalmlptwostreamfusion_kernel(tc, x, s, w1, w2_bytes, w2_scale, r, wf,
                 op=ALU.mult,
             )
 
-        def weigh_o1(c, h):
-            weighed[c, h] = o1[c, h]
-            if pooled(c, h):
-                weighed[c, h] = buffer("weighed", [P, 4, TB], F32, 2)
-            for t in range(4):
+        def weigh_o1(c, h, pair):
+            if pair == 0:
+                weighed[c, h] = buffer("weighed", [P, 4, TB], F32, 2) if pooled(c, h) else o1[c, h]
+            for t in (2 * pair, 2 * pair + 1):
                 nc.scalar.activation(
                     out=weighed[c, h][:, t, :], in_=o1[c, h][:, t, :], func=ACT.Copy, scale=a_f[:, h, t : t + 1]
                 )
@@ -509,7 +508,7 @@ def tile_finalmlptwostreamfusion_kernel(tc, x, s, w1, w2_bytes, w2_scale, r, wf,
         stretch(
             both(fuse, 0) + both(gain_z1, 1) + [(gate_x, 2, 1, 0)],
             both(mul_z1, 2) + both(turn_out, 0),
-            [unit(weigh_o1, 0)] + both(relu_z2, 1) + both(relu_z1, 1),
+            both(weigh_o1, 0) + both(relu_z2, 1) + both(relu_z1, 1),
             [(group_pool, W2[1, 0])],
         )
         stretch(
@@ -520,57 +519,57 @@ def tile_finalmlptwostreamfusion_kernel(tc, x, s, w1, w2_bytes, w2_scale, r, wf,
         stretch(
             both(fuse, 1) + both(gain_z1, 2) + [(gate_x, 2, 1, 1)],
             both(mul_z1, 3) + both(turn_out, 1),
-            [unit(weigh_o1, 1)] + both(relu_z1, 4) + both(relu_z1, 2),
+            both(weigh_o1, 1) + both(relu_z1, 4) + both(relu_z1, 2),
             [(group_pool, W2[1, 1])],
         )
         stretch(
             [unit(quant_u, 2)] + on_x(quant_x, (2, 0, 1), (2, 1, 1)) + [(quant_w, W2[1, 1])],
-            on_x(turn_x, (3, 0), (3, 1)) + both(mul_z2, 2),
-            both(copy_scalar, 1) + [unit(weigh_o1, 2)],
+            on_x(turn_x, (3, 0), (3, 1)) + both(mul_z1, 5),
+            both(copy_scalar, 1) + [unit(weigh_o1, 2, 0)],
         )
         stretch(
             both(gain_z1, 3) + on_x(gate_x, (3, 0, 0), (3, 1, 0)),
-            both(mul_z2, 3) + both(mul_z1, 5),
-            both(relu_z2, 2) + both(relu_z1, 3) + both(relu_z2, 3),
+            both(mul_z2, 2) + both(mul_z2, 3),
+            both(relu_z1, 5) + both(relu_z1, 3) + both(relu_z2, 2),
             [(group_pool, WF[1])],
         )
         stretch(
             [unit(quant_u, 3)] + on_x(quant_x, (3, 0, 0), (3, 1, 0)) + [(quant_w, WF[1])],
             both(mul_z2, 4) + both(mul_z2, 5),
-            both(relu_z1, 5),
+            both(relu_z2, 3),
         )
         stretch(
             on_x(gate_x, (3, 0, 1), (3, 1, 1)) + both(fuse, 2),
             both(mul_f, 2) + both(mul_f, 3) + both(mul_z1, 7),
-            both(relu_z2, 4) + both(relu_z2, 5),
+            both(relu_z2, 4) + both(relu_z2, 5) + [unit(weigh_o1, 2, 1)],
             [unit(gain_pool, 4)],
         )
         stretch(
             on_x(quant_x, (3, 0, 1), (3, 1, 1)) + [unit(quant_u, 4)],
-            both(turn_out, 2),
-            [unit(weigh_o1, 5)],
+            [unit(mul_z1, 6, 0)] + both(turn_out, 2),
+            [unit(weigh_o1, 5, 0), unit(relu_z1, 6, 0), unit(weigh_o1, 5, 1)],
         )
         stretch(
             both(fuse, 3) + both(gain_z1, 7) + both(fuse, 4),
-            both(mul_f, 4) + both(mul_z1, 6) + both(mul_z2, 7),
-            both(copy_scalar, 2) + both(relu_z1, 6) + both(relu_z2, 7),
+            both(mul_f, 4) + [unit(mul_z1, 6, 1)] + both(mul_z2, 7),
+            both(copy_scalar, 2) + [unit(relu_z1, 6, 1)] + both(relu_z2, 7),
             [unit(gain_pool, 5)],
         )
         stretch(
             [unit(merge, 3), unit(quant_u, 7), unit(merge, 4), unit(quant_u, 5)],
-            both(mul_z2, 6) + both(turn_out, 3) + both(mul_f, 7) + [unit(turn_out, 4, 0)],
-            both(relu_z2, 6) + both(copy_scalar, 3),
+            both(mul_z2, 6) + both(turn_out, 3) + both(mul_f, 7) + both(turn_out, 4),
+            both(relu_z2, 6) + both(copy_scalar, 3) + [unit(weigh_o1, 6, 0)],
         )
         stretch(
             both(weigh_z1, 7) + both(fuse, 5) + [unit(fuse_rows, 7, 0)],
-            both(mul_f, 5) + [unit(turn_out, 4, 1)] + both(open_out, 7) + both(turn_out, 5),
-            [unit(copy_scalar, 4, 0), unit(weigh_o1, 6), unit(copy_scalar, 4, 1)],
+            both(mul_f, 5) + both(open_out, 7) + [unit(open_out, 6, 0)] + both(turn_out, 5),
+            [unit(copy_scalar, 4, 0), unit(weigh_o1, 6, 1), unit(copy_scalar, 4, 1), unit(copy_scalar, 5, 0)],
             [unit(gain_pool, 6)],
         )
         stretch(
             [unit(quant_u, 6), unit(fuse_rows, 7, 1)] + both(fuse_rows, 6) + [unit(copy_vector, 6, 1)],
-            both(mul_f, 6) + both(close_out, 7) + both(open_out, 6) + both(close_out, 6),
-            both(copy_scalar, 5) + both(copy_scalar, 7) + [unit(copy_scalar, 6, 0)],
+            [unit(close_out, 7, 0)] + both(mul_f, 6) + [unit(close_out, 7, 1), unit(open_out, 6, 1)] + both(close_out, 6),
+            [unit(copy_scalar, 5, 1)] + both(copy_scalar, 7) + [unit(copy_scalar, 6, 0)],
         )
 
         def needs(fn, *args):
@@ -593,7 +592,7 @@ def tile_finalmlptwostreamfusion_kernel(tc, x, s, w1, w2_bytes, w2_scale, r, wf,
                 return halves
             c, h = args[:2]
             k = UNITS.index((c, h))
-            weighs = both(weigh_z1, k) if k in VECTOR_WEIGHED else [unit(weigh_o1, k)]
+            weighs = both(weigh_z1 if k in VECTOR_WEIGHED else weigh_o1, k)
             if fn in (mul_z1, mul_z2):
                 weight, stream = (W1, 0) if fn is mul_z1 else (W2, 1)
                 return [(quant_w, weight[h, g]) for g in range(PASSES)] + [(quant_x, c, g, stream) for g in range(PASSES)]
@@ -628,7 +627,7 @@ def tile_finalmlptwostreamfusion_kernel(tc, x, s, w1, w2_bytes, w2_scale, r, wf,
         def banks_wanted(fn, *args):
             return 1 if fn in (turn_x, turn_tile_x, mix_w, mul_z1, mul_z2, mul_f, turn_out, open_out) else 0
 
-        long_stages = (gate_x, gate_tile_x, merge, group_scalar, weigh_o1, mix_w)
+        long_stages = (gate_x, gate_tile_x, merge, group_scalar, mix_w)
         done = set()
         rested = set()
         for programs in stretches:

@@ -28,7 +28,7 @@ BANKS = 8
 MERGED = (3, 4)
 OPENED = (6, 7)
 
-XG_BUFS, WIDE_BUFS, WG_BUFS, UG_BUFS, O_BUFS, FUSED_BUFS, ROW_BUFS = 8, 3, 4, 2, 5, 4, 6
+XG_BUFS, WIDE_BUFS, WG_BUFS, UG_BUFS, O_BUFS, FUSED_BUFS, ROW_BUFS = 5, 3, 4, 2, 5, 3, 6
 
 
 def tile_finalmlptwostreamfusion_kernel(tc, x, s, w1, w2_bytes, w2_scale, r, wf, a, out):
@@ -187,13 +187,13 @@ def tile_finalmlptwostreamfusion_kernel(tc, x, s, w1, w2_bytes, w2_scale, r, wf,
                 nc.tensor.transpose(xt[0, g, i][:, u, :], x_part[0, i, g].bitcast(F32)[:, u::2], ident[:])
 
         def gate(c, g, stream, bank, n0, n):
-            if (c, g, stream) not in xg:
-                gated_in[c, g, stream] = free_gated.pop(0)
-                name = "xg%d" % gated_in[c, g, stream]
-                xg[c, g, stream] = work.tile([P, TB, 4], BF16, name=name, bufs=1, align_bytes=64)
+            if (c, stream) not in xg:
+                gated_in[c, stream] = free_gated.pop(0)
+                name = "xg%d" % gated_in[c, stream]
+                xg[c, stream] = work.tile([P, PASSES, TB, 4], BF16, name=name, bufs=1, align_bytes=64)
             factor = gates[:, PASSES * stream + g, :].rearrange("p (u e) -> p u e", e=2).unsqueeze(1)
             nc.vector.tensor_tensor(
-                out=xg[c, g, stream][:, n0 : n0 + n, :].rearrange("p n (u e) -> p n u e", e=2),
+                out=xg[c, stream][:, g, n0 : n0 + n, :].rearrange("p n (u e) -> p n u e", e=2),
                 in0=bank[:].bitcast(BF16).rearrange("p u (n e) -> p n u e", e=2),
                 in1=factor.to_broadcast([P, n, 2, 2]),
                 op=ALU.mult,
@@ -201,7 +201,7 @@ def tile_finalmlptwostreamfusion_kernel(tc, x, s, w1, w2_bytes, w2_scale, r, wf,
 
         def gate_x(c, g, stream):
             gate(c, g, stream, xt[c, g], 0, TB)
-            if (c, g, 1 - stream) in xg:
+            if stream == 1:
                 give_back(("x", c, g))
 
         def gate_tile_x(i, g):
@@ -209,10 +209,10 @@ def tile_finalmlptwostreamfusion_kernel(tc, x, s, w1, w2_bytes, w2_scale, r, wf,
                 gate(0, g, stream, xt[0, g, i], i * P, P)
             give_back(("x", 0, g, i))
 
-        def quant_x(c, g, stream):
-            grouped = xg[c, g, stream][:].rearrange("p n j -> p (n j)")
-            g_q[c, g, stream] = quantize(grouped, TB, "g%dq%d_%d" % (stream, c, g))
-            free_gated.append(gated_in[c, g, stream])
+        def quant_x(c, stream):
+            grouped = xg[c, stream][:].rearrange("p g n j -> p (g n j)")
+            g_q[c, stream] = quantize(grouped, PASSES * TB, "g%dq%d" % (stream, c))
+            free_gated.append(gated_in[c, stream])
 
         mixed = {}
         wg = {}
@@ -291,7 +291,7 @@ def tile_finalmlptwostreamfusion_kernel(tc, x, s, w1, w2_bytes, w2_scale, r, wf,
                 parts = [(z1[c, h, n][:, t, :], t, n * P, P) for t in range(4)]
             for dst, t, n0, tokens in parts:
                 for g in range(PASSES):
-                    mx(dst, w_q["w1", h, g], t, g_q[c, g, 0], n0, tokens, g == 0, g == PASSES - 1)
+                    mx(dst, w_q["w1", h, g], t, g_q[c, 0], g * TB + n0, tokens, g == 0, g == PASSES - 1)
 
         def gain_z1(c, h, i):
             if i == 0:
@@ -355,7 +355,7 @@ def tile_finalmlptwostreamfusion_kernel(tc, x, s, w1, w2_bytes, w2_scale, r, wf,
             for v in range(2):
                 for g in range(PASSES):
                     dst = z2[c, h, pair][:, v, :]
-                    mx(dst, w_q["w2", h, g], 2 * pair + v, g_q[c, g, 1], 0, TB, g == 0, g == PASSES - 1)
+                    mx(dst, w_q["w2", h, g], 2 * pair + v, g_q[c, 1], g * TB, TB, g == 0, g == PASSES - 1)
 
         def relu_z2(c, h, pair):
             if pair == 0:
@@ -488,7 +488,7 @@ def tile_finalmlptwostreamfusion_kernel(tc, x, s, w1, w2_bytes, w2_scale, r, wf,
             [(group_pool, W1[0, 0]), (group_pool, W1[0, 1])],
         )
         stretch(
-            on_x(quant_x, (0, 0, 0), (0, 1, 0)) + [(quant_w, W1[0, 0]), (quant_w, W1[0, 1])],
+            [(quant_x, 0, 0)] + [(quant_w, W1[0, 0]), (quant_w, W1[0, 1])],
             both(mix_w, W2[0, 1]),
             [(take_w, W2[0, 0], 1)] + widened(1, 0, 3, 3) + widened(1, 1, 0, 1),
         )
@@ -499,8 +499,8 @@ def tile_finalmlptwostreamfusion_kernel(tc, x, s, w1, w2_bytes, w2_scale, r, wf,
             [(group_pool, W1[1, 1])],
         )
         stretch(
-            on_x(quant_x, (1, 0, 0), (1, 1, 0)) + [(quant_w, W2[0, 0])] + on_x(quant_x, (0, 0, 1), (0, 1, 1))
-            + [(quant_w, W2[0, 1]), unit(quant_u, 0), (quant_w, WF[0])] + on_x(quant_x, (1, 0, 1), (1, 1, 1))
+            [(quant_x, 1, 0)] + [(quant_w, W2[0, 0])] + [(quant_x, 0, 1)]
+            + [(quant_w, W2[0, 1]), unit(quant_u, 0), (quant_w, WF[0])] + [(quant_x, 1, 1)]
             + [(quant_w, W1[1, 0]), (quant_w, W1[1, 1])],
             both(mul_z1, 1) + both(mul_z2, 0) + both(mul_f, 0) + [(turn_x, 2, 1)] + both(mul_z2, 1),
             [(group_scalar, W1[1, 0], 1), (take_w, WF[0], 1)] + both(relu_z1, 0) + [(widen_a,)] + both(relu_z2, 0) + widened(1, 1, 2, 3),
@@ -512,7 +512,7 @@ def tile_finalmlptwostreamfusion_kernel(tc, x, s, w1, w2_bytes, w2_scale, r, wf,
             [(group_pool, W2[1, 0])],
         )
         stretch(
-            [unit(quant_u, 1)] + on_x(quant_x, (2, 0, 0), (2, 1, 0)) + [(quant_w, W2[1, 0])],
+            [unit(quant_u, 1)] + [(quant_x, 2, 0)] + [(quant_w, W2[1, 0])],
             both(mul_f, 1) + both(mul_z1, 4),
             both(copy_scalar, 0),
         )
@@ -523,7 +523,7 @@ def tile_finalmlptwostreamfusion_kernel(tc, x, s, w1, w2_bytes, w2_scale, r, wf,
             [(group_pool, W2[1, 1])],
         )
         stretch(
-            [unit(quant_u, 2)] + on_x(quant_x, (2, 0, 1), (2, 1, 1)) + [(quant_w, W2[1, 1])],
+            [unit(quant_u, 2)] + [(quant_x, 2, 1)] + [(quant_w, W2[1, 1])],
             on_x(turn_x, (3, 0), (3, 1)) + both(mul_z1, 5),
             both(copy_scalar, 1) + [unit(weigh_o1, 2, 0)],
         )
@@ -534,7 +534,7 @@ def tile_finalmlptwostreamfusion_kernel(tc, x, s, w1, w2_bytes, w2_scale, r, wf,
             [(group_pool, WF[1])],
         )
         stretch(
-            [unit(quant_u, 3)] + on_x(quant_x, (3, 0, 0), (3, 1, 0)) + [(quant_w, WF[1])],
+            [unit(quant_u, 3)] + [(quant_x, 3, 0)] + [(quant_w, WF[1])],
             both(mul_z2, 4) + both(mul_z2, 5),
             both(relu_z2, 3),
         )
@@ -545,7 +545,7 @@ def tile_finalmlptwostreamfusion_kernel(tc, x, s, w1, w2_bytes, w2_scale, r, wf,
             [unit(gain_pool, 4)],
         )
         stretch(
-            on_x(quant_x, (3, 0, 1), (3, 1, 1)) + [unit(quant_u, 4)],
+            [(quant_x, 3, 1)] + [unit(quant_u, 4)],
             [unit(mul_z1, 6, 0)] + both(turn_out, 2),
             [unit(weigh_o1, 5, 0), unit(relu_z1, 6, 0), unit(weigh_o1, 5, 1)],
         )
@@ -557,19 +557,19 @@ def tile_finalmlptwostreamfusion_kernel(tc, x, s, w1, w2_bytes, w2_scale, r, wf,
         )
         stretch(
             [unit(merge, 3), unit(quant_u, 7), unit(merge, 4), unit(quant_u, 5)],
-            both(mul_z2, 6) + both(turn_out, 3) + both(mul_f, 7) + both(turn_out, 4),
-            both(relu_z2, 6) + both(copy_scalar, 3) + [unit(weigh_o1, 6, 0)],
+            both(mul_z2, 6) + both(turn_out, 3) + both(mul_f, 7) + [unit(turn_out, 4, 0)],
+            both(relu_z2, 6) + both(copy_scalar, 3),
         )
         stretch(
             both(weigh_z1, 7) + both(fuse, 5) + [unit(fuse_rows, 7, 0)],
-            both(mul_f, 5) + both(open_out, 7) + [unit(open_out, 6, 0)] + both(turn_out, 5),
-            [unit(copy_scalar, 4, 0), unit(weigh_o1, 6, 1), unit(copy_scalar, 4, 1), unit(copy_scalar, 5, 0)],
+            both(mul_f, 5) + [unit(turn_out, 4, 1)] + both(open_out, 7) + both(turn_out, 5),
+            [unit(copy_scalar, 4, 0)] + both(weigh_o1, 6) + [unit(copy_scalar, 4, 1)],
             [unit(gain_pool, 6)],
         )
         stretch(
             [unit(quant_u, 6), unit(fuse_rows, 7, 1)] + both(fuse_rows, 6) + [unit(copy_vector, 6, 1)],
-            [unit(close_out, 7, 0)] + both(mul_f, 6) + [unit(close_out, 7, 1), unit(open_out, 6, 1)] + both(close_out, 6),
-            [unit(copy_scalar, 5, 1)] + both(copy_scalar, 7) + [unit(copy_scalar, 6, 0)],
+            both(mul_f, 6) + both(close_out, 7) + both(open_out, 6) + both(close_out, 6),
+            both(copy_scalar, 5) + both(copy_scalar, 7) + [unit(copy_scalar, 6, 0)],
         )
 
         def needs(fn, *args):
@@ -580,7 +580,8 @@ def tile_finalmlptwostreamfusion_kernel(tc, x, s, w1, w2_bytes, w2_scale, r, wf,
             if fn is gate_tile_x:
                 return [(turn_tile_x, *args)]
             if fn is quant_x:
-                return [(gate_x, *args) if args[0] else (gate_tile_x, TT - 1, args[1])]
+                c, stream = args
+                return [(gate_x, c, g, stream) if c else (gate_tile_x, TT - 1, g) for g in range(PASSES)]
             if fn in (mix_w, group_scalar, group_pool):
                 return [(widen_w2, *args[0][1:], 3)] if args[0][0] == "w2" else []
             if fn is take_w:
@@ -595,7 +596,7 @@ def tile_finalmlptwostreamfusion_kernel(tc, x, s, w1, w2_bytes, w2_scale, r, wf,
             weighs = both(weigh_z1 if k in VECTOR_WEIGHED else weigh_o1, k)
             if fn in (mul_z1, mul_z2):
                 weight, stream = (W1, 0) if fn is mul_z1 else (W2, 1)
-                return [(quant_w, weight[h, g]) for g in range(PASSES)] + [(quant_x, c, g, stream) for g in range(PASSES)]
+                return [(quant_w, weight[h, g]) for g in range(PASSES)] + [(quant_x, c, stream)]
             if fn is gain_z1:
                 return [(mul_z1, *args), (widen_r,)]
             if fn is relu_z1:

@@ -23,7 +23,7 @@ TB = 256
 TT = TB // P
 M = P // 2
 
-UNITS = [(0, 0), (1, 0), (0, 1), (1, 1), (2, 0), (2, 1), (3, 0), (3, 1)]
+UNITS = [(0, 0), (1, 0), (2, 0), (0, 1), (1, 1), (2, 1), (3, 0), (3, 1)]
 BANKS = 8
 MERGED = (3, 4)
 OPENED = (6, 7)
@@ -126,14 +126,13 @@ def tile_finalmlptwostreamfusion_kernel(tc, x, s, w1, w2_bytes, w2_scale, r, wf,
         load_w1(0, 0)
         load_w2(1)
         load_w1(0, 1)
-        load_x_pass(2, 0)
+        load_x(2)
         load_wf(0)
-        load_w1(1, 1)
-        load_channels(r_bf, r.rearrange("(h m c) -> m h c", h=HEADS, c=8))
         load_w1(1, 0)
-        load_channels(a_bf, a.rearrange("k (h m c) -> m (k h) c", h=HEADS, c=8))
-        load_x_pass(2, 1)
+        load_channels(r_bf, r.rearrange("(h m c) -> m h c", h=HEADS, c=8))
         load_wf(1)
+        load_channels(a_bf, a.rearrange("k (h m c) -> m (k h) c", h=HEADS, c=8))
+        load_w1(1, 1)
         load_x(3)
 
         sig = keep.tile([P, 2 * PASSES, 4], F32, name="sig")
@@ -473,7 +472,7 @@ def tile_finalmlptwostreamfusion_kernel(tc, x, s, w1, w2_bytes, w2_scale, r, wf,
             return [(fn, *part) for part in parts]
 
         MIXED = [(piece, half) for piece in (W2[0, 0], W2[0, 1], WF[0]) for half in range(2)] + [(W1[0, 1], 1)]
-        POOLED = (W1[0, 0], W1[0, 1], W1[1, 1], W2[1, 0], W2[1, 1], WF[1])
+        POOLED = (W1[0, 0], W1[0, 1], W1[1, 0], W1[1, 1], W2[1, 0], W2[1, 1])
         POOL_GAINED = (4, 5, 6)
         VECTOR_WEIGHED = (7,)
         stretches = []
@@ -488,71 +487,70 @@ def tile_finalmlptwostreamfusion_kernel(tc, x, s, w1, w2_bytes, w2_scale, r, wf,
             [(group_pool, W1[0, 0]), (group_pool, W1[0, 1])],
         )
         stretch(
-            [(quant_x, 0, 0)] + [(quant_w, W1[0, 0]), (quant_w, W1[0, 1])],
-            both(mix_w, W2[0, 1]),
+            [(quant_x, 0, 0), (quant_w, W1[0, 0]), (quant_w, W1[0, 1])],
+            [(mix_w, W2[0, 1], 0), (turn_x, 2, 1)],
             [(take_w, W2[0, 0], 1)] + widened(1, 0, 3, 3) + widened(1, 1, 0, 1),
         )
         stretch(
-            on_x(gate_x, (2, 0, 0), (2, 0, 1)) + both(gain_z1, 0),
-            both(mul_z1, 0) + both(mix_w, WF[0]),
-            both(take_w, W2[0, 1]) + [(widen_r,), (group_scalar, W1[1, 0], 0), (take_w, WF[0], 0)],
+            on_x(gate_x, (2, 0, 0), (2, 1, 0)) + both(gain_z1, 0),
+            both(mul_z1, 0) + [(mix_w, W2[0, 1], 1)] + both(mix_w, WF[0]),
+            [(take_w, W2[0, 1], 0), (widen_r,)] + widened(1, 1, 2, 3) + [(group_scalar, WF[1], 0), (take_w, W2[0, 1], 1)],
+            [(group_pool, W1[1, 0])],
+        )
+        stretch(
+            [(quant_x, 1, 0), (quant_w, W2[0, 0]), (quant_x, 0, 1), (quant_w, W2[0, 1]), unit(quant_u, 0), (quant_x, 1, 1)]
+            + [(quant_w, WF[0]), (quant_x, 2, 0), (quant_w, W1[1, 0])],
+            both(mul_z1, 1) + both(mul_z2, 0) + both(mul_f, 0) + both(mul_z2, 1),
+            both(relu_z1, 0) + both(take_w, WF[0]) + [(widen_a,)] + both(relu_z2, 0) + both(weigh_o1, 0),
+        )
+        stretch(
+            both(fuse, 0) + both(gain_z1, 1) + [(gate_x, 2, 0, 1)],
+            both(mul_z1, 2) + both(turn_out, 0),
+            both(relu_z2, 1) + both(relu_z1, 1),
             [(group_pool, W1[1, 1])],
         )
         stretch(
-            [(quant_x, 1, 0)] + [(quant_w, W2[0, 0])] + [(quant_x, 0, 1)]
-            + [(quant_w, W2[0, 1]), unit(quant_u, 0), (quant_w, WF[0])] + [(quant_x, 1, 1)]
-            + [(quant_w, W1[1, 0]), (quant_w, W1[1, 1])],
-            both(mul_z1, 1) + both(mul_z2, 0) + both(mul_f, 0) + [(turn_x, 2, 1)] + both(mul_z2, 1),
-            [(group_scalar, W1[1, 0], 1), (take_w, WF[0], 1)] + both(relu_z1, 0) + [(widen_a,)] + both(relu_z2, 0) + widened(1, 1, 2, 3),
-        )
-        stretch(
-            both(fuse, 0) + both(gain_z1, 1) + [(gate_x, 2, 1, 0)],
-            both(mul_z1, 2) + both(turn_out, 0),
-            both(weigh_o1, 0) + both(relu_z2, 1) + both(relu_z1, 1),
-            [(group_pool, W2[1, 0])],
-        )
-        stretch(
-            [unit(quant_u, 1)] + [(quant_x, 2, 0)] + [(quant_w, W2[1, 0])],
-            both(mul_f, 1) + both(mul_z1, 4),
+            [unit(quant_u, 1), (quant_w, W1[1, 1])],
+            both(mul_f, 1),
             both(copy_scalar, 0),
         )
         stretch(
-            both(fuse, 1) + both(gain_z1, 2) + [(gate_x, 2, 1, 1)],
-            both(mul_z1, 3) + both(turn_out, 1),
-            both(weigh_o1, 1) + both(relu_z1, 4) + both(relu_z1, 2),
-            [(group_pool, W2[1, 1])],
+            both(gain_z1, 2) + both(fuse, 1) + [(gate_x, 2, 1, 1)],
+            both(mul_z1, 4) + [unit(mul_z1, 3, 0)] + both(turn_out, 1) + [unit(mul_z1, 3, 1)],
+            both(weigh_o1, 1) + both(relu_z1, 2) + both(relu_z1, 4),
+            [(group_pool, W2[1, 0])],
         )
         stretch(
-            [unit(quant_u, 2)] + [(quant_x, 2, 1)] + [(quant_w, W2[1, 1])],
-            on_x(turn_x, (3, 0), (3, 1)) + both(mul_z1, 5),
-            both(copy_scalar, 1) + [unit(weigh_o1, 2, 0)],
+            [unit(quant_u, 2), (quant_x, 2, 1), (quant_w, W2[1, 0])],
+            on_x(turn_x, (3, 0), (3, 1)) + both(mul_f, 2),
+            both(copy_scalar, 1) + [(group_scalar, WF[1], 1)],
         )
         stretch(
             both(gain_z1, 3) + on_x(gate_x, (3, 0, 0), (3, 1, 0)),
-            both(mul_z2, 2) + both(mul_z2, 3),
-            both(relu_z1, 5) + both(relu_z1, 3) + both(relu_z2, 2),
-            [(group_pool, WF[1])],
+            both(mul_z2, 2) + both(mul_z1, 5),
+            both(relu_z1, 3) + both(relu_z2, 2),
+            [(group_pool, W2[1, 1])],
         )
         stretch(
-            [unit(quant_u, 3)] + [(quant_x, 3, 0)] + [(quant_w, WF[1])],
-            both(mul_z2, 4) + both(mul_z2, 5),
-            both(relu_z2, 3),
+            [unit(quant_u, 3), (quant_x, 3, 0), (quant_w, WF[1]), (quant_w, W2[1, 1])],
+            both(mul_z1, 6),
+            both(relu_z1, 5) + [unit(weigh_o1, 2, 0)],
         )
         stretch(
-            on_x(gate_x, (3, 0, 1), (3, 1, 1)) + both(fuse, 2),
-            both(mul_f, 2) + both(mul_f, 3) + both(mul_z1, 7),
-            both(relu_z2, 4) + both(relu_z2, 5) + [unit(weigh_o1, 2, 1)],
+            [(gate_x, 3, 0, 1)] + both(fuse, 2) + [(gate_x, 3, 1, 1)],
+            both(mul_z2, 3) + both(mul_f, 3) + both(turn_out, 2) + both(mul_z1, 7),
+            both(relu_z1, 6) + [unit(weigh_o1, 2, 1)] + both(relu_z2, 3),
             [unit(gain_pool, 4)],
         )
         stretch(
-            [(quant_x, 3, 1)] + [unit(quant_u, 4)],
-            [unit(mul_z1, 6, 0)] + both(turn_out, 2),
-            [unit(weigh_o1, 5, 0), unit(relu_z1, 6, 0), unit(weigh_o1, 5, 1)],
+            [(quant_x, 3, 1), unit(quant_u, 4)],
+            both(mul_z2, 4),
+            both(copy_scalar, 2) + [unit(weigh_o1, 5, 0)],
         )
         stretch(
             both(fuse, 3) + both(gain_z1, 7) + both(fuse, 4),
-            both(mul_f, 4) + [unit(mul_z1, 6, 1)] + both(mul_z2, 7),
-            both(copy_scalar, 2) + [unit(relu_z1, 6, 1)] + both(relu_z2, 7),
+            both(mul_f, 4) + both(mul_z2, 5) + both(mul_z2, 7),
+            both(relu_z2, 4) + [unit(weigh_o1, 5, 1)] + both(relu_z2, 5) + both(relu_z2, 7),
             [unit(gain_pool, 5)],
         )
         stretch(

@@ -127,8 +127,8 @@ def tile_finalmlptwostreamfusion_kernel(tc, x, s, w1, w2_bytes, w2_scale, r, wf,
         load_w2(1)
         load_w1(0, 1)
         load_x(2)
-        load_wf(0)
         load_w1(1, 0)
+        load_wf(0)
         load_channels(r_bf, r.rearrange("(h m c) -> m h c", h=HEADS, c=8))
         load_wf(1)
         load_channels(a_bf, a.rearrange("k (h m c) -> m (k h) c", h=HEADS, c=8))
@@ -249,8 +249,8 @@ def tile_finalmlptwostreamfusion_kernel(tc, x, s, w1, w2_bytes, w2_scale, r, wf,
             )
             give_back(("mix", piece, half))
 
-        def group_scalar(piece, half):
-            pairs = slice(half * M // 2, (half + 1) * M // 2)
+        def group_scalar(piece, quarter):
+            pairs = slice(quarter * M // 4, (quarter + 1) * M // 4)
             nc.scalar.copy(
                 out=staged(piece).rearrange("p (t m e j) -> p m t j e", t=4, e=2, j=4)[:, pairs],
                 in_=rows4[piece][:].rearrange("p j (m t e) -> p m t j e", e=2, t=4)[:, pairs],
@@ -501,12 +501,12 @@ def tile_finalmlptwostreamfusion_kernel(tc, x, s, w1, w2_bytes, w2_scale, r, wf,
             [(quant_x, 1, 0), (quant_w, W2[0, 0]), (quant_x, 0, 1), (quant_w, W2[0, 1]), unit(quant_u, 0), (quant_x, 1, 1)]
             + [(quant_w, WF[0]), (quant_x, 2, 0), (quant_w, W1[1, 0])],
             both(mul_z1, 1) + both(mul_z2, 0) + both(mul_f, 0) + both(mul_z2, 1),
-            both(relu_z1, 0) + both(take_w, WF[0]) + [(widen_a,)] + both(relu_z2, 0) + both(weigh_o1, 0),
+            both(relu_z1, 0) + both(take_w, WF[0]) + [(widen_a,), (group_scalar, WF[1], 1), unit(weigh_o1, 0, 0)] + both(relu_z2, 0) + [unit(weigh_o1, 0, 1)],
         )
         stretch(
             both(fuse, 0) + both(gain_z1, 1) + [(gate_x, 2, 0, 1)],
-            both(mul_z1, 2) + both(turn_out, 0),
-            both(relu_z2, 1) + both(relu_z1, 1),
+            both(mul_z1, 2) + both(turn_out, 0) + [(turn_x, 3, 0)],
+            both(relu_z2, 1) + both(relu_z1, 1) + [(group_scalar, WF[1], 2)],
             [(group_pool, W1[1, 1])],
         )
         stretch(
@@ -515,42 +515,42 @@ def tile_finalmlptwostreamfusion_kernel(tc, x, s, w1, w2_bytes, w2_scale, r, wf,
             both(copy_scalar, 0),
         )
         stretch(
-            both(gain_z1, 2) + both(fuse, 1) + [(gate_x, 2, 1, 1)],
-            both(mul_z1, 4) + [unit(mul_z1, 3, 0)] + both(turn_out, 1) + [unit(mul_z1, 3, 1)],
-            both(weigh_o1, 1) + both(relu_z1, 2) + both(relu_z1, 4),
+            [(gate_x, 2, 1, 1)] + both(fuse, 1) + both(gain_z1, 2),
+            both(mul_z1, 4) + both(mul_z1, 3) + both(turn_out, 1),
+            both(weigh_o1, 1) + both(relu_z1, 4) + [(group_scalar, WF[1], 3)] + both(relu_z1, 2),
             [(group_pool, W2[1, 0])],
         )
         stretch(
-            [unit(quant_u, 2), (quant_x, 2, 1), (quant_w, W2[1, 0])],
-            on_x(turn_x, (3, 0), (3, 1)) + both(mul_f, 2),
-            both(copy_scalar, 1) + [(group_scalar, WF[1], 1)],
+            [(quant_x, 2, 1), unit(quant_u, 2), (quant_w, W2[1, 0])],
+            both(mul_z2, 2),
+            both(copy_scalar, 1),
         )
         stretch(
-            both(gain_z1, 3) + on_x(gate_x, (3, 0, 0), (3, 1, 0)),
-            both(mul_z2, 2) + both(mul_z1, 5),
-            both(relu_z1, 3) + both(relu_z2, 2),
+            both(gain_z1, 3) + [(gate_x, 3, 0, 0)] + both(fuse, 2),
+            both(mul_f, 2) + both(mul_z1, 5) + [(turn_x, 3, 1)],
+            both(relu_z2, 2) + both(weigh_o1, 2),
             [(group_pool, W2[1, 1])],
         )
         stretch(
-            [unit(quant_u, 3), (quant_x, 3, 0), (quant_w, WF[1]), (quant_w, W2[1, 1])],
-            both(mul_z1, 6),
-            both(relu_z1, 5) + [unit(weigh_o1, 2, 0)],
+            [unit(quant_u, 3), (quant_w, WF[1]), (quant_w, W2[1, 1])],
+            both(turn_out, 2),
+            both(relu_z1, 3) + both(relu_z1, 5),
         )
         stretch(
-            [(gate_x, 3, 0, 1)] + both(fuse, 2) + [(gate_x, 3, 1, 1)],
-            both(mul_z2, 3) + both(mul_f, 3) + both(turn_out, 2) + both(mul_z1, 7),
-            both(relu_z1, 6) + [unit(weigh_o1, 2, 1)] + both(relu_z2, 3),
+            on_x(gate_x, (3, 1, 0), (3, 0, 1), (3, 1, 1)),
+            both(mul_f, 3) + both(mul_z2, 3) + both(mul_z2, 4) + both(mul_z2, 5),
+            both(copy_scalar, 2) + both(relu_z2, 3) + both(relu_z2, 4) + [unit(weigh_o1, 5, 0)],
             [unit(gain_pool, 4)],
         )
         stretch(
-            [(quant_x, 3, 1), unit(quant_u, 4)],
-            both(mul_z2, 4),
-            both(copy_scalar, 2) + [unit(weigh_o1, 5, 0)],
+            [(quant_x, 3, 0), (quant_x, 3, 1), unit(quant_u, 4)],
+            both(mul_z1, 7),
+            [unit(weigh_o1, 5, 1)] + both(relu_z2, 5),
         )
         stretch(
             both(fuse, 3) + both(gain_z1, 7) + both(fuse, 4),
-            both(mul_f, 4) + both(mul_z2, 5) + both(mul_z2, 7),
-            both(relu_z2, 4) + [unit(weigh_o1, 5, 1)] + both(relu_z2, 5) + both(relu_z2, 7),
+            both(mul_f, 4) + both(mul_z1, 6) + both(mul_z2, 7),
+            both(relu_z1, 6) + both(relu_z2, 7),
             [unit(gain_pool, 5)],
         )
         stretch(
@@ -566,7 +566,7 @@ def tile_finalmlptwostreamfusion_kernel(tc, x, s, w1, w2_bytes, w2_scale, r, wf,
         )
         stretch(
             [unit(quant_u, 6), unit(fuse_rows, 7, 1)] + both(fuse_rows, 6) + [unit(copy_vector, 6, 1)],
-            both(mul_f, 6) + both(close_out, 7) + both(open_out, 6) + both(close_out, 6),
+            [unit(close_out, 7, 0)] + both(mul_f, 6) + [unit(close_out, 7, 1), unit(open_out, 6, 0), unit(close_out, 6, 0), unit(open_out, 6, 1), unit(close_out, 6, 1)],
             both(copy_scalar, 5) + both(copy_scalar, 7) + [unit(copy_scalar, 6, 0)],
         )
 
@@ -588,7 +588,7 @@ def tile_finalmlptwostreamfusion_kernel(tc, x, s, w1, w2_bytes, w2_scale, r, wf,
                 halves = [(take_w if (*args, half) in MIXED else group_scalar, *args, half) for half in range(2)]
                 if args[0] in POOLED:
                     return [(group_pool, *args)] + [stage for stage in halves if stage[0] is take_w]
-                return halves
+                return halves if (*args, 0) in MIXED else [(group_scalar, *args, quarter) for quarter in range(4)]
             c, h = args[:2]
             k = UNITS.index((c, h))
             weighs = both(weigh_z1 if k in VECTOR_WEIGHED else weigh_o1, k)
@@ -626,7 +626,7 @@ def tile_finalmlptwostreamfusion_kernel(tc, x, s, w1, w2_bytes, w2_scale, r, wf,
         def banks_wanted(fn, *args):
             return 1 if fn in (turn_x, turn_tile_x, mix_w, mul_z1, mul_z2, mul_f, turn_out, open_out) else 0
 
-        long_stages = (gate_x, gate_tile_x, merge, group_scalar, mix_w)
+        long_stages = (gate_x, gate_tile_x, merge, mix_w)
         done = set()
         rested = set()
         for programs in stretches:

from contextlib import ExitStack

import concourse.mybir as mybir
from concourse.masks import make_identity

F32 = mybir.dt.float32
BF16 = mybir.dt.bfloat16
U32 = mybir.dt.uint32
U8 = mybir.dt.uint8
FP8 = mybir.dt.float8_e4m3fn
X4 = mybir.dt.float8_e4m3fn_x4
ALU = mybir.AluOpType
ACT = mybir.ActivationFunctionType

B, D, HEADS, W = 1024, 1024, 2, 512
H = HEADS * W
FLOPS = 2 * (2 * B * D * H + HEADS * B * W * W)

P = 128
KP = 4 * P
PASSES = D // KP
TB = 256
TT = TB // P
M = P // 2

UNITS = [(0, 0), (1, 0), (2, 0), (0, 1), (1, 1), (2, 1), (3, 0), (3, 1)]
BANKS = 8
MERGED = (3, 4)
OPENED = (6, 7)

XG_BUFS, WIDE_BUFS, WG_BUFS, UG_BUFS, O_BUFS, FUSED_BUFS, ROW_BUFS = 5, 3, 4, 2, 5, 3, 6


def tile_finalmlptwostreamfusion_kernel(tc, x, s, w1, w2_bytes, w2_scale, r, wf, a, out):
    nc = tc.nc
    with ExitStack() as ctx:
        keep = ctx.enter_context(tc.tile_pool(name="keep", bufs=1))
        work = ctx.enter_context(tc.tile_pool(name="work", bufs=1))
        psum = ctx.enter_context(tc.psum_pool(name="psum", bufs=1))
        free_banks = list(range(BANKS))
        held = {}

        def bank_for(key, shape, dtype):
            held[key] = free_banks.pop(0)
            return psum.tile(shape, dtype, name="bank%d" % held[key])

        asked = {}

        def buffer(name, shape, dtype, count):
            asked[name] = asked.get(name, -1) + 1
            return work.tile(shape, dtype, name="%s%d" % (name, asked[name] % count), bufs=1, align_bytes=64)

        def give_back(key):
            free_banks.append(held.pop(key))

        ident = keep.tile([P, P], F32, name="ident")
        make_identity(nc, ident[:])

        ctx.enter_context(tc.manual_schedule())

        s_bf = keep.tile([P, 2 * PASSES, 4], BF16, name="s_bf")
        ws = keep.tile([P, PASSES, 4], F32, name="ws")
        r_bf = keep.tile([P, HEADS, 8], BF16, name="r_bf")
        a_bf = keep.tile([P, 2 * HEADS, 8], BF16, name="a_bf")
        x_part = {}
        w2_raw = {}
        rows4 = {}

        def load_x_first():
            for g in range(PASSES):
                first = keep.tile([P, KP], BF16, name="x_first%d" % g)
                nc.sync.dma_start(out=first[:], in_=x[0:P, g * KP : (g + 1) * KP])
                x_part[0, 0, g] = first[:]
            second = keep.tile([P, D], BF16, name="x_second")
            nc.sync.dma_start(out=second[:], in_=x[P:TB, :])
            for g in range(PASSES):
                x_part[0, 1, g] = second[:, g * KP : (g + 1) * KP]

        def load_x(c):
            rows_c = keep.tile([P, TT * D], BF16, name="x_raw%d" % c)
            nc.sync.dma_start(
                out=rows_c[:].rearrange("p (i k) -> p i k", i=TT),
                in_=x[c * TB : (c + 1) * TB, :].rearrange("(i p) k -> p i k", p=P),
            )
            for i in range(TT):
                for g in range(PASSES):
                    x_part[c, i, g] = rows_c[:, i * D + g * KP : i * D + (g + 1) * KP]

        def load_x_pass(c, g):
            rows_cg = keep.tile([P, TT * KP], BF16, name="x_raw%d_%d" % (c, g))
            nc.sync.dma_start(
                out=rows_cg[:].rearrange("p (i k) -> p i k", i=TT),
                in_=x[c * TB : (c + 1) * TB, g * KP : (g + 1) * KP].rearrange("(i p) k -> p i k", p=P),
            )
            for i in range(TT):
                x_part[c, i, g] = rows_cg[:, i * KP : (i + 1) * KP]

        def load_w1(h, g):
            rows4["w1", h, g] = keep.tile([P, 4, W], BF16, name="w1_raw%d_%d" % (h, g))
            nc.sync.dma_start(
                out=rows4["w1", h, g][:],
                in_=w1[g * KP : (g + 1) * KP, h * W : (h + 1) * W].rearrange("(p j) n -> p j n", j=4),
            )

        def load_w2(g):
            raw = keep.tile([P, 4, H], U8, name="w2_raw%d" % g)
            nc.sync.dma_start(out=raw[:], in_=w2_bytes[g * KP : (g + 1) * KP, :].rearrange("(p j) n -> p j n", j=4))
            for h in range(HEADS):
                w2_raw[h, g] = raw[:, :, h * W : (h + 1) * W]

        def load_wf(h):
            rows4["wf", h, 0] = keep.tile([P, 4, W], BF16, name="wf_raw%d" % h)
            rows = wf[h].rearrange("(m t e) n -> e m t n", t=4, e=2)
            for e in range(2):
                nc.sync.dma_start(out=rows4["wf", h, 0][e::2, :, :], in_=rows[e])

        def load_channels(dst, src):
            for e in range(2):
                nc.sync.dma_start(out=dst[e::2, :, 0:7], in_=src[:, :, e : e + 7])

        nc.scalar.dma_start(out=s_bf[:], in_=s.rearrange("k (g p t) -> p (k g) t", p=P, t=4))
        load_x_first()
        nc.scalar.dma_start(out=ws[:], in_=w2_scale.rearrange("(g p t) o -> p g (t o)", p=P, t=4))
        load_w2(0)
        load_x(1)
        load_w1(0, 0)
        load_w2(1)
        load_w1(0, 1)
        load_x(2)
        load_w1(1, 0)
        load_wf(0)
        load_channels(r_bf, r.rearrange("(h m c) -> m h c", h=HEADS, c=8))
        load_wf(1)
        load_channels(a_bf, a.rearrange("k (h m c) -> m (k h) c", h=HEADS, c=8))
        load_w1(1, 1)
        load_x(3)

        sig = keep.tile([P, 2 * PASSES, 4], F32, name="sig")
        nc.scalar.activation(out=sig[:], in_=s_bf[:], func=ACT.Sigmoid)
        gates = keep.tile([P, 2 * PASSES, 4], F32, name="gates")
        nc.vector.tensor_scalar(out=gates[:], in0=sig[:], scalar1=2.0, scalar2=None, op0=ALU.mult)
        ident_bf = keep.tile([P, P], BF16, name="ident_bf")
        nc.scalar.copy(out=ident_bf[:], in_=ident[:])
        r_f = keep.tile([P, HEADS, 4], F32, name="r_f")
        a_f = keep.tile([P, 2 * HEADS, 4], F32, name="a_f")

        def widen_r():
            nc.scalar.copy(out=r_f[:], in_=r_bf[:, :, 0:7:2])

        def widen_a():
            nc.scalar.copy(out=a_f[:], in_=a_bf[:, :, 0:7:2])

        def quantize(grouped, columns, name):
            codes = keep.tile([P, columns], U32, name=name + "_c", align_bytes=64)
            scales = keep.tile([P, columns], U8, name=name + "_s", align_bytes=64)
            nc.vector.quantize_mx(out=codes[:].bitcast(X4), scales=scales[:], in_=grouped)
            return codes, scales

        def mx(dst, weight, t, moving, n0, n, start, stop):
            nc.tensor.matmul_mx(
                out=dst,
                lhsT=weight[0][:, t * P : (t + 1) * P].bitcast(X4),
                lhsT_scale=weight[1][:, t * P : (t + 1) * P],
                rhs=moving[0][:, n0 : n0 + n].bitcast(X4),
                rhs_scale=moving[1][:, n0 : n0 + n],
                start=start,
                stop=stop,
            )

        xt = {}
        xg = {}
        free_gated = list(range(XG_BUFS))
        gated_in = {}
        g_q = {}

        def turn_x(c, g):
            xt[c, g] = bank_for(("x", c, g), [P, 2, TB], F32)
            for u in range(2):
                for i in range(TT):
                    words = x_part[c, i, g].bitcast(F32)
                    nc.tensor.transpose(xt[c, g][:, u, i * P : (i + 1) * P], words[:, u::2], ident[:])

        def turn_tile_x(i, g):
            xt[0, g, i] = bank_for(("x", 0, g, i), [P, 2, P], F32)
            for u in range(2):
                nc.tensor.transpose(xt[0, g, i][:, u, :], x_part[0, i, g].bitcast(F32)[:, u::2], ident[:])

        def gate(c, g, stream, bank, n0, n):
            if (c, stream) not in xg:
                gated_in[c, stream] = free_gated.pop(0)
                name = "xg%d" % gated_in[c, stream]
                xg[c, stream] = work.tile([P, PASSES, TB, 4], BF16, name=name, bufs=1, align_bytes=64)
            factor = gates[:, PASSES * stream + g, :].rearrange("p (u e) -> p u e", e=2).unsqueeze(1)
            nc.vector.tensor_tensor(
                out=xg[c, stream][:, g, n0 : n0 + n, :].rearrange("p n (u e) -> p n u e", e=2),
                in0=bank[:].bitcast(BF16).rearrange("p u (n e) -> p n u e", e=2),
                in1=factor.to_broadcast([P, n, 2, 2]),
                op=ALU.mult,
            )

        def gate_x(c, g, stream):
            gate(c, g, stream, xt[c, g], 0, TB)
            if stream == 1:
                give_back(("x", c, g))

        def gate_tile_x(i, g):
            for stream in range(2):
                gate(0, g, stream, xt[0, g, i], i * P, P)
            give_back(("x", 0, g, i))

        def quant_x(c, stream):
            grouped = xg[c, stream][:].rearrange("p g n j -> p (g n j)")
            g_q[c, stream] = quantize(grouped, PASSES * TB, "g%dq%d" % (stream, c))
            free_gated.append(gated_in[c, stream])

        mixed = {}
        wg = {}
        w_q = {}

        def widen_w2(h, g, j):
            if j == 0:
                rows4["w2", h, g] = buffer("wide", [P, 4, W], BF16, WIDE_BUFS)
            nc.scalar.activation(
                out=rows4["w2", h, g][:, j, :],
                in_=w2_raw[h, g][:, j, :].bitcast(FP8),
                func=ACT.Copy,
                scale=ws[:, g, j : j + 1],
            )

        def mix_w(piece, half):
            bank = bank_for(("mix", piece, half), [P, 2, P, 4], BF16)
            for v in range(2):
                n0 = (2 * half + v) * P
                dst = bank[:, v, :, :].rearrange("p n j -> p j n")
                nc.tensor.matmul(dst, lhsT=ident_bf[:], rhs=rows4[piece][:, :, n0 : n0 + P], start=True, stop=True)
            mixed[piece, half] = bank

        def staged(piece):
            if piece not in wg:
                wg[piece] = buffer("wg", [P, 4 * W], BF16, WG_BUFS)
            return wg[piece][:]

        def take_w(piece, half):
            dst = staged(piece).bitcast(F32).rearrange("p (t m v) -> p t m v", t=4, v=4)
            src = mixed[piece, half][:].rearrange("p a n j -> p (a n j)").bitcast(F32)
            nc.scalar.copy(
                out=dst[:, :, half * M // 2 : (half + 1) * M // 2, :],
                in_=src.rearrange("p (m t v) -> p t m v", t=4, v=4),
            )
            give_back(("mix", piece, half))

        def group_scalar(piece, quarter):
            pairs = slice(quarter * M // 4, (quarter + 1) * M // 4)
            nc.scalar.copy(
                out=staged(piece).rearrange("p (t m e j) -> p m t j e", t=4, e=2, j=4)[:, pairs],
                in_=rows4[piece][:].rearrange("p j (m t e) -> p m t j e", e=2, t=4)[:, pairs],
            )

        def group_pool(piece):
            name = "wg_pool1" if piece == POOLED[0] else "wg_pool0"
            wg[piece] = work.tile([P, 4 * W], BF16, name=name, bufs=1, align_bytes=64)
            pairs = slice(0, M // 2 if (piece, 1) in MIXED else M)
            nc.gpsimd.tensor_scalar(
                out=wg[piece][:].rearrange("p (t m e j) -> p m t e j", t=4, e=2, j=4)[:, pairs],
                in0=rows4[piece][:].rearrange("p j (m t e) -> p m t e j", t=4, e=2)[:, pairs],
                scalar1=1.0,
                scalar2=0.0,
                op0=ALU.mult,
                op1=ALU.add,
            )

        def quant_w(piece):
            w_q[piece] = quantize(wg[piece][:], W, "%sq%d_%d" % piece)

        z1 = {}
        ug = {}
        o1 = {}
        u_q = {}
        weighed = {}

        def pooled(c, h):
            return UNITS.index((c, h)) in POOL_GAINED

        def mul_z1(c, h, n):
            if pooled(c, h):
                z1[c, h, n] = bank_for(("z1", c, h, n), [P, 2, TB], F32)
                parts = [(z1[c, h, n][:, v, :], 2 * n + v, 0, TB) for v in range(2)]
            else:
                z1[c, h, n] = bank_for(("z1", c, h, n), [P, 4, P], F32)
                parts = [(z1[c, h, n][:, t, :], t, n * P, P) for t in range(4)]
            for dst, t, n0, tokens in parts:
                for g in range(PASSES):
                    mx(dst, w_q["w1", h, g], t, g_q[c, 0], g * TB + n0, tokens, g == 0, g == PASSES - 1)

        def gain_z1(c, h, i):
            if i == 0:
                ug[c, h] = buffer("ug", [P, TT, P, 4], BF16, UG_BUFS)
            nc.vector.scalar_tensor_tensor(
                out=ug[c, h][:, i, :, :],
                in0=z1[c, h, i][:].rearrange("p t n -> p n t"),
                scalar=0.0,
                in1=r_f[:, h, :].unsqueeze(1).to_broadcast([P, P, 4]),
                op0=ALU.max,
                op1=ALU.mult,
            )

        def relu_z1(c, h, n):
            if n == 0:
                o1[c, h] = buffer("o1", [P, 4, TB], F32, O_BUFS)
            dst = o1[c, h][:, 2 * n : 2 * n + 2, :] if pooled(c, h) else o1[c, h][:, :, n * P : (n + 1) * P]
            nc.scalar.activation(out=dst, in_=z1[c, h, n][:], func=ACT.Relu)
            give_back(("z1", c, h, n))

        def gain_pool(c, h):
            ug[c, h] = work.tile([P, TT, P, 4], BF16, name="wg_pool0", bufs=1, align_bytes=64)
            nc.gpsimd.tensor_tensor(
                out=ug[c, h][:].rearrange("p i n t -> p (i n) t"),
                in0=o1[c, h][:].rearrange("p t n -> p n t"),
                in1=r_f[:, h, :].unsqueeze(1).to_broadcast([P, TB, 4]),
                op=ALU.mult,
            )

        def weigh_o1(c, h, pair):
            if pair == 0:
                weighed[c, h] = buffer("weighed", [P, 4, TB], F32, 2) if pooled(c, h) else o1[c, h]
            for t in (2 * pair, 2 * pair + 1):
                nc.scalar.activation(
                    out=weighed[c, h][:, t, :], in_=o1[c, h][:, t, :], func=ACT.Copy, scale=a_f[:, h, t : t + 1]
                )

        def weigh_z1(c, h, i):
            if i == 0:
                weighed[c, h] = buffer("o1", [P, 4, TB], F32, O_BUFS)
            nc.vector.scalar_tensor_tensor(
                out=weighed[c, h][:, :, i * P : (i + 1) * P],
                in0=z1[c, h, i][:],
                scalar=0.0,
                in1=a_f[:, h, :].unsqueeze(2).to_broadcast([P, 4, P]),
                op0=ALU.max,
                op1=ALU.mult,
            )
            give_back(("z1", c, h, i))

        def quant_u(c, h):
            u_q[c, h] = quantize(ug[c, h][:].rearrange("p i n t -> p (i n t)"), TB, "uq%d_%d" % (c, h))

        z2 = {}
        o2 = {}
        fb = {}
        fused = {}

        def mul_z2(c, h, pair):
            z2[c, h, pair] = bank_for(("z2", c, h, pair), [P, 2, TB], F32)
            for v in range(2):
                for g in range(PASSES):
                    dst = z2[c, h, pair][:, v, :]
                    mx(dst, w_q["w2", h, g], 2 * pair + v, g_q[c, 1], g * TB, TB, g == 0, g == PASSES - 1)

        def relu_z2(c, h, pair):
            if pair == 0:
                o2[c, h] = buffer("o2", [P, 4, TB], F32, O_BUFS)
            nc.scalar.activation(out=o2[c, h][:, 2 * pair : 2 * pair + 2, :], in_=z2[c, h, pair][:], func=ACT.Relu)
            give_back(("z2", c, h, pair))

        def mul_f(c, h, pair):
            fb[c, h, pair] = bank_for(("f", c, h, pair), [P, 2, TB], F32)
            for v in range(2):
                mx(fb[c, h, pair][:, v, :], w_q["wf", h, 0], 2 * pair + v, u_q[c, h], 0, TB, True, True)

        def fuse(c, h, pair):
            if pair == 0:
                fused[c, h] = buffer("fused", [P, 4, TB], F32, FUSED_BUFS)
            for v in range(2):
                t = 2 * pair + v
                nc.vector.scalar_tensor_tensor(
                    out=fused[c, h][:, t, :],
                    in0=fb[c, h, pair][:, v, :],
                    scalar=a_f[:, HEADS + h, t : t + 1],
                    in1=o2[c, h][:, t, :],
                    op0=ALU.add,
                    op1=ALU.mult,
                )
            give_back(("f", c, h, pair))

        def fuse_rows(c, h, i):
            if i == 0:
                fused[c, h] = buffer("fused", [P, 4, TB], F32, FUSED_BUFS)
            tokens = slice(i * P, (i + 1) * P)
            for t in range(4):
                nc.vector.scalar_tensor_tensor(
                    out=fused[c, h][:, t, tokens],
                    in0=fb[c, h, t // 2][:, t % 2, tokens],
                    scalar=a_f[:, HEADS + h, t : t + 1],
                    in1=o2[c, h][:, t, tokens],
                    op0=ALU.add,
                    op1=ALU.mult,
                )
                if i == TT - 1 and t % 2 == 1:
                    give_back(("f", c, h, t // 2))

        def merge(c, h):
            for t in range(4):
                nc.vector.scalar_tensor_tensor(
                    out=fused[c, h][:, t, :],
                    in0=o1[c, h][:, t, :],
                    scalar=a_f[:, h, t : t + 1],
                    in1=fused[c, h][:, t, :],
                    op0=ALU.mult,
                    op1=ALU.add,
                )

        tr = {}

        def turn_tile(term, c, h, i, t, start, stop):
            nc.tensor.matmul(
                tr[c, h, i][:, :, t, :],
                lhsT=term[c, h][:, t, i * P : (i + 1) * P],
                rhs=ident[:],
                start=start,
                stop=stop,
                is_transpose=True,
            )

        def turn_out(c, h, i):
            terms = (fused,) if UNITS.index((c, h)) in MERGED else (weighed, fused)
            tr[c, h, i] = bank_for(("out", c, h, i), [P, M, 4, 2], F32)
            for t in range(4):
                for n, term in enumerate(terms):
                    turn_tile(term, c, h, i, t, n == 0, n == len(terms) - 1)

        def open_out(c, h, i):
            tr[c, h, i] = bank_for(("out", c, h, i), [P, M, 4, 2], F32)
            for t in range(4):
                turn_tile(weighed, c, h, i, t, t == 0, False)

        def close_out(c, h, i):
            for t in range(4):
                turn_tile(fused, c, h, i, t, False, t == 3)

        rows = {}

        def copy_out(c, h, i, copy):
            rows[c, h, i] = buffer("rows", [P, W], F32, ROW_BUFS)
            copy(out=rows[c, h, i][:], in_=tr[c, h, i][:].rearrange("n m t e -> n (m t e)"))
            give_back(("out", c, h, i))

        def copy_scalar(c, h, i):
            copy_out(c, h, i, nc.scalar.copy)

        def copy_vector(c, h, i):
            copy_out(c, h, i, nc.vector.tensor_copy)

        def store(c, h, i):
            n0 = c * TB + i * P
            nc.sync.dma_start(out=out[n0 : n0 + P, h * W : (h + 1) * W], in_=rows[c, h, i][:])

        W1 = {(h, g): ("w1", h, g) for h in range(HEADS) for g in range(PASSES)}
        W2 = {(h, g): ("w2", h, g) for h in range(HEADS) for g in range(PASSES)}
        WF = {h: ("wf", h, 0) for h in range(HEADS)}

        def unit(fn, k, *rest):
            return (fn, *UNITS[k], *rest)

        def both(fn, *what):
            args = UNITS[what[0]] if what[0] in range(len(UNITS)) else what
            return [(fn, *args, 0), (fn, *args, 1)]

        def widened(h, g, first=0, last=3):
            return [(widen_w2, h, g, j) for j in range(first, last + 1)]

        def on_x(fn, *parts):
            return [(fn, *part) for part in parts]

        MIXED = [(piece, half) for piece in (W2[0, 0], W2[0, 1], WF[0]) for half in range(2)] + [(W1[0, 1], 1)]
        POOLED = (W1[0, 0], W1[0, 1], W1[1, 0], W1[1, 1], W2[1, 0], W2[1, 1])
        POOL_GAINED = (4, 5, 6)
        VECTOR_WEIGHED = (7,)
        stretches = []

        def stretch(vector, tensor, scalar, pool=()):
            stretches.append([tensor, vector, scalar, list(pool)])

        stretch(
            [(gate_tile_x, i, g) for i in range(TT) for g in range(PASSES)] + [(gate_x, 1, g, stream) for g in range(PASSES) for stream in range(2)],
            [(turn_tile_x, i, g) for i in range(TT) for g in range(PASSES)] + on_x(turn_x, (1, 0), (1, 1)) + both(mix_w, W2[0, 0]) + [(mix_w, W1[0, 1], 1), (turn_x, 2, 0)],
            widened(0, 0) + widened(1, 0, 0, 2) + widened(0, 1) + [(take_w, W2[0, 0], 0), (take_w, W1[0, 1], 1)],
            [(group_pool, W1[0, 0]), (group_pool, W1[0, 1])],
        )
        stretch(
            [(quant_x, 0, 0), (quant_w, W1[0, 0]), (quant_w, W1[0, 1])],
            [(mix_w, W2[0, 1], 0), (turn_x, 2, 1)],
            [(take_w, W2[0, 0], 1)] + widened(1, 0, 3, 3) + widened(1, 1, 0, 1),
        )
        stretch(
            on_x(gate_x, (2, 0, 0), (2, 1, 0)) + both(gain_z1, 0),
            both(mul_z1, 0) + [(mix_w, W2[0, 1], 1)] + both(mix_w, WF[0]),
            [(take_w, W2[0, 1], 0), (widen_r,)] + widened(1, 1, 2, 3) + [(group_scalar, WF[1], 0), (take_w, W2[0, 1], 1)],
            [(group_pool, W1[1, 0])],
        )
        stretch(
            [(quant_x, 1, 0), (quant_w, W2[0, 0]), (quant_x, 0, 1), (quant_w, W2[0, 1]), unit(quant_u, 0), (quant_x, 1, 1)]
            + [(quant_w, WF[0]), (quant_x, 2, 0), (quant_w, W1[1, 0])],
            both(mul_z1, 1) + both(mul_z2, 0) + both(mul_f, 0) + both(mul_z2, 1),
            both(relu_z1, 0) + both(take_w, WF[0]) + [(widen_a,), (group_scalar, WF[1], 1), unit(weigh_o1, 0, 0)] + both(relu_z2, 0) + [unit(weigh_o1, 0, 1)],
        )
        stretch(
            both(fuse, 0) + both(gain_z1, 1) + [(gate_x, 2, 0, 1)],
            both(mul_z1, 2) + both(turn_out, 0) + [(turn_x, 3, 0)],
            both(relu_z2, 1) + both(relu_z1, 1) + [(group_scalar, WF[1], 2)],
            [(group_pool, W1[1, 1])],
        )
        stretch(
            [unit(quant_u, 1), (quant_w, W1[1, 1])],
            both(mul_f, 1),
            both(copy_scalar, 0),
        )
        stretch(
            [(gate_x, 2, 1, 1)] + both(fuse, 1) + both(gain_z1, 2),
            both(mul_z1, 4) + both(mul_z1, 3) + both(turn_out, 1),
            both(weigh_o1, 1) + both(relu_z1, 4) + [(group_scalar, WF[1], 3)] + both(relu_z1, 2),
            [(group_pool, W2[1, 0])],
        )
        stretch(
            [(quant_x, 2, 1), unit(quant_u, 2), (quant_w, W2[1, 0])],
            both(mul_z2, 2),
            both(copy_scalar, 1),
        )
        stretch(
            both(gain_z1, 3) + [(gate_x, 3, 0, 0)] + both(fuse, 2),
            both(mul_f, 2) + both(mul_z1, 5) + [(turn_x, 3, 1)],
            both(relu_z2, 2) + both(weigh_o1, 2),
            [(group_pool, W2[1, 1])],
        )
        stretch(
            [unit(quant_u, 3), (quant_w, WF[1]), (quant_w, W2[1, 1])],
            both(turn_out, 2),
            both(relu_z1, 3) + both(relu_z1, 5),
        )
        stretch(
            on_x(gate_x, (3, 1, 0), (3, 0, 1), (3, 1, 1)),
            both(mul_f, 3) + both(mul_z2, 3) + both(mul_z2, 4) + both(mul_z2, 5),
            both(copy_scalar, 2) + both(relu_z2, 3) + both(relu_z2, 4) + [unit(weigh_o1, 5, 0)],
            [unit(gain_pool, 4)],
        )
        stretch(
            [(quant_x, 3, 0), (quant_x, 3, 1), unit(quant_u, 4)],
            both(mul_z1, 7),
            [unit(weigh_o1, 5, 1)] + both(relu_z2, 5),
        )
        stretch(
            both(fuse, 3) + both(gain_z1, 7) + both(fuse, 4),
            both(mul_f, 4) + both(mul_z1, 6) + both(mul_z2, 7),
            both(relu_z1, 6) + both(relu_z2, 7),
            [unit(gain_pool, 5)],
        )
        stretch(
            [unit(merge, 3), unit(quant_u, 7), unit(merge, 4), unit(quant_u, 5)],
            both(mul_z2, 6) + both(turn_out, 3) + both(mul_f, 7) + [unit(turn_out, 4, 0)],
            both(relu_z2, 6) + both(copy_scalar, 3),
        )
        stretch(
            both(weigh_z1, 7) + both(fuse, 5) + [unit(fuse_rows, 7, 0)],
            both(mul_f, 5) + [unit(turn_out, 4, 1)] + both(open_out, 7) + both(turn_out, 5),
            [unit(copy_scalar, 4, 0)] + both(weigh_o1, 6) + [unit(copy_scalar, 4, 1)],
            [unit(gain_pool, 6)],
        )
        stretch(
            [unit(quant_u, 6), unit(fuse_rows, 7, 1)] + both(fuse_rows, 6) + [unit(copy_vector, 6, 1)],
            [unit(close_out, 7, 0)] + both(mul_f, 6) + [unit(close_out, 7, 1), unit(open_out, 6, 0), unit(close_out, 6, 0), unit(open_out, 6, 1), unit(close_out, 6, 1)],
            both(copy_scalar, 5) + both(copy_scalar, 7) + [unit(copy_scalar, 6, 0)],
        )

        def needs(fn, *args):
            if fn in (turn_x, turn_tile_x, widen_w2, widen_r, widen_a):
                return []
            if fn is gate_x:
                return [(turn_x, *args[:2])]
            if fn is gate_tile_x:
                return [(turn_tile_x, *args)]
            if fn is quant_x:
                c, stream = args
                return [(gate_x, c, g, stream) if c else (gate_tile_x, TT - 1, g) for g in range(PASSES)]
            if fn in (mix_w, group_scalar, group_pool):
                return [(widen_w2, *args[0][1:], 3)] if args[0][0] == "w2" else []
            if fn is take_w:
                return [(mix_w, *args)] + ([(group_pool, args[0])] if args[0] in POOLED else [])
            if fn is quant_w:
                halves = [(take_w if (*args, half) in MIXED else group_scalar, *args, half) for half in range(2)]
                if args[0] in POOLED:
                    return [(group_pool, *args)] + [stage for stage in halves if stage[0] is take_w]
                return halves if (*args, 0) in MIXED else [(group_scalar, *args, quarter) for quarter in range(4)]
            c, h = args[:2]
            k = UNITS.index((c, h))
            weighs = both(weigh_z1 if k in VECTOR_WEIGHED else weigh_o1, k)
            if fn in (mul_z1, mul_z2):
                weight, stream = (W1, 0) if fn is mul_z1 else (W2, 1)
                return [(quant_w, weight[h, g]) for g in range(PASSES)] + [(quant_x, c, stream)]
            if fn is gain_z1:
                return [(mul_z1, *args), (widen_r,)]
            if fn is relu_z1:
                return [(mul_z1 if pooled(c, h) else gain_z1, *args)]
            if fn is weigh_z1:
                return [(gain_z1, *args), (widen_a,)]
            if fn in (gain_pool, weigh_o1):
                return both(relu_z1, k) + [(widen_r,), (widen_a,)]
            if fn is quant_u:
                return [unit(gain_pool, k)] if pooled(c, h) else both(gain_z1, k)
            if fn is relu_z2:
                return [(mul_z2, *args)]
            if fn is mul_f:
                return [unit(quant_u, k), (quant_w, WF[h])]
            if fn is fuse:
                return [(mul_f, *args), (relu_z2, *args), (widen_a,)]
            if fn is fuse_rows:
                return both(mul_f, k) + both(relu_z2, k)
            if fn is merge:
                return both(fuse, k) + both(relu_z1, k)
            if fn is turn_out:
                return [unit(merge, k)] if k in MERGED else both(fuse, k) + weighs
            if fn is open_out:
                return weighs
            if fn is close_out:
                return [(fuse_rows, *args), (open_out, *args)]
            return [(close_out if k in OPENED else turn_out, *args)]

        def banks_wanted(fn, *args):
            return 1 if fn in (turn_x, turn_tile_x, mix_w, mul_z1, mul_z2, mul_f, turn_out, open_out) else 0

        long_stages = (gate_x, gate_tile_x, merge, mix_w)
        done = set()
        rested = set()
        for programs in stretches:
            while any(programs):
                before = len(done) + len(rested)
                for program in programs:
                    if not program or banks_wanted(*program[0]) > len(free_banks):
                        continue
                    if not all(stage in done for stage in needs(*program[0])):
                        continue
                    if program[0][0] in long_stages and program[0] not in rested:
                        rested.add(program[0])
                        continue
                    stage = program.pop(0)
                    stage[0](*stage[1:])
                    if stage[0] in (copy_scalar, copy_vector):
                        store(*stage[1:])
                    done.add(stage)
                assert len(done) + len(rested) > before
